import numpy as np
import ml_dtypes


def mxq(x, axis, fmt="e4m3"):
    dtype, down = {"e4m3": (ml_dtypes.float8_e4m3fn, 7), "e5m2": (ml_dtypes.float8_e5m2, 14)}[fmt]
    v = np.moveaxis(np.asarray(x, np.float32).astype(ml_dtypes.bfloat16).astype(np.float64), axis, -1)
    blocks = v.reshape(v.shape[:-1] + (-1, 32))
    amax = np.abs(blocks).max(-1, keepdims=True)
    byte = np.maximum(np.where(amax > 0, np.frexp(amax)[1] - 1 + 127, 0) - down, 1)
    scale = np.exp2(byte - 127.0)
    codes = (blocks / scale).astype(np.float32).astype(dtype).astype(np.float64)
    return np.moveaxis((codes * scale).reshape(v.shape), -1, axis)


WIDE = False


def mx_kscale(k):
    if not WIDE:
        return np.ones(k)
    levels = np.array([10, -10, 5, -5, 0])
    if k % 512:
        return np.exp2(np.random.permutation(np.resize(levels, k // 32))).repeat(32)
    a = np.empty((k // 512, 16))
    for p in range(k // 512):
        a[p, :8] = np.random.permutation(np.resize(levels, 8))
        for g in range(8):
            far = levels[np.abs(levels - a[p, g]) >= 10]
            a[p, g + 8] = far[np.random.randint(len(far))]
    return np.exp2(a.ravel()).repeat(32)


def f64(x):
    return np.asarray(x).astype(np.float64)


def striped(idx):
    return np.tile(np.asarray(idx).reshape(-1, 16).T, (8, 1)).astype(np.uint16)


def unstriped(offs):
    return offs[:16].T.reshape(-1).astype(np.int64)


E2M1 = np.array([0.0, 0.5, 1.0, 1.5, 2.0, 3.0, 4.0, 6.0, -0.0, -0.5, -1.0, -1.5, -2.0, -3.0, -4.0, -6.0])


def pack_weight(w, fmt):
    k, n = w.shape
    w = f64(np.asarray(w, np.float32).astype(ml_dtypes.bfloat16)).reshape(k // 32, 32, n)
    amax = np.abs(w).max(1)
    if fmt == "e4m3":
        byte = np.frexp(amax)[1] - 1 + 127 - 7
    else:
        mant, ex = np.frexp(amax / 6.0)
        byte = np.where(mant > 0.5, ex, ex - 1) + 127
    byte = np.clip(np.where(amax > 0, byte, 1), 1, 254)
    scaled = (w * np.exp2(127.0 - byte)[:, None, :]).reshape(k, n).astype(np.float32)
    by_word = np.ascontiguousarray(scaled.reshape(k // 512, 128, 4, n).transpose(0, 1, 3, 2))
    if fmt == "e4m3":
        words = by_word.astype(ml_dtypes.float8_e4m3fn).view(np.uint8)
    else:
        c = by_word.astype(ml_dtypes.float4_e2m1fn).view(np.uint8) & 0xF
        words = (c[..., 0::2] | (c[..., 1::2] << 4)).reshape(k // 512, 128, 2 * n)
    return np.ascontiguousarray(words), np.ascontiguousarray(byte.astype(np.uint8).reshape(k // 512, 16, n))


def unpack_weight(words, scales, fmt):
    g, _, n = scales.shape
    words = np.ascontiguousarray(words).reshape(g, 128, n, -1)
    if fmt == "e4m3":
        vals = words.view(ml_dtypes.float8_e4m3fn).astype(np.float64)
    else:
        nib = np.empty((g, 128, n, 4), np.uint8)
        nib[..., 0::2] = words & 0xF
        nib[..., 1::2] = words >> 4
        vals = E2M1[nib]
    vals = vals * np.repeat(np.exp2(scales.astype(np.float64) - 127.0), 8, axis=1)[..., None]
    return vals.transpose(0, 1, 3, 2).reshape(g * 512, n)


B, N, T, D, DV, NQ = 1, 2048, 4096, 1024, 256, 128
PAGE = 512
CAP = 2.0


def setup_inputs():
    n = np.random.standard_normal
    pages = np.random.permutation(T // PAGE)[:B * N // PAGE]
    idx = (pages[:, None] * PAGE + np.arange(PAGE)[None, :]).reshape(-1)
    s = mx_kscale(D)[:, None]
    u = np.ones(T)
    u[idx] = mx_kscale(B * N)
    r = np.random.uniform(0.5, 2.0, T)
    qp = [pack_weight(x, "e4m3") for x in n((B, D, NQ)) * s * (1.00 / np.sqrt(D))]
    k = n((D, T)) / s
    v = n((DV, T)) / (u * r)
    kp = pack_weight(k, "e2m1")
    vp = pack_weight(v.T, "e4m3")
    return {
        "q_words": np.stack([x[0] for x in qp]),
        "q_scales": np.stack([x[1] for x in qp]),
        "k_words": np.ascontiguousarray(kp[0].reshape(D // 1024, 2, 128, T, 2).transpose(0, 2, 3, 1, 4)).reshape(D // 1024, 128, T, 4),
        "k_scales": kp[1],
        "v_words": vp[0],
        "v_scales": vp[1],
        "vs": np.tile(u * r, (128, 1)).astype(np.float32),
        "offs": striped(idx),
        "voffs": striped((pages[:, None] * DV + np.arange(DV)[None, :]).reshape(-1)),
    }


def reference(q_words, q_scales, k_words, k_scales, v_words, v_scales, vs, offs, voffs):
    idx = unstriped(offs)
    k = unpack_weight(k_words.reshape(D // 1024, 128, T, 2, 2).transpose(0, 3, 1, 2, 4).reshape(D // 512, 128, 2 * T), k_scales, "e2m1")
    v = unpack_weight(v_words, v_scales, "e4m3")
    v = v.reshape(T // 512, 512, DV)[unstriped(voffs)[::DV] // DV].reshape(B, N, DV)
    pick = lambda x: x[:, idx].reshape(x.shape[0], B, N).transpose(1, 0, 2)
    q = np.stack([unpack_weight(q_words[b], q_scales[b], "e4m3") for b in range(B)])
    score = q.transpose(0, 2, 1) @ pick(k)
    score = CAP * np.tanh(score / CAP)
    p = np.square(np.maximum(score, 0.0))
    total = p.sum(-1, keepdims=True) + 1.0
    w = p * pick(f64(vs))[:, :1, :]
    y = mxq(w, 2, "e4m3") @ v
    y = y / total
    return y

@@ -1,0 +1,173 @@
+from contextlib import ExitStack
+
+import concourse.mybir as mybir
+
+F32 = mybir.dt.float32
+BF16 = mybir.dt.bfloat16
+I32 = mybir.dt.int32
+U32 = mybir.dt.uint32
+U16 = mybir.dt.uint16
+U8 = mybir.dt.uint8
+FP8X4 = mybir.dt.float8_e4m3fn_x4
+FP4X4 = mybir.dt.float4_e2m1fn_x4
+ACT = mybir.ActivationFunctionType
+ALU = mybir.AluOpType
+
+P = 128
+N, T, D, DV, NQ = 2048, 4096, 1024, 256, 128
+PAGE = 512
+PAGES = N // PAGE
+POOL_PAGES = T // PAGE
+PASSES = D // 512
+CAP = 2.0
+HALVES = 2
+SECOND = 16
+
+FLOPS = 2 * NQ * N * D + 2 * NQ * N * DV
+
+
+def tile_attend_pkv4q_rel2_cap_kernel(tc, q_words, q_scales, k_words, k_scales, v_words, v_scales, vs, offs, voffs, out):
+    nc = tc.nc
+    with ExitStack() as ctx:
+        lists = ctx.enter_context(tc.tile_pool(name="lists", bufs=1))
+        held = ctx.enter_context(tc.tile_pool(name="held", bufs=1))
+        pages = ctx.enter_context(tc.tile_pool(name="pages", bufs=PAGES))
+        score_banks = ctx.enter_context(tc.psum_pool(name="score_banks", bufs=PAGES))
+        turn_banks = ctx.enter_context(tc.psum_pool(name="turn_banks", bufs=3))
+        sum_bank = ctx.enter_context(tc.psum_pool(name="sum_bank", bufs=1))
+
+        token_list = lists.tile([P, N // 16], U16, name="token_list")
+        nc.sync.dma_start(token_list[:], offs)
+
+        ks_pool = held.tile([P, T], U8, name="ks_pool", tag="second", align_bytes=64)
+        nc.vector.memset(ks_pool[:].bitcast(I32), 0)
+        ks_rows = k_scales.rearrange("o (g j) t -> j g o t", j=4)
+        for j in range(4):
+            nc.sync.dma_start(ks_pool[j:P:SECOND, :].bitcast(I32), ks_rows[j].bitcast(I32))
+
+        ramp = held.tile([P, P], I32, name="ramp", tag="first", align_bytes=64)
+        nc.gpsimd.iota(ramp[:], [[1, P]], base=0, channel_multiplier=-1)
+        identity = held.tile([P, P], F32, name="identity", align_bytes=64)
+        nc.vector.tensor_scalar(identity[:], ramp[:], 0.0, None, ALU.is_equal)
+
+        value_list = lists.tile([P, PAGES * DV // 16], U16, name="value_list")
+        nc.sync.dma_start(value_list[:], voffs)
+        q_codes = held.tile([P, PASSES, NQ], I32, name="q_codes", align_bytes=64)
+        nc.sync.dma_start(q_codes[:], q_words[0].rearrange("o g q r -> g o (q r)").bitcast(I32))
+
+        kw_pool = held.tile([P, T], I32, name="kw_pool", tag="first", align_bytes=64)
+        nc.sync.dma_start(kw_pool[:], k_words[0].rearrange("g t b -> g (t b)").bitcast(I32))
+
+        q_plane = held.tile([P, PASSES * NQ], U8, name="q_plane", align_bytes=64)
+        nc.vector.memset(q_plane[:].bitcast(I32), 0)
+        ks_second = held.tile([P, N], U8, name="ks_second", align_bytes=64)
+        nc.vector.memset(ks_second[:].bitcast(I32), 0)
+        vs_pool = held.tile([P, T], F32, name="vs_pool", tag="third", align_bytes=64)
+        nc.vector.memset(vs_pool[:], 0.0)
+        nc.scalar.dma_start(vs_pool[0:1, :], vs[0:1, :])
+        qs_rows = q_scales[0].rearrange("o (g j) q -> j g o q", j=4)
+        for j in range(4):
+            nc.scalar.dma_start(q_plane[j:P:32, :].bitcast(I32).rearrange("g (o w) -> g o w", o=PASSES), qs_rows[j].bitcast(I32))
+
+        sums = held.tile([P, PAGES * HALVES + 1], F32, name="sums")
+        nc.gpsimd.memset(sums[:, PAGES * HALVES :], 1.0)
+
+        ks_first = held.tile([P, N], U8, name="ks_first", align_bytes=64)
+        nc.vector.tensor_copy(ks_first[:], ks_pool[:].indirect(token_list[:]))
+        nc.scalar.dma_start(ks_second[0 : P - SECOND, :].bitcast(I32), ks_first[SECOND:P, :].bitcast(I32))
+        k_planes = (ks_first, ks_second)
+
+        vw_pool = held.tile([P, POOL_PAGES * DV], I32, name="vw_pool", tag="second", align_bytes=64)
+        nc.sync.dma_start(
+            vw_pool[:].rearrange("g (u e) -> g u e", u=POOL_PAGES),
+            v_words.rearrange("u g e r -> g u (e r)").bitcast(I32),
+        )
+
+        vs_listed = held.tile([P, N], F32, name="vs_listed", align_bytes=64)
+        nc.vector.tensor_copy(vs_listed[:], vs_pool[:].indirect(token_list[:]))
+        vs_cols = []
+        for u in range(PAGES):
+            cols = pages.tile([P, 4], F32, name="vs_cols", align_bytes=64)
+            nc.sync.dma_start(cols[:], vs_listed[0:1, u * PAGE : (u + 1) * PAGE])
+            vs_cols.append(cols)
+
+        vsc_pool = held.tile([P, POOL_PAGES * DV], U8, name="vsc_pool", tag="third", align_bytes=64)
+        nc.vector.memset(vsc_pool[:].bitcast(I32), 0)
+        vsc_rows = v_scales.rearrange("u (g j) e -> j g u e", j=4)
+        for j in range(4):
+            nc.sync.dma_start(vsc_pool[j:P:32, :].bitcast(I32).rearrange("g (u w) -> g u w", u=POOL_PAGES), vsc_rows[j].bitcast(I32))
+
+        turned = []
+        for u in range(PAGES):
+            slots = slice(u * PAGE, (u + 1) * PAGE)
+            k_pairs = pages.tile([P, PAGE], U32, name="k_pairs", align_bytes=64)
+            nc.vector.tensor_copy(k_pairs[:], kw_pool[:].bitcast(U32).indirect(token_list[:, u * PAGE // 16 : (u + 1) * PAGE // 16]))
+            k_codes = pages.tile([P, PASSES, PAGE], U16, name="k_codes", align_bytes=64)
+            nc.vector.tensor_copy(k_codes[:], k_pairs[:].bitcast(U16).rearrange("g (i o) -> g o i", o=PASSES))
+            score = score_banks.tile([P, PAGE], F32, name="score")
+            for o in range(PASSES):
+                nc.tensor.matmul_mx(
+                    out=score[:],
+                    lhsT=q_codes[:, o, :].bitcast(FP8X4),
+                    lhsT_scale=q_plane[:, o * NQ : (o + 1) * NQ],
+                    rhs=k_codes[:, o, :].bitcast(FP4X4),
+                    rhs_scale=k_planes[o][:, slots],
+                    start=(o == 0),
+                    stop=(o == PASSES - 1),
+                )
+            dealt = score[:].rearrange("q (s t) -> q t s", t=4)
+            capped = pages.tile([P, 4, P], F32, name="capped", align_bytes=64)
+            positive = pages.tile([P, 4, P], F32, name="positive", align_bytes=64)
+            weight = pages.tile([P, 4, P], F32, name="weight", align_bytes=64)
+            halves = [slice(2 * h, 2 * h + 2) for h in range(HALVES)]
+            for ts in halves:
+                nc.scalar.activation(capped[:, ts, :], dealt[:, ts, :], ACT.Tanh, scale=1.0 / CAP)
+            for ts in halves:
+                nc.scalar.activation(positive[:, ts, :], capped[:, ts, :], ACT.Relu)
+            for h, ts in enumerate(halves):
+                col = u * HALVES + h
+                nc.scalar.activation(weight[:, ts, :], positive[:, ts, :], ACT.Square, scale=CAP, accum_out=sums[:, col : col + 1])
+            bank = turn_banks.tile([P, 4, NQ], F32, name="turned")
+            for t in range(4):
+                nc.tensor.transpose(bank[:, t, :], weight[:, t, :], identity[:])
+            turned.append(bank)
+
+        v_plane = held.tile([P, PAGES * DV], U8, name="v_plane", align_bytes=64)
+        nc.vector.tensor_copy(v_plane[:], vsc_pool[:].indirect(value_list[:]))
+
+        acc = sum_bank.tile([P, DV], F32, name="acc")
+        total = held.tile([P, 1], F32, name="total")
+        inverse = held.tile([P, 1], F32, name="inverse")
+        for u in range(PAGES):
+            last = u == PAGES - 1
+            v_codes = pages.tile([P, DV], U32, name="v_codes", align_bytes=64)
+            listed = vw_pool[:].bitcast(U32).indirect(value_list[:, u * DV // 16 : (u + 1) * DV // 16])
+            if last:
+                nc.vector.tensor_copy(v_codes[:], listed)
+                nc.vector.tensor_reduce(total[:], sums[:], mybir.AxisListType.X, ALU.add)
+            w_bf16 = pages.tile([P, NQ, 4], BF16, name="w_bf16", align_bytes=64)
+            nc.vector.tensor_tensor(
+                w_bf16[:],
+                turned[u][:].rearrange("s t q -> s q t"),
+                vs_cols[u][:].unsqueeze(1).to_broadcast([P, NQ, 4]),
+                ALU.mult,
+            )
+            if last:
+                nc.vector.reciprocal(inverse[:], total[:])
+            else:
+                nc.vector.tensor_copy(v_codes[:], listed)
+            w_codes = pages.tile([P, NQ], U32, name="w_codes", align_bytes=64)
+            w_plane = pages.tile([P, NQ], U8, name="w_plane", align_bytes=64)
+            nc.vector.quantize_mx(out=w_codes[:].bitcast(FP8X4), scales=w_plane[:], in_=w_bf16[:].rearrange("s q t -> s (q t)"))
+            nc.tensor.matmul_mx(
+                out=acc[:],
+                lhsT=w_codes[:].bitcast(FP8X4),
+                lhsT_scale=w_plane[:],
+                rhs=v_codes[:].bitcast(FP8X4),
+                rhs_scale=v_plane[:, u * DV : (u + 1) * DV],
+                start=(u == 0),
+                stop=last,
+            )
+        result = held.tile([P, DV], F32, name="result")
+        nc.scalar.activation(result[:], acc[:], ACT.Copy, scale=inverse[:])
+        nc.scalar.dma_start(out[0], result[:])

@@ -1,6 +1,7 @@
 from contextlib import ExitStack
 
 import concourse.mybir as mybir
+from concourse.masks import make_identity
 
 F32 = mybir.dt.float32
 BF16 = mybir.dt.bfloat16
@@ -21,7 +22,9 @@ POOL_PAGES = T // PAGE
 PASSES = D // 512
 CAP = 2.0
 HALVES = 2
-SECOND = 16
+KS_ROWS = 32
+KS_FIRST = P - KS_ROWS
+ON_SCALAR = 2
 
 FLOPS = 2 * NQ * N * D + 2 * NQ * N * DV
 
@@ -32,50 +35,44 @@ def tile_attend_pkv4q_rel2_cap_kernel(tc, q_words, q_scales, k_words, k_scales, 
         lists = ctx.enter_context(tc.tile_pool(name="lists", bufs=1))
         held = ctx.enter_context(tc.tile_pool(name="held", bufs=1))
         pages = ctx.enter_context(tc.tile_pool(name="pages", bufs=PAGES))
-        score_banks = ctx.enter_context(tc.psum_pool(name="score_banks", bufs=PAGES))
-        turn_banks = ctx.enter_context(tc.psum_pool(name="turn_banks", bufs=3))
+        score_banks = ctx.enter_context(tc.psum_pool(name="score_banks", bufs=3))
+        turn_banks = ctx.enter_context(tc.psum_pool(name="turn_banks", bufs=PAGES))
         sum_bank = ctx.enter_context(tc.psum_pool(name="sum_bank", bufs=1))
 
+        ks_pool = held.tile([P, T], U8, name="ks_pool", tag="second", align_bytes=64)
+        nc.sync.dma_start(ks_pool[KS_FIRST:P, :].bitcast(I32), k_scales.rearrange("o f t -> (o f) t").bitcast(I32))
         token_list = lists.tile([P, N // 16], U16, name="token_list")
         nc.sync.dma_start(token_list[:], offs)
-
-        ks_pool = held.tile([P, T], U8, name="ks_pool", tag="second", align_bytes=64)
-        nc.vector.memset(ks_pool[:].bitcast(I32), 0)
-        ks_rows = k_scales.rearrange("o (g j) t -> j g o t", j=4)
-        for j in range(4):
-            nc.sync.dma_start(ks_pool[j:P:SECOND, :].bitcast(I32), ks_rows[j].bitcast(I32))
-
-        ramp = held.tile([P, P], I32, name="ramp", tag="first", align_bytes=64)
-        nc.gpsimd.iota(ramp[:], [[1, P]], base=0, channel_multiplier=-1)
-        identity = held.tile([P, P], F32, name="identity", align_bytes=64)
-        nc.vector.tensor_scalar(identity[:], ramp[:], 0.0, None, ALU.is_equal)
-
-        value_list = lists.tile([P, PAGES * DV // 16], U16, name="value_list")
-        nc.sync.dma_start(value_list[:], voffs)
+        kw_pool = held.tile([P, T], I32, name="kw_pool", align_bytes=64)
+        nc.sync.dma_start(kw_pool[:], k_words[0].rearrange("g t b -> g (t b)").bitcast(I32))
         q_codes = held.tile([P, PASSES, NQ], I32, name="q_codes", align_bytes=64)
         nc.sync.dma_start(q_codes[:], q_words[0].rearrange("o g q r -> g o (q r)").bitcast(I32))
+        value_list = lists.tile([P, PAGES * DV // 16], U16, name="value_list")
+        nc.sync.dma_start(value_list[:], voffs)
 
-        kw_pool = held.tile([P, T], I32, name="kw_pool", tag="first", align_bytes=64)
-        nc.sync.dma_start(kw_pool[:], k_words[0].rearrange("g t b -> g (t b)").bitcast(I32))
-
+        nc.vector.memset(ks_pool[0:KS_FIRST, :].bitcast(I32), 0)
         q_plane = held.tile([P, PASSES * NQ], U8, name="q_plane", align_bytes=64)
         nc.vector.memset(q_plane[:].bitcast(I32), 0)
-        ks_second = held.tile([P, N], U8, name="ks_second", align_bytes=64)
-        nc.vector.memset(ks_second[:].bitcast(I32), 0)
-        vs_pool = held.tile([P, T], F32, name="vs_pool", tag="third", align_bytes=64)
+        k_planes = held.tile([P, PASSES * N], U8, name="k_planes", align_bytes=64)
+        nc.vector.memset(k_planes[:].bitcast(I32), 0)
+        vs_pool = held.tile([P, T], F32, name="vs_pool", tag="fourth", align_bytes=64)
         nc.vector.memset(vs_pool[:], 0.0)
         nc.scalar.dma_start(vs_pool[0:1, :], vs[0:1, :])
         qs_rows = q_scales[0].rearrange("o (g j) q -> j g o q", j=4)
         for j in range(4):
             nc.scalar.dma_start(q_plane[j:P:32, :].bitcast(I32).rearrange("g (o w) -> g o w", o=PASSES), qs_rows[j].bitcast(I32))
 
+        identity = held.tile([P, P], F32, name="identity", align_bytes=64)
+        make_identity(nc, identity[:])
         sums = held.tile([P, PAGES * HALVES + 1], F32, name="sums")
         nc.gpsimd.memset(sums[:, PAGES * HALVES :], 1.0)
 
-        ks_first = held.tile([P, N], U8, name="ks_first", align_bytes=64)
-        nc.vector.tensor_copy(ks_first[:], ks_pool[:].indirect(token_list[:]))
-        nc.scalar.dma_start(ks_second[0 : P - SECOND, :].bitcast(I32), ks_first[SECOND:P, :].bitcast(I32))
-        k_planes = (ks_first, ks_second)
+        ks_listed = held.tile([P, N], U8, name="ks_listed", tag="third", align_bytes=64)
+        nc.vector.tensor_copy(ks_listed[:], ks_pool[:].indirect(token_list[:]))
+        for o in range(PASSES):
+            for g in range(4):
+                row = KS_FIRST + 16 * o + 4 * g
+                nc.sync.dma_start(k_planes[32 * g : 32 * g + 4, o * N : (o + 1) * N].bitcast(I32), ks_listed[row : row + 4, :].bitcast(I32))
 
         vw_pool = held.tile([P, POOL_PAGES * DV], I32, name="vw_pool", tag="second", align_bytes=64)
         nc.sync.dma_start(
@@ -83,27 +80,24 @@ def tile_attend_pkv4q_rel2_cap_kernel(tc, q_words, q_scales, k_words, k_scales, 
             v_words.rearrange("u g e r -> g u (e r)").bitcast(I32),
         )
 
-        vs_listed = held.tile([P, N], F32, name="vs_listed", align_bytes=64)
-        nc.vector.tensor_copy(vs_listed[:], vs_pool[:].indirect(token_list[:]))
-        vs_cols = []
-        for u in range(PAGES):
-            cols = pages.tile([P, 4], F32, name="vs_cols", align_bytes=64)
-            nc.sync.dma_start(cols[:], vs_listed[0:1, u * PAGE : (u + 1) * PAGE])
-            vs_cols.append(cols)
-
         vsc_pool = held.tile([P, POOL_PAGES * DV], U8, name="vsc_pool", tag="third", align_bytes=64)
-        nc.vector.memset(vsc_pool[:].bitcast(I32), 0)
+        nc.gpsimd.memset(vsc_pool[:].bitcast(I32), 0)
         vsc_rows = v_scales.rearrange("u (g j) e -> j g u e", j=4)
         for j in range(4):
             nc.sync.dma_start(vsc_pool[j:P:32, :].bitcast(I32).rearrange("g (u w) -> g u w", u=POOL_PAGES), vsc_rows[j].bitcast(I32))
 
         turned = []
+        vs_cols = []
         for u in range(PAGES):
-            slots = slice(u * PAGE, (u + 1) * PAGE)
-            k_pairs = pages.tile([P, PAGE], U32, name="k_pairs", align_bytes=64)
+            k_pairs = held.tile([P, PAGE], U32, name="k_pairs", tag="pairs%d" % u, align_bytes=64)
             nc.vector.tensor_copy(k_pairs[:], kw_pool[:].bitcast(U32).indirect(token_list[:, u * PAGE // 16 : (u + 1) * PAGE // 16]))
             k_codes = pages.tile([P, PASSES, PAGE], U16, name="k_codes", align_bytes=64)
             nc.vector.tensor_copy(k_codes[:], k_pairs[:].bitcast(U16).rearrange("g (i o) -> g o i", o=PASSES))
+            vs_listed = held.tile([P, PAGE], F32, name="vs_listed", tag="pairs%d" % u, align_bytes=64)
+            nc.vector.tensor_copy(vs_listed[:], vs_pool[:].indirect(token_list[:, u * PAGE // 16 : (u + 1) * PAGE // 16]))
+            cols = pages.tile([P, 4], F32, name="vs_cols", align_bytes=64)
+            nc.sync.dma_start(cols[:], vs_listed[0:1, :])
+            vs_cols.append(cols)
             score = score_banks.tile([P, PAGE], F32, name="score")
             for o in range(PASSES):
                 nc.tensor.matmul_mx(
@@ -111,7 +105,7 @@ def tile_attend_pkv4q_rel2_cap_kernel(tc, q_words, q_scales, k_words, k_scales, 
                     lhsT=q_codes[:, o, :].bitcast(FP8X4),
                     lhsT_scale=q_plane[:, o * NQ : (o + 1) * NQ],
                     rhs=k_codes[:, o, :].bitcast(FP4X4),
-                    rhs_scale=k_planes[o][:, slots],
+                    rhs_scale=k_planes[:, o * N + u * PAGE : o * N + (u + 1) * PAGE],
                     start=(o == 0),
                     stop=(o == PASSES - 1),
                 )
@@ -132,7 +126,7 @@ def tile_attend_pkv4q_rel2_cap_kernel(tc, q_words, q_scales, k_words, k_scales, 
                 nc.tensor.transpose(bank[:, t, :], weight[:, t, :], identity[:])
             turned.append(bank)
 
-        v_plane = held.tile([P, PAGES * DV], U8, name="v_plane", align_bytes=64)
+        v_plane = held.tile([P, PAGES * DV], U8, name="v_plane", tag="fourth", align_bytes=64)
         nc.vector.tensor_copy(v_plane[:], vsc_pool[:].indirect(value_list[:]))
 
         acc = sum_bank.tile([P, DV], F32, name="acc")
@@ -146,12 +140,18 @@ def tile_attend_pkv4q_rel2_cap_kernel(tc, q_words, q_scales, k_words, k_scales, 
                 nc.vector.tensor_copy(v_codes[:], listed)
                 nc.vector.tensor_reduce(total[:], sums[:], mybir.AxisListType.X, ALU.add)
             w_bf16 = pages.tile([P, NQ, 4], BF16, name="w_bf16", align_bytes=64)
-            nc.vector.tensor_tensor(
-                w_bf16[:],
-                turned[u][:].rearrange("s t q -> s q t"),
-                vs_cols[u][:].unsqueeze(1).to_broadcast([P, NQ, 4]),
-                ALU.mult,
-            )
+            if u < ON_SCALAR:
+                w_places = pages.tile([P, 4, NQ], BF16, name="w_places", align_bytes=64)
+                for t in range(4):
+                    nc.scalar.activation(w_places[:, t, :], turned[u][:, t, :], ACT.Copy, scale=vs_cols[u][:, t : t + 1])
+                nc.scalar.copy(w_bf16[:], w_places[:].rearrange("s t q -> s q t"))
+            else:
+                nc.vector.tensor_tensor(
+                    w_bf16[:],
+                    turned[u][:].rearrange("s t q -> s q t"),
+                    vs_cols[u][:].unsqueeze(1).to_broadcast([P, NQ, 4]),
+                    ALU.mult,
+                )
             if last:
                 nc.vector.reciprocal(inverse[:], total[:])
             else:

@@ -24,7 +24,7 @@ CAP = 2.0
 HALVES = 2
 KS_ROWS = 32
 KS_FIRST = P - KS_ROWS
-ON_SCALAR = 2
+ON_SCALAR = 4
 
 FLOPS = 2 * NQ * N * D + 2 * NQ * N * DV
 
@@ -43,7 +43,7 @@ def tile_attend_pkv4q_rel2_cap_kernel(tc, q_words, q_scales, k_words, k_scales, 
         nc.sync.dma_start(ks_pool[KS_FIRST:P, :].bitcast(I32), k_scales.rearrange("o f t -> (o f) t").bitcast(I32))
         token_list = lists.tile([P, N // 16], U16, name="token_list")
         nc.sync.dma_start(token_list[:], offs)
-        kw_pool = held.tile([P, T], I32, name="kw_pool", align_bytes=64)
+        kw_pool = held.tile([P, T], I32, name="kw_pool", tag="keys", align_bytes=64)
         nc.sync.dma_start(kw_pool[:], k_words[0].rearrange("g t b -> g (t b)").bitcast(I32))
         q_codes = held.tile([P, PASSES, NQ], I32, name="q_codes", align_bytes=64)
         nc.sync.dma_start(q_codes[:], q_words[0].rearrange("o g q r -> g o (q r)").bitcast(I32))
@@ -53,14 +53,16 @@ def tile_attend_pkv4q_rel2_cap_kernel(tc, q_words, q_scales, k_words, k_scales, 
         nc.vector.memset(ks_pool[0:KS_FIRST, :].bitcast(I32), 0)
         q_plane = held.tile([P, PASSES * NQ], U8, name="q_plane", align_bytes=64)
         nc.vector.memset(q_plane[:].bitcast(I32), 0)
+        vsc_pool = held.tile([P, POOL_PAGES * DV], U8, name="vsc_pool", align_bytes=64)
+        nc.vector.memset(vsc_pool[:].bitcast(I32), 0)
         k_planes = held.tile([P, PASSES * N], U8, name="k_planes", align_bytes=64)
         nc.vector.memset(k_planes[:].bitcast(I32), 0)
-        vs_pool = held.tile([P, T], F32, name="vs_pool", tag="fourth", align_bytes=64)
-        nc.vector.memset(vs_pool[:], 0.0)
-        nc.scalar.dma_start(vs_pool[0:1, :], vs[0:1, :])
         qs_rows = q_scales[0].rearrange("o (g j) q -> j g o q", j=4)
         for j in range(4):
             nc.scalar.dma_start(q_plane[j:P:32, :].bitcast(I32).rearrange("g (o w) -> g o w", o=PASSES), qs_rows[j].bitcast(I32))
+        vsc_rows = v_scales.rearrange("u (g j) e -> j g u e", j=4)
+        for j in range(4):
+            nc.gpsimd.dma_start(vsc_pool[j:P:32, :].bitcast(I32).rearrange("g (u w) -> g u w", u=POOL_PAGES), vsc_rows[j].bitcast(I32))
 
         identity = held.tile([P, P], F32, name="identity", align_bytes=64)
         make_identity(nc, identity[:])
@@ -70,34 +72,29 @@ def tile_attend_pkv4q_rel2_cap_kernel(tc, q_words, q_scales, k_words, k_scales, 
         ks_listed = held.tile([P, N], U8, name="ks_listed", tag="third", align_bytes=64)
         nc.vector.tensor_copy(ks_listed[:], ks_pool[:].indirect(token_list[:]))
         for o in range(PASSES):
-            for g in range(4):
-                row = KS_FIRST + 16 * o + 4 * g
-                nc.sync.dma_start(k_planes[32 * g : 32 * g + 4, o * N : (o + 1) * N].bitcast(I32), ks_listed[row : row + 4, :].bitcast(I32))
+            for j in range(4):
+                row = KS_FIRST + 16 * o
+                nc.sync.dma_start(k_planes[j:P:32, o * N : (o + 1) * N].bitcast(I32), ks_listed[row + j : row + 16 : 4, :].bitcast(I32))
 
-        vw_pool = held.tile([P, POOL_PAGES * DV], I32, name="vw_pool", tag="second", align_bytes=64)
+        vs_pool = held.tile([P, T], F32, name="vs_pool", tag="second", align_bytes=64)
+        nc.sync.dma_start(vs_pool[:], vs)
+        vw_pool = held.tile([P, POOL_PAGES * DV], I32, name="vw_pool", tag="third", align_bytes=64)
         nc.sync.dma_start(
             vw_pool[:].rearrange("g (u e) -> g u e", u=POOL_PAGES),
             v_words.rearrange("u g e r -> g u (e r)").bitcast(I32),
         )
 
-        vsc_pool = held.tile([P, POOL_PAGES * DV], U8, name="vsc_pool", tag="third", align_bytes=64)
-        nc.gpsimd.memset(vsc_pool[:].bitcast(I32), 0)
-        vsc_rows = v_scales.rearrange("u (g j) e -> j g u e", j=4)
-        for j in range(4):
-            nc.sync.dma_start(vsc_pool[j:P:32, :].bitcast(I32).rearrange("g (u w) -> g u w", u=POOL_PAGES), vsc_rows[j].bitcast(I32))
-
+        k_pairs = []
         turned = []
-        vs_cols = []
-        for u in range(PAGES):
-            k_pairs = held.tile([P, PAGE], U32, name="k_pairs", tag="pairs%d" % u, align_bytes=64)
-            nc.vector.tensor_copy(k_pairs[:], kw_pool[:].bitcast(U32).indirect(token_list[:, u * PAGE // 16 : (u + 1) * PAGE // 16]))
+
+        def gather_keys(u):
+            pairs = pages.tile([P, PAGE], U32, name="k_pairs", align_bytes=64)
+            nc.vector.tensor_copy(pairs[:], kw_pool[:].bitcast(U32).indirect(token_list[:, u * PAGE // 16 : (u + 1) * PAGE // 16]))
+            k_pairs.append(pairs)
+
+        def weigh(u):
             k_codes = pages.tile([P, PASSES, PAGE], U16, name="k_codes", align_bytes=64)
-            nc.vector.tensor_copy(k_codes[:], k_pairs[:].bitcast(U16).rearrange("g (i o) -> g o i", o=PASSES))
-            vs_listed = held.tile([P, PAGE], F32, name="vs_listed", tag="pairs%d" % u, align_bytes=64)
-            nc.vector.tensor_copy(vs_listed[:], vs_pool[:].indirect(token_list[:, u * PAGE // 16 : (u + 1) * PAGE // 16]))
-            cols = pages.tile([P, 4], F32, name="vs_cols", align_bytes=64)
-            nc.sync.dma_start(cols[:], vs_listed[0:1, :])
-            vs_cols.append(cols)
+            nc.vector.tensor_copy(k_codes[:], k_pairs[u][:].bitcast(U16).rearrange("g (i o) -> g o i", o=PASSES))
             score = score_banks.tile([P, PAGE], F32, name="score")
             for o in range(PASSES):
                 nc.tensor.matmul_mx(
@@ -126,47 +123,62 @@ def tile_attend_pkv4q_rel2_cap_kernel(tc, q_words, q_scales, k_words, k_scales, 
                 nc.tensor.transpose(bank[:, t, :], weight[:, t, :], identity[:])
             turned.append(bank)
 
-        v_plane = held.tile([P, PAGES * DV], U8, name="v_plane", tag="fourth", align_bytes=64)
-        nc.vector.tensor_copy(v_plane[:], vsc_pool[:].indirect(value_list[:]))
-
-        acc = sum_bank.tile([P, DV], F32, name="acc")
-        total = held.tile([P, 1], F32, name="total")
-        inverse = held.tile([P, 1], F32, name="inverse")
+        v_plane = held.tile([P, PAGES * DV], U8, name="v_plane", tag="keys", align_bytes=64)
+        gather_keys(0)
         for u in range(PAGES):
-            last = u == PAGES - 1
-            v_codes = pages.tile([P, DV], U32, name="v_codes", align_bytes=64)
-            listed = vw_pool[:].bitcast(U32).indirect(value_list[:, u * DV // 16 : (u + 1) * DV // 16])
-            if last:
-                nc.vector.tensor_copy(v_codes[:], listed)
-                nc.vector.tensor_reduce(total[:], sums[:], mybir.AxisListType.X, ALU.add)
+            if u + 1 < PAGES:
+                gather_keys(u + 1)
+            else:
+                nc.vector.tensor_copy(v_plane[:], vsc_pool[:].indirect(value_list[:]))
+            weigh(u)
+
+        w_woven = []
+        for u in range(PAGES):
+            vs_listed = pages.tile([P, PAGE], F32, name="vs_listed", align_bytes=64)
+            nc.vector.tensor_copy(vs_listed[:], vs_pool[:].indirect(token_list[:, u * PAGE // 16 : (u + 1) * PAGE // 16]))
+            vs_bank = score_banks.tile([P, PAGE], F32, name="score")
+            for t in range(4):
+                nc.tensor.transpose(vs_bank[:, t * P : (t + 1) * P], vs_listed[:, t:PAGE:4], identity[:])
+            cols = pages.tile([P, 4], F32, name="vs_cols", align_bytes=64)
+            nc.scalar.copy(cols[:], vs_bank[:, 0:PAGE:P])
             w_bf16 = pages.tile([P, NQ, 4], BF16, name="w_bf16", align_bytes=64)
             if u < ON_SCALAR:
                 w_places = pages.tile([P, 4, NQ], BF16, name="w_places", align_bytes=64)
                 for t in range(4):
-                    nc.scalar.activation(w_places[:, t, :], turned[u][:, t, :], ACT.Copy, scale=vs_cols[u][:, t : t + 1])
+                    nc.scalar.activation(w_places[:, t, :], turned[u][:, t, :], ACT.Copy, scale=cols[:, t : t + 1])
                 nc.scalar.copy(w_bf16[:], w_places[:].rearrange("s t q -> s q t"))
             else:
                 nc.vector.tensor_tensor(
                     w_bf16[:],
                     turned[u][:].rearrange("s t q -> s q t"),
-                    vs_cols[u][:].unsqueeze(1).to_broadcast([P, NQ, 4]),
+                    cols[:].unsqueeze(1).to_broadcast([P, NQ, 4]),
                     ALU.mult,
                 )
-            if last:
-                nc.vector.reciprocal(inverse[:], total[:])
-            else:
-                nc.vector.tensor_copy(v_codes[:], listed)
+            w_woven.append(w_bf16)
+
+        acc = sum_bank.tile([P, DV], F32, name="acc")
+        total = held.tile([P, 1], F32, name="total")
+        inverse = held.tile([P, 1], F32, name="inverse")
+        v_codes = []
+        for u in range(PAGES):
+            codes = pages.tile([P, DV], U32, name="v_codes", align_bytes=64)
+            nc.vector.tensor_copy(codes[:], vw_pool[:].bitcast(U32).indirect(value_list[:, u * DV // 16 : (u + 1) * DV // 16]))
+            v_codes.append(codes)
+        nc.vector.tensor_reduce(total[:], sums[:], mybir.AxisListType.X, ALU.add)
+        for u in range(PAGES):
             w_codes = pages.tile([P, NQ], U32, name="w_codes", align_bytes=64)
             w_plane = pages.tile([P, NQ], U8, name="w_plane", align_bytes=64)
-            nc.vector.quantize_mx(out=w_codes[:].bitcast(FP8X4), scales=w_plane[:], in_=w_bf16[:].rearrange("s q t -> s (q t)"))
+            nc.vector.quantize_mx(out=w_codes[:].bitcast(FP8X4), scales=w_plane[:], in_=w_woven[u][:].rearrange("s q t -> s (q t)"))
+            if u == 0:
+                nc.vector.reciprocal(inverse[:], total[:])
             nc.tensor.matmul_mx(
                 out=acc[:],
                 lhsT=w_codes[:].bitcast(FP8X4),
                 lhsT_scale=w_plane[:],
-                rhs=v_codes[:].bitcast(FP8X4),
+                rhs=v_codes[u][:].bitcast(FP8X4),
                 rhs_scale=v_plane[:, u * DV : (u + 1) * DV],
                 start=(u == 0),
-                stop=last,
+                stop=(u == PAGES - 1),
             )
         result = held.tile([P, DV], F32, name="result")
         nc.scalar.activation(result[:], acc[:], ACT.Copy, scale=inverse[:])

@@ -24,7 +24,7 @@ CAP = 2.0
 HALVES = 2
 KS_ROWS = 32
 KS_FIRST = P - KS_ROWS
-ON_SCALAR = 4
+ON_SCALAR = 3
 
 FLOPS = 2 * NQ * N * D + 2 * NQ * N * DV
 
@@ -60,9 +60,12 @@ def tile_attend_pkv4q_rel2_cap_kernel(tc, q_words, q_scales, k_words, k_scales, 
         qs_rows = q_scales[0].rearrange("o (g j) q -> j g o q", j=4)
         for j in range(4):
             nc.scalar.dma_start(q_plane[j:P:32, :].bitcast(I32).rearrange("g (o w) -> g o w", o=PASSES), qs_rows[j].bitcast(I32))
-        vsc_rows = v_scales.rearrange("u (g j) e -> j g u e", j=4)
-        for j in range(4):
-            nc.gpsimd.dma_start(vsc_pool[j:P:32, :].bitcast(I32).rearrange("g (u w) -> g u w", u=POOL_PAGES), vsc_rows[j].bitcast(I32))
+        nc.sync.dma_start(
+            vsc_pool[KS_FIRST : KS_FIRST + 16, :].bitcast(I32).rearrange("f (u w) -> f u w", u=POOL_PAGES),
+            v_scales.rearrange("u f e -> f u e").bitcast(I32),
+        )
+        v_plane = held.tile([P, PAGES * DV], U8, name="v_plane", align_bytes=64)
+        nc.vector.memset(v_plane[:].bitcast(I32), 0)
 
         identity = held.tile([P, P], F32, name="identity", align_bytes=64)
         make_identity(nc, identity[:])
@@ -123,24 +126,23 @@ def tile_attend_pkv4q_rel2_cap_kernel(tc, q_words, q_scales, k_words, k_scales, 
                 nc.tensor.transpose(bank[:, t, :], weight[:, t, :], identity[:])
             turned.append(bank)
 
-        v_plane = held.tile([P, PAGES * DV], U8, name="v_plane", tag="keys", align_bytes=64)
+        vsc_listed = held.tile([P, PAGES * DV], U8, name="vsc_listed", tag="keys", align_bytes=64)
         gather_keys(0)
         for u in range(PAGES):
             if u + 1 < PAGES:
                 gather_keys(u + 1)
             else:
-                nc.vector.tensor_copy(v_plane[:], vsc_pool[:].indirect(value_list[:]))
+                nc.vector.tensor_copy(vsc_listed[:], vsc_pool[:].indirect(value_list[:]))
+                for j in range(4):
+                    nc.sync.dma_start(v_plane[j:P:32, :].bitcast(I32), vsc_listed[KS_FIRST + j : KS_FIRST + 16 : 4, :].bitcast(I32))
             weigh(u)
 
         w_woven = []
         for u in range(PAGES):
             vs_listed = pages.tile([P, PAGE], F32, name="vs_listed", align_bytes=64)
             nc.vector.tensor_copy(vs_listed[:], vs_pool[:].indirect(token_list[:, u * PAGE // 16 : (u + 1) * PAGE // 16]))
-            vs_bank = score_banks.tile([P, PAGE], F32, name="score")
-            for t in range(4):
-                nc.tensor.transpose(vs_bank[:, t * P : (t + 1) * P], vs_listed[:, t:PAGE:4], identity[:])
             cols = pages.tile([P, 4], F32, name="vs_cols", align_bytes=64)
-            nc.scalar.copy(cols[:], vs_bank[:, 0:PAGE:P])
+            nc.sync.dma_start(cols[:], vs_listed[0:1, :])
             w_bf16 = pages.tile([P, NQ, 4], BF16, name="w_bf16", align_bytes=64)
             if u < ON_SCALAR:
                 w_places = pages.tile([P, 4, NQ], BF16, name="w_places", align_bytes=64)

@@ -21,7 +21,7 @@ PAGES = N // PAGE
 POOL_PAGES = T // PAGE
 PASSES = D // 512
 CAP = 2.0
-HALVES = 2
+HALVES = 1
 KS_ROWS = 32
 KS_FIRST = P - KS_ROWS
 ON_SCALAR = 3
@@ -39,61 +39,68 @@ def tile_attend_pkv4q_rel2_cap_kernel(tc, q_words, q_scales, k_words, k_scales, 
         turn_banks = ctx.enter_context(tc.psum_pool(name="turn_banks", bufs=PAGES))
         sum_bank = ctx.enter_context(tc.psum_pool(name="sum_bank", bufs=1))
 
-        ks_pool = held.tile([P, T], U8, name="ks_pool", tag="second", align_bytes=64)
+        ks_pool = held.tile([P, T], U8, name="ks_pool", tag="first", align_bytes=64)
         nc.sync.dma_start(ks_pool[KS_FIRST:P, :].bitcast(I32), k_scales.rearrange("o f t -> (o f) t").bitcast(I32))
         token_list = lists.tile([P, N // 16], U16, name="token_list")
         nc.sync.dma_start(token_list[:], offs)
-        kw_pool = held.tile([P, T], I32, name="kw_pool", tag="keys", align_bytes=64)
+        kw_pool = held.tile([P, T], I32, name="kw_pool", align_bytes=64)
         nc.sync.dma_start(kw_pool[:], k_words[0].rearrange("g t b -> g (t b)").bitcast(I32))
         q_codes = held.tile([P, PASSES, NQ], I32, name="q_codes", align_bytes=64)
         nc.sync.dma_start(q_codes[:], q_words[0].rearrange("o g q r -> g o (q r)").bitcast(I32))
         value_list = lists.tile([P, PAGES * DV // 16], U16, name="value_list")
         nc.sync.dma_start(value_list[:], voffs)
 
-        nc.vector.memset(ks_pool[0:KS_FIRST, :].bitcast(I32), 0)
+        nc.gpsimd.memset(ks_pool[0:KS_FIRST, :].bitcast(I32), 0)
         q_plane = held.tile([P, PASSES * NQ], U8, name="q_plane", align_bytes=64)
-        nc.vector.memset(q_plane[:].bitcast(I32), 0)
-        vsc_pool = held.tile([P, POOL_PAGES * DV], U8, name="vsc_pool", align_bytes=64)
-        nc.vector.memset(vsc_pool[:].bitcast(I32), 0)
-        k_planes = held.tile([P, PASSES * N], U8, name="k_planes", align_bytes=64)
-        nc.vector.memset(k_planes[:].bitcast(I32), 0)
+        nc.gpsimd.memset(q_plane[:].bitcast(I32), 0)
         qs_rows = q_scales[0].rearrange("o (g j) q -> j g o q", j=4)
         for j in range(4):
             nc.scalar.dma_start(q_plane[j:P:32, :].bitcast(I32).rearrange("g (o w) -> g o w", o=PASSES), qs_rows[j].bitcast(I32))
-        nc.sync.dma_start(
-            vsc_pool[KS_FIRST : KS_FIRST + 16, :].bitcast(I32).rearrange("f (u w) -> f u w", u=POOL_PAGES),
-            v_scales.rearrange("u f e -> f u e").bitcast(I32),
-        )
-        v_plane = held.tile([P, PAGES * DV], U8, name="v_plane", align_bytes=64)
-        nc.vector.memset(v_plane[:].bitcast(I32), 0)
-
         identity = held.tile([P, P], F32, name="identity", align_bytes=64)
         make_identity(nc, identity[:])
         sums = held.tile([P, PAGES * HALVES + 1], F32, name="sums")
         nc.gpsimd.memset(sums[:, PAGES * HALVES :], 1.0)
+        k_planes = held.tile([P, PASSES * N], U8, name="k_planes", align_bytes=64)
+        nc.gpsimd.memset(k_planes[:].bitcast(I32), 0)
+        vs_pool = held.tile([P, T], F32, name="vs_pool", align_bytes=64)
+        nc.gpsimd.memset(vs_pool[:], 0.0)
+        vsc_pool = held.tile([P, POOL_PAGES * DV], U8, name="vsc_pool", align_bytes=64)
+        nc.gpsimd.memset(vsc_pool[:].bitcast(I32), 0)
 
-        ks_listed = held.tile([P, N], U8, name="ks_listed", tag="third", align_bytes=64)
+        ks_listed = held.tile([P, N], U8, name="ks_listed", align_bytes=64)
         nc.vector.tensor_copy(ks_listed[:], ks_pool[:].indirect(token_list[:]))
         for o in range(PASSES):
             for j in range(4):
                 row = KS_FIRST + 16 * o
                 nc.sync.dma_start(k_planes[j:P:32, o * N : (o + 1) * N].bitcast(I32), ks_listed[row + j : row + 16 : 4, :].bitcast(I32))
 
-        vs_pool = held.tile([P, T], F32, name="vs_pool", tag="second", align_bytes=64)
-        nc.sync.dma_start(vs_pool[:], vs)
-        vw_pool = held.tile([P, POOL_PAGES * DV], I32, name="vw_pool", tag="third", align_bytes=64)
+        nc.sync.dma_start(vs_pool[0:1, :], vs[0:1, :])
+        vw_pool = held.tile([P, POOL_PAGES * DV], I32, name="vw_pool", tag="first", align_bytes=64)
         nc.sync.dma_start(
             vw_pool[:].rearrange("g (u e) -> g u e", u=POOL_PAGES),
             v_words.rearrange("u g e r -> g u (e r)").bitcast(I32),
         )
+        vsc_rows = v_scales.rearrange("u (g j) e -> j g u e", j=4)
+        for j in range(4):
+            nc.sync.dma_start(vsc_pool[j:P:32, :].bitcast(I32).rearrange("g (u w) -> g u w", u=POOL_PAGES), vsc_rows[j].bitcast(I32))
 
         k_pairs = []
         turned = []
+        scores = []
+        stage = {}
+        vs_cols = []
 
         def gather_keys(u):
-            pairs = pages.tile([P, PAGE], U32, name="k_pairs", align_bytes=64)
+            pairs = held.tile([P, PAGE], U32, name="k_pairs", tag="pairs%d" % (u % 2), align_bytes=64)
             nc.vector.tensor_copy(pairs[:], kw_pool[:].bitcast(U32).indirect(token_list[:, u * PAGE // 16 : (u + 1) * PAGE // 16]))
             k_pairs.append(pairs)
+
+        def gather_vs(u):
+            vs_listed = held.tile([P, PAGE], F32, name="vs_listed", tag="listed%d" % u, align_bytes=64)
+            nc.vector.tensor_copy(vs_listed[:], vs_pool[:].indirect(token_list[:, u * PAGE // 16 : (u + 1) * PAGE // 16]))
+            cols = pages.tile([P, 4], F32, name="vs_cols", align_bytes=64)
+            nc.sync.dma_start(cols[:], vs_listed[0:1, :])
+            vs_cols.append(cols)
 
         def weigh(u):
             k_codes = pages.tile([P, PASSES, PAGE], U16, name="k_codes", align_bytes=64)
@@ -109,79 +116,112 @@ def tile_attend_pkv4q_rel2_cap_kernel(tc, q_words, q_scales, k_words, k_scales, 
                     start=(o == 0),
                     stop=(o == PASSES - 1),
                 )
-            dealt = score[:].rearrange("q (s t) -> q t s", t=4)
+            scores.append(score)
+
+        def cap(u):
             capped = pages.tile([P, 4, P], F32, name="capped", align_bytes=64)
+            nc.scalar.activation(capped[:], scores[u][:].rearrange("q (s t) -> q t s", t=4), ACT.Tanh, scale=1.0 / CAP)
+            stage[u] = capped
+
+        def clip(u):
             positive = pages.tile([P, 4, P], F32, name="positive", align_bytes=64)
-            weight = pages.tile([P, 4, P], F32, name="weight", align_bytes=64)
-            halves = [slice(2 * h, 2 * h + 2) for h in range(HALVES)]
-            for ts in halves:
-                nc.scalar.activation(capped[:, ts, :], dealt[:, ts, :], ACT.Tanh, scale=1.0 / CAP)
-            for ts in halves:
-                nc.scalar.activation(positive[:, ts, :], capped[:, ts, :], ACT.Relu)
-            for h, ts in enumerate(halves):
-                col = u * HALVES + h
-                nc.scalar.activation(weight[:, ts, :], positive[:, ts, :], ACT.Square, scale=CAP, accum_out=sums[:, col : col + 1])
+            nc.scalar.activation(positive[:], stage[u][:], ACT.Relu)
+            stage[u] = positive
+
+        def square(u):
+            weight = held.tile([P, 4, P], F32, name="weight", tag="weight%d" % u, align_bytes=64)
+            nc.scalar.activation(weight[:], stage[u][:], ACT.Square, scale=CAP, accum_out=sums[:, u : u + 1])
             bank = turn_banks.tile([P, 4, NQ], F32, name="turned")
             for t in range(4):
                 nc.tensor.transpose(bank[:, t, :], weight[:, t, :], identity[:])
             turned.append(bank)
 
-        vsc_listed = held.tile([P, PAGES * DV], U8, name="vsc_listed", tag="keys", align_bytes=64)
-        gather_keys(0)
+        for first in range(0, PAGES, 2):
+            for u in (first, first + 1):
+                gather_keys(u)
+            for u in (first, first + 1):
+                weigh(u)
         for u in range(PAGES):
-            if u + 1 < PAGES:
-                gather_keys(u + 1)
-            else:
-                nc.vector.tensor_copy(vsc_listed[:], vsc_pool[:].indirect(value_list[:]))
-                for j in range(4):
-                    nc.sync.dma_start(v_plane[j:P:32, :].bitcast(I32), vsc_listed[KS_FIRST + j : KS_FIRST + 16 : 4, :].bitcast(I32))
-            weigh(u)
+            gather_vs(u)
+        v_plane = held.tile([P, PAGES * DV], U8, name="v_plane", tag="listed0", align_bytes=64)
+        nc.vector.tensor_copy(v_plane[:], vsc_pool[:].indirect(value_list[:]))
 
-        w_woven = []
-        for u in range(PAGES):
-            vs_listed = pages.tile([P, PAGE], F32, name="vs_listed", align_bytes=64)
-            nc.vector.tensor_copy(vs_listed[:], vs_pool[:].indirect(token_list[:, u * PAGE // 16 : (u + 1) * PAGE // 16]))
-            cols = pages.tile([P, 4], F32, name="vs_cols", align_bytes=64)
-            nc.sync.dma_start(cols[:], vs_listed[0:1, :])
-            w_bf16 = pages.tile([P, NQ, 4], BF16, name="w_bf16", align_bytes=64)
-            if u < ON_SCALAR:
-                w_places = pages.tile([P, 4, NQ], BF16, name="w_places", align_bytes=64)
-                for t in range(4):
-                    nc.scalar.activation(w_places[:, t, :], turned[u][:, t, :], ACT.Copy, scale=cols[:, t : t + 1])
-                nc.scalar.copy(w_bf16[:], w_places[:].rearrange("s t q -> s q t"))
-            else:
-                nc.vector.tensor_tensor(
-                    w_bf16[:],
-                    turned[u][:].rearrange("s t q -> s q t"),
-                    cols[:].unsqueeze(1).to_broadcast([P, NQ, 4]),
-                    ALU.mult,
-                )
-            w_woven.append(w_bf16)
+        cap(0)
+        clip(0)
+        for u in range(1, PAGES):
+            cap(u)
+            square(u - 1)
+            clip(u)
+
+        w_woven = {}
+        placed = {}
+        v_codes = {}
+
+        def scale_on_scalar(u):
+            w_places = held.tile([P, 4, NQ], BF16, name="w_places", tag="places%d" % u, align_bytes=64)
+            for t in range(4):
+                nc.scalar.activation(w_places[:, t, :], turned[u][:, t, :], ACT.Copy, scale=vs_cols[u][:, t : t + 1])
+            placed[u] = w_places
+
+        def weave(u):
+            w_bf16 = held.tile([P, NQ, 4], BF16, name="w_bf16", tag="woven%d" % u, align_bytes=64)
+            nc.scalar.copy(w_bf16[:], placed[u][:].rearrange("s t q -> s q t"))
+            w_woven[u] = w_bf16
+
+        def scale_on_vector(u):
+            w_bf16 = held.tile([P, NQ, 4], BF16, name="w_bf16", tag="woven%d" % u, align_bytes=64)
+            nc.vector.tensor_tensor(
+                w_bf16[:],
+                turned[u][:].rearrange("s t q -> s q t"),
+                vs_cols[u][:].unsqueeze(1).to_broadcast([P, NQ, 4]),
+                ALU.mult,
+            )
+            w_woven[u] = w_bf16
+
+        def gather_values(u, tag):
+            codes = held.tile([P, DV], U32, name="v_codes", tag=tag, align_bytes=64)
+            nc.vector.tensor_copy(codes[:], vw_pool[:].bitcast(U32).indirect(value_list[:, u * DV // 16 : (u + 1) * DV // 16]))
+            v_codes[u] = codes
 
         acc = sum_bank.tile([P, DV], F32, name="acc")
-        total = held.tile([P, 1], F32, name="total")
-        inverse = held.tile([P, 1], F32, name="inverse")
-        v_codes = []
-        for u in range(PAGES):
-            codes = pages.tile([P, DV], U32, name="v_codes", align_bytes=64)
-            nc.vector.tensor_copy(codes[:], vw_pool[:].bitcast(U32).indirect(value_list[:, u * DV // 16 : (u + 1) * DV // 16]))
-            v_codes.append(codes)
-        nc.vector.tensor_reduce(total[:], sums[:], mybir.AxisListType.X, ALU.add)
-        for u in range(PAGES):
+        quantised = {}
+
+        def quantise(u):
             w_codes = pages.tile([P, NQ], U32, name="w_codes", align_bytes=64)
             w_plane = pages.tile([P, NQ], U8, name="w_plane", align_bytes=64)
             nc.vector.quantize_mx(out=w_codes[:].bitcast(FP8X4), scales=w_plane[:], in_=w_woven[u][:].rearrange("s q t -> s (q t)"))
-            if u == 0:
-                nc.vector.reciprocal(inverse[:], total[:])
+            quantised[u] = (w_codes, w_plane)
+
+        def multiply(u, first, last):
+            w_codes, w_plane = quantised[u]
             nc.tensor.matmul_mx(
                 out=acc[:],
                 lhsT=w_codes[:].bitcast(FP8X4),
                 lhsT_scale=w_plane[:],
                 rhs=v_codes[u][:].bitcast(FP8X4),
                 rhs_scale=v_plane[:, u * DV : (u + 1) * DV],
-                start=(u == 0),
-                stop=(u == PAGES - 1),
+                start=first,
+                stop=last,
             )
+
+        total = held.tile([P, 1], F32, name="total")
+        inverse = held.tile([P, 1], F32, name="inverse")
+        scale_on_scalar(0)
+        square(PAGES - 1)
+        weave(0)
+        scale_on_scalar(1)
+        scale_on_scalar(2)
+        weave(1)
+        weave(2)
+        for u in range(PAGES):
+            gather_values(u, "codes%d" % u)
+        scale_on_vector(3)
+        nc.vector.tensor_reduce(total[:], sums[:], mybir.AxisListType.X, ALU.add)
+        for u in range(PAGES):
+            quantise(u)
+            if u == 0:
+                nc.vector.reciprocal(inverse[:], total[:])
+            multiply(u, u == 0, u == PAGES - 1)
         result = held.tile([P, DV], F32, name="result")
         nc.scalar.activation(result[:], acc[:], ACT.Copy, scale=inverse[:])
         nc.scalar.dma_start(out[0], result[:])

@@ -24,7 +24,7 @@ CAP = 2.0
 HALVES = 1
 KS_ROWS = 32
 KS_FIRST = P - KS_ROWS
-ON_SCALAR = 3
+ON_SCALAR = 2
 
 FLOPS = 2 * NQ * N * D + 2 * NQ * N * DV
 
@@ -210,18 +210,17 @@ def tile_attend_pkv4q_rel2_cap_kernel(tc, q_words, q_scales, k_words, k_scales, 
         square(PAGES - 1)
         weave(0)
         scale_on_scalar(1)
-        scale_on_scalar(2)
         weave(1)
-        weave(2)
         for u in range(PAGES):
             gather_values(u, "codes%d" % u)
+        scale_on_vector(2)
         scale_on_vector(3)
         nc.vector.tensor_reduce(total[:], sums[:], mybir.AxisListType.X, ALU.add)
-        for u in range(PAGES):
+        for u in (0, 2, 3, 1):
             quantise(u)
             if u == 0:
                 nc.vector.reciprocal(inverse[:], total[:])
-            multiply(u, u == 0, u == PAGES - 1)
+            multiply(u, u == 0, u == 1)
         result = held.tile([P, DV], F32, name="result")
         nc.scalar.activation(result[:], acc[:], ACT.Copy, scale=inverse[:])
         nc.scalar.dma_start(out[0], result[:])

@@ -20,11 +20,12 @@ PAGE = 512
 PAGES = N // PAGE
 POOL_PAGES = T // PAGE
 PASSES = D // 512
+PACK = 4
+BLOCKS = 16
 CAP = 2.0
-HALVES = 1
-KS_ROWS = 32
-KS_FIRST = P - KS_ROWS
-ON_SCALAR = 2
+KS_FIRST = P - PASSES * BLOCKS
+LIST_COLS = PAGE // 16
+SCORE_BANKS = 3
 
 FLOPS = 2 * NQ * N * D + 2 * NQ * N * DV
 
@@ -35,7 +36,7 @@ def tile_attend_pkv4q_rel2_cap_kernel(tc, q_words, q_scales, k_words, k_scales, 
         lists = ctx.enter_context(tc.tile_pool(name="lists", bufs=1))
         held = ctx.enter_context(tc.tile_pool(name="held", bufs=1))
         pages = ctx.enter_context(tc.tile_pool(name="pages", bufs=PAGES))
-        score_banks = ctx.enter_context(tc.psum_pool(name="score_banks", bufs=3))
+        score_banks = ctx.enter_context(tc.psum_pool(name="score_banks", bufs=SCORE_BANKS))
         turn_banks = ctx.enter_context(tc.psum_pool(name="turn_banks", bufs=PAGES))
         sum_bank = ctx.enter_context(tc.psum_pool(name="sum_bank", bufs=1))
 
@@ -58,8 +59,8 @@ def tile_attend_pkv4q_rel2_cap_kernel(tc, q_words, q_scales, k_words, k_scales, 
             nc.scalar.dma_start(q_plane[j:P:32, :].bitcast(I32).rearrange("g (o w) -> g o w", o=PASSES), qs_rows[j].bitcast(I32))
         identity = held.tile([P, P], F32, name="identity", align_bytes=64)
         make_identity(nc, identity[:])
-        sums = held.tile([P, PAGES * HALVES + 1], F32, name="sums")
-        nc.gpsimd.memset(sums[:, PAGES * HALVES :], 1.0)
+        sums = held.tile([P, PAGES + 1], F32, name="sums")
+        nc.gpsimd.memset(sums[:, PAGES:], 1.0)
         k_planes = held.tile([P, PASSES * N], U8, name="k_planes", align_bytes=64)
         nc.gpsimd.memset(k_planes[:].bitcast(I32), 0)
         vs_pool = held.tile([P, T], F32, name="vs_pool", align_bytes=64)
@@ -71,8 +72,8 @@ def tile_attend_pkv4q_rel2_cap_kernel(tc, q_words, q_scales, k_words, k_scales, 
         nc.vector.tensor_copy(ks_listed[:], ks_pool[:].indirect(token_list[:]))
         for o in range(PASSES):
             for j in range(4):
-                row = KS_FIRST + 16 * o
-                nc.sync.dma_start(k_planes[j:P:32, o * N : (o + 1) * N].bitcast(I32), ks_listed[row + j : row + 16 : 4, :].bitcast(I32))
+                row = KS_FIRST + BLOCKS * o
+                nc.sync.dma_start(k_planes[j:P:32, o * N : (o + 1) * N].bitcast(I32), ks_listed[row + j : row + BLOCKS : 4, :].bitcast(I32))
 
         nc.sync.dma_start(vs_pool[0:1, :], vs[0:1, :])
         vw_pool = held.tile([P, POOL_PAGES * DV], I32, name="vw_pool", tag="first", align_bytes=64)
@@ -85,26 +86,35 @@ def tile_attend_pkv4q_rel2_cap_kernel(tc, q_words, q_scales, k_words, k_scales, 
             nc.sync.dma_start(vsc_pool[j:P:32, :].bitcast(I32).rearrange("g (u w) -> g u w", u=POOL_PAGES), vsc_rows[j].bitcast(I32))
 
         k_pairs = []
-        turned = []
         scores = []
-        stage = {}
         vs_cols = []
+        capped = {}
+        positive = {}
+        turned = []
+        placed = {}
+        woven = {}
+        quantised = {}
 
         def gather_keys(u):
             pairs = held.tile([P, PAGE], U32, name="k_pairs", tag="pairs%d" % (u % 2), align_bytes=64)
-            nc.vector.tensor_copy(pairs[:], kw_pool[:].bitcast(U32).indirect(token_list[:, u * PAGE // 16 : (u + 1) * PAGE // 16]))
+            nc.vector.tensor_copy(pairs[:], kw_pool[:].bitcast(U32).indirect(token_list[:, u * LIST_COLS : (u + 1) * LIST_COLS]))
             k_pairs.append(pairs)
 
         def gather_vs(u):
             vs_listed = held.tile([P, PAGE], F32, name="vs_listed", tag="listed%d" % u, align_bytes=64)
-            nc.vector.tensor_copy(vs_listed[:], vs_pool[:].indirect(token_list[:, u * PAGE // 16 : (u + 1) * PAGE // 16]))
-            cols = pages.tile([P, 4], F32, name="vs_cols", align_bytes=64)
+            nc.vector.tensor_copy(vs_listed[:], vs_pool[:].indirect(token_list[:, u * LIST_COLS : (u + 1) * LIST_COLS]))
+            cols = held.tile([P, PACK], F32, name="vs_cols", tag="cols%d" % u, align_bytes=64)
             nc.sync.dma_start(cols[:], vs_listed[0:1, :])
             vs_cols.append(cols)
 
-        def weigh(u):
+        def score_page(u):
             k_codes = pages.tile([P, PASSES, PAGE], U16, name="k_codes", align_bytes=64)
-            nc.vector.tensor_copy(k_codes[:], k_pairs[u][:].bitcast(U16).rearrange("g (i o) -> g o i", o=PASSES))
+            parted = k_pairs[u][:].bitcast(U16).rearrange("g (i o) -> g o i", o=PASSES)
+            if u == 0:
+                for o in range(PASSES):
+                    nc.vector.tensor_copy(k_codes[:, o, :], parted[:, o, :])
+            else:
+                nc.vector.tensor_copy(k_codes[:], parted)
             score = score_banks.tile([P, PAGE], F32, name="score")
             for o in range(PASSES):
                 nc.tensor.matmul_mx(
@@ -119,20 +129,18 @@ def tile_attend_pkv4q_rel2_cap_kernel(tc, q_words, q_scales, k_words, k_scales, 
             scores.append(score)
 
         def cap(u):
-            capped = pages.tile([P, 4, P], F32, name="capped", align_bytes=64)
-            nc.scalar.activation(capped[:], scores[u][:].rearrange("q (s t) -> q t s", t=4), ACT.Tanh, scale=1.0 / CAP)
-            stage[u] = capped
+            capped[u] = pages.tile([P, PACK, P], F32, name="capped", align_bytes=64)
+            nc.scalar.activation(capped[u][:], scores[u][:].rearrange("q (s t) -> q t s", t=PACK), ACT.Tanh, scale=1.0 / CAP)
 
         def clip(u):
-            positive = pages.tile([P, 4, P], F32, name="positive", align_bytes=64)
-            nc.scalar.activation(positive[:], stage[u][:], ACT.Relu)
-            stage[u] = positive
+            positive[u] = pages.tile([P, PACK, P], F32, name="positive", align_bytes=64)
+            nc.scalar.activation(positive[u][:], capped[u][:], ACT.Relu)
 
         def square(u):
-            weight = held.tile([P, 4, P], F32, name="weight", tag="weight%d" % u, align_bytes=64)
-            nc.scalar.activation(weight[:], stage[u][:], ACT.Square, scale=CAP, accum_out=sums[:, u : u + 1])
-            bank = turn_banks.tile([P, 4, NQ], F32, name="turned")
-            for t in range(4):
+            weight = held.tile([P, PACK, P], F32, name="weight", tag="weight%d" % u, align_bytes=64)
+            nc.scalar.activation(weight[:], positive[u][:], ACT.Square, scale=CAP, accum_out=sums[:, u : u + 1])
+            bank = turn_banks.tile([P, PACK, NQ], F32, name="turned")
+            for t in range(PACK):
                 nc.tensor.transpose(bank[:, t, :], weight[:, t, :], identity[:])
             turned.append(bank)
 
@@ -140,7 +148,7 @@ def tile_attend_pkv4q_rel2_cap_kernel(tc, q_words, q_scales, k_words, k_scales, 
             for u in (first, first + 1):
                 gather_keys(u)
             for u in (first, first + 1):
-                weigh(u)
+                score_page(u)
         for u in range(PAGES):
             gather_vs(u)
         v_plane = held.tile([P, PAGES * DV], U8, name="v_plane", tag="listed0", align_bytes=64)
@@ -153,43 +161,30 @@ def tile_attend_pkv4q_rel2_cap_kernel(tc, q_words, q_scales, k_words, k_scales, 
             square(u - 1)
             clip(u)
 
-        w_woven = {}
-        placed = {}
-        v_codes = {}
-
         def scale_on_scalar(u):
-            w_places = held.tile([P, 4, NQ], BF16, name="w_places", tag="places%d" % u, align_bytes=64)
-            for t in range(4):
-                nc.scalar.activation(w_places[:, t, :], turned[u][:, t, :], ACT.Copy, scale=vs_cols[u][:, t : t + 1])
-            placed[u] = w_places
+            placed[u] = held.tile([P, PACK, NQ], BF16, name="w_places", tag="places%d" % u, align_bytes=64)
+            for t in range(PACK):
+                nc.scalar.activation(placed[u][:, t, :], turned[u][:, t, :], ACT.Copy, scale=vs_cols[u][:, t : t + 1])
 
         def weave(u):
-            w_bf16 = held.tile([P, NQ, 4], BF16, name="w_bf16", tag="woven%d" % u, align_bytes=64)
-            nc.scalar.copy(w_bf16[:], placed[u][:].rearrange("s t q -> s q t"))
-            w_woven[u] = w_bf16
+            woven[u] = held.tile([P, NQ, PACK], BF16, name="w_woven", tag="woven%d" % u, align_bytes=64)
+            nc.scalar.copy(woven[u][:], placed[u][:].rearrange("s t q -> s q t"))
 
-        def scale_on_vector(u):
-            w_bf16 = held.tile([P, NQ, 4], BF16, name="w_bf16", tag="woven%d" % u, align_bytes=64)
+        def scale_on_vector(u, slot):
+            woven[u] = held.tile([P, NQ, PACK], BF16, name="w_woven", tag=slot, align_bytes=64)
             nc.vector.tensor_tensor(
-                w_bf16[:],
+                woven[u][:],
                 turned[u][:].rearrange("s t q -> s q t"),
-                vs_cols[u][:].unsqueeze(1).to_broadcast([P, NQ, 4]),
+                vs_cols[u][:].unsqueeze(1).to_broadcast([P, NQ, PACK]),
                 ALU.mult,
             )
-            w_woven[u] = w_bf16
-
-        def gather_values(u, tag):
-            codes = held.tile([P, DV], U32, name="v_codes", tag=tag, align_bytes=64)
-            nc.vector.tensor_copy(codes[:], vw_pool[:].bitcast(U32).indirect(value_list[:, u * DV // 16 : (u + 1) * DV // 16]))
-            v_codes[u] = codes
 
         acc = sum_bank.tile([P, DV], F32, name="acc")
-        quantised = {}
 
-        def quantise(u):
-            w_codes = pages.tile([P, NQ], U32, name="w_codes", align_bytes=64)
+        def quantise(u, slot):
+            w_codes = held.tile([P, NQ], U32, name="w_codes", tag=slot, align_bytes=64)
             w_plane = pages.tile([P, NQ], U8, name="w_plane", align_bytes=64)
-            nc.vector.quantize_mx(out=w_codes[:].bitcast(FP8X4), scales=w_plane[:], in_=w_woven[u][:].rearrange("s q t -> s (q t)"))
+            nc.vector.quantize_mx(out=w_codes[:].bitcast(FP8X4), scales=w_plane[:], in_=woven[u][:].rearrange("s q t -> s (q t)"))
             quantised[u] = (w_codes, w_plane)
 
         def multiply(u, first, last):
@@ -198,29 +193,34 @@ def tile_attend_pkv4q_rel2_cap_kernel(tc, q_words, q_scales, k_words, k_scales, 
                 out=acc[:],
                 lhsT=w_codes[:].bitcast(FP8X4),
                 lhsT_scale=w_plane[:],
-                rhs=v_codes[u][:].bitcast(FP8X4),
+                rhs=v_codes[:, u * DV : (u + 1) * DV].bitcast(FP8X4),
                 rhs_scale=v_plane[:, u * DV : (u + 1) * DV],
                 start=first,
                 stop=last,
             )
 
         total = held.tile([P, 1], F32, name="total")
-        inverse = held.tile([P, 1], F32, name="inverse")
         scale_on_scalar(0)
         square(PAGES - 1)
         weave(0)
         scale_on_scalar(1)
+        summed = held.tile([P, PAGES + 1], F32, name="summed", tag="cols0", align_bytes=64)
+        nc.scalar.activation(summed[:], sums[:], ACT.Copy, accum_out=total[:])
         weave(1)
-        for u in range(PAGES):
-            gather_values(u, "codes%d" % u)
-        scale_on_vector(2)
-        scale_on_vector(3)
-        nc.vector.tensor_reduce(total[:], sums[:], mybir.AxisListType.X, ALU.add)
-        for u in (0, 2, 3, 1):
-            quantise(u)
-            if u == 0:
-                nc.vector.reciprocal(inverse[:], total[:])
-            multiply(u, u == 0, u == 1)
+        v_codes = held.tile([P, PAGES * DV], U32, name="v_codes", align_bytes=64)
+        nc.vector.tensor_copy(v_codes[:], vw_pool[:].bitcast(U32).indirect(value_list[:]))
+        scale_on_vector(3, "woven3")
+        quantise(0, "codes0")
+        multiply(0, True, False)
+        scale_on_vector(2, "places0")
+        quantise(3, "woven0")
+        multiply(3, False, False)
+        quantise(2, "codes2")
+        multiply(2, False, False)
+        quantise(1, "codes1")
+        multiply(1, False, True)
+        inverse = held.tile([P, 1], F32, name="inverse")
+        nc.vector.reciprocal(inverse[:], total[:])
         result = held.tile([P, DV], F32, name="result")
         nc.scalar.activation(result[:], acc[:], ACT.Copy, scale=inverse[:])
         nc.scalar.dma_start(out[0], result[:])

@@ -24,7 +24,10 @@ PACK = 4
 BLOCKS = 16
 CAP = 2.0
 KS_FIRST = P - PASSES * BLOCKS
+VS_FIRST = P - BLOCKS
 LIST_COLS = PAGE // 16
+VLIST_COLS = DV // 16
+RUN = T // P
 SCORE_BANKS = 3
 
 FLOPS = 2 * NQ * N * D + 2 * NQ * N * DV
@@ -40,33 +43,51 @@ def tile_attend_pkv4q_rel2_cap_kernel(tc, q_words, q_scales, k_words, k_scales, 
         turn_banks = ctx.enter_context(tc.psum_pool(name="turn_banks", bufs=PAGES))
         sum_bank = ctx.enter_context(tc.psum_pool(name="sum_bank", bufs=1))
 
+        vs_runs = held.tile([P, RUN], F32, name="vs_runs", align_bytes=64)
+        nc.sync.dma_start(vs_runs[:], vs[0].rearrange("(p c) -> p c", c=RUN))
         ks_pool = held.tile([P, T], U8, name="ks_pool", tag="first", align_bytes=64)
         nc.sync.dma_start(ks_pool[KS_FIRST:P, :].bitcast(I32), k_scales.rearrange("o f t -> (o f) t").bitcast(I32))
         token_list = lists.tile([P, N // 16], U16, name="token_list")
         nc.sync.dma_start(token_list[:], offs)
+        value_list = lists.tile([P, PAGES * DV // 16], U16, name="value_list")
+        nc.sync.dma_start(value_list[:], voffs)
+        vsc_pool = held.tile([P, POOL_PAGES * DV], U8, name="vsc_pool", align_bytes=64)
+        nc.scalar.dma_start(
+            vsc_pool[VS_FIRST:P, :].bitcast(I32).rearrange("f (u w) -> f u w", u=POOL_PAGES),
+            v_scales.rearrange("u f e -> f u e").bitcast(I32),
+        )
         kw_pool = held.tile([P, T], I32, name="kw_pool", align_bytes=64)
         nc.sync.dma_start(kw_pool[:], k_words[0].rearrange("g t b -> g (t b)").bitcast(I32))
         q_codes = held.tile([P, PASSES, NQ], I32, name="q_codes", align_bytes=64)
         nc.sync.dma_start(q_codes[:], q_words[0].rearrange("o g q r -> g o (q r)").bitcast(I32))
-        value_list = lists.tile([P, PAGES * DV // 16], U16, name="value_list")
-        nc.sync.dma_start(value_list[:], voffs)
 
-        nc.gpsimd.memset(ks_pool[0:KS_FIRST, :].bitcast(I32), 0)
+        identity = held.tile([P, P], F32, name="identity", align_bytes=64)
+        make_identity(nc, identity[:])
         q_plane = held.tile([P, PASSES * NQ], U8, name="q_plane", align_bytes=64)
         nc.gpsimd.memset(q_plane[:].bitcast(I32), 0)
         qs_rows = q_scales[0].rearrange("o (g j) q -> j g o q", j=4)
         for j in range(4):
-            nc.scalar.dma_start(q_plane[j:P:32, :].bitcast(I32).rearrange("g (o w) -> g o w", o=PASSES), qs_rows[j].bitcast(I32))
-        identity = held.tile([P, P], F32, name="identity", align_bytes=64)
-        make_identity(nc, identity[:])
-        sums = held.tile([P, PAGES + 1], F32, name="sums")
-        nc.gpsimd.memset(sums[:, PAGES:], 1.0)
+            nc.gpsimd.dma_start(q_plane[j:P:32, :].bitcast(I32).rearrange("g (o w) -> g o w", o=PASSES), qs_rows[j].bitcast(I32))
+
+        nc.vector.memset(ks_pool[0:KS_FIRST, :].bitcast(I32), 0)
+        nc.vector.memset(vsc_pool[0:96, :].bitcast(I32), 0)
+        nc.vector.memset(vsc_pool[96:VS_FIRST, :].bitcast(I32), 0)
         k_planes = held.tile([P, PASSES * N], U8, name="k_planes", align_bytes=64)
-        nc.gpsimd.memset(k_planes[:].bitcast(I32), 0)
+        nc.vector.memset(k_planes[:].bitcast(I32), 0)
+        v_plane = held.tile([P, PAGES * DV], U8, name="v_plane", align_bytes=64)
+        nc.vector.memset(v_plane[:].bitcast(I32), 0)
+        sums = held.tile([P, PAGES + 1], F32, name="sums")
+        nc.vector.memset(sums[:, PAGES:], 1.0 / (CAP * CAP))
+
         vs_pool = held.tile([P, T], F32, name="vs_pool", align_bytes=64)
-        nc.gpsimd.memset(vs_pool[:], 0.0)
-        vsc_pool = held.tile([P, POOL_PAGES * DV], U8, name="vsc_pool", align_bytes=64)
-        nc.gpsimd.memset(vsc_pool[:].bitcast(I32), 0)
+        vs_dealt = vs_pool[:].rearrange("m (u t a h i) -> m t h u a i", u=POOL_PAGES, t=PACK, h=2, i=PACK)
+        for t in range(PACK):
+            for h in range(2):
+                spread = turn_banks.tile([P, PACK, P], F32, name="turned")
+                for i in range(PACK):
+                    c = t + PACK * (PACK * h + i)
+                    nc.tensor.transpose(spread[:, i, :], vs_runs[:, c : c + 1].to_broadcast([P, P]), identity[:])
+                nc.scalar.activation(vs_dealt[:, t, h], spread[:].rearrange("m i (u a) -> m u a i", u=POOL_PAGES), ACT.Copy)
 
         ks_listed = held.tile([P, N], U8, name="ks_listed", align_bytes=64)
         nc.vector.tensor_copy(ks_listed[:], ks_pool[:].indirect(token_list[:]))
@@ -74,38 +95,32 @@ def tile_attend_pkv4q_rel2_cap_kernel(tc, q_words, q_scales, k_words, k_scales, 
             for j in range(4):
                 row = KS_FIRST + BLOCKS * o
                 nc.sync.dma_start(k_planes[j:P:32, o * N : (o + 1) * N].bitcast(I32), ks_listed[row + j : row + BLOCKS : 4, :].bitcast(I32))
-
-        nc.sync.dma_start(vs_pool[0:1, :], vs[0:1, :])
+        vsc_listed = held.tile([P, PAGES * DV], U8, name="vsc_listed", align_bytes=64)
+        nc.vector.tensor_copy(vsc_listed[:], vsc_pool[:].indirect(value_list[:]))
         vw_pool = held.tile([P, POOL_PAGES * DV], I32, name="vw_pool", tag="first", align_bytes=64)
         nc.sync.dma_start(
             vw_pool[:].rearrange("g (u e) -> g u e", u=POOL_PAGES),
             v_words.rearrange("u g e r -> g u (e r)").bitcast(I32),
         )
-        vsc_rows = v_scales.rearrange("u (g j) e -> j g u e", j=4)
         for j in range(4):
-            nc.sync.dma_start(vsc_pool[j:P:32, :].bitcast(I32).rearrange("g (u w) -> g u w", u=POOL_PAGES), vsc_rows[j].bitcast(I32))
+            nc.sync.dma_start(v_plane[j:P:32, :].bitcast(I32), vsc_listed[VS_FIRST + j : P : 4, :].bitcast(I32))
 
-        k_pairs = []
-        scores = []
-        vs_cols = []
+        k_pairs = {}
+        scores = {}
         capped = {}
         positive = {}
-        turned = []
-        placed = {}
+        squared = {}
+        turned = {}
         woven = {}
+        v_codes = {}
         quantised = {}
 
-        def gather_keys(u):
-            pairs = held.tile([P, PAGE], U32, name="k_pairs", tag="pairs%d" % (u % 2), align_bytes=64)
-            nc.vector.tensor_copy(pairs[:], kw_pool[:].bitcast(U32).indirect(token_list[:, u * LIST_COLS : (u + 1) * LIST_COLS]))
-            k_pairs.append(pairs)
+        def page_offsets(u):
+            return token_list[:, u * LIST_COLS : (u + 1) * LIST_COLS]
 
-        def gather_vs(u):
-            vs_listed = held.tile([P, PAGE], F32, name="vs_listed", tag="listed%d" % u, align_bytes=64)
-            nc.vector.tensor_copy(vs_listed[:], vs_pool[:].indirect(token_list[:, u * LIST_COLS : (u + 1) * LIST_COLS]))
-            cols = held.tile([P, PACK], F32, name="vs_cols", tag="cols%d" % u, align_bytes=64)
-            nc.sync.dma_start(cols[:], vs_listed[0:1, :])
-            vs_cols.append(cols)
+        def gather_keys(u):
+            k_pairs[u] = held.tile([P, PAGE], U32, name="k_pairs", tag="pairs%d" % u, align_bytes=64)
+            nc.vector.tensor_copy(k_pairs[u][:], kw_pool[:].bitcast(U32).indirect(page_offsets(u)))
 
         def score_page(u):
             k_codes = pages.tile([P, PASSES, PAGE], U16, name="k_codes", align_bytes=64)
@@ -115,10 +130,10 @@ def tile_attend_pkv4q_rel2_cap_kernel(tc, q_words, q_scales, k_words, k_scales, 
                     nc.vector.tensor_copy(k_codes[:, o, :], parted[:, o, :])
             else:
                 nc.vector.tensor_copy(k_codes[:], parted)
-            score = score_banks.tile([P, PAGE], F32, name="score")
+            scores[u] = score_banks.tile([P, PAGE], F32, name="score")
             for o in range(PASSES):
                 nc.tensor.matmul_mx(
-                    out=score[:],
+                    out=scores[u][:],
                     lhsT=q_codes[:, o, :].bitcast(FP8X4),
                     lhsT_scale=q_plane[:, o * NQ : (o + 1) * NQ],
                     rhs=k_codes[:, o, :].bitcast(FP4X4),
@@ -126,63 +141,49 @@ def tile_attend_pkv4q_rel2_cap_kernel(tc, q_words, q_scales, k_words, k_scales, 
                     start=(o == 0),
                     stop=(o == PASSES - 1),
                 )
-            scores.append(score)
 
         def cap(u):
-            capped[u] = pages.tile([P, PACK, P], F32, name="capped", align_bytes=64)
-            nc.scalar.activation(capped[u][:], scores[u][:].rearrange("q (s t) -> q t s", t=PACK), ACT.Tanh, scale=1.0 / CAP)
+            capped[u] = pages.tile([P, PAGE], F32, name="capped", align_bytes=64)
+            nc.scalar.activation(
+                capped[u][:].rearrange("q (t s) -> q t s", t=PACK),
+                scores[u][:].rearrange("q (s t) -> q t s", t=PACK),
+                ACT.Tanh,
+                scale=1.0 / CAP,
+            )
 
         def clip(u):
-            positive[u] = pages.tile([P, PACK, P], F32, name="positive", align_bytes=64)
+            positive[u] = pages.tile([P, PAGE], F32, name="positive", align_bytes=64)
             nc.scalar.activation(positive[u][:], capped[u][:], ACT.Relu)
 
         def square(u):
-            weight = held.tile([P, PACK, P], F32, name="weight", tag="weight%d" % u, align_bytes=64)
-            nc.scalar.activation(weight[:], positive[u][:], ACT.Square, scale=CAP, accum_out=sums[:, u : u + 1])
-            bank = turn_banks.tile([P, PACK, NQ], F32, name="turned")
+            squared[u] = held.tile([P, PAGE], F32, name="squared", tag="squared%d" % u, align_bytes=64)
+            nc.scalar.activation(squared[u][:], positive[u][:], ACT.Square, accum_out=sums[:, u : u + 1])
+
+        def clip_square(u):
+            squared[u] = held.tile([P, PAGE], F32, name="squared", tag="squared%d" % u, align_bytes=64)
+            nc.vector.scalar_tensor_tensor(squared[u][:], capped[u][:], 0.0, capped[u][:], ALU.max, ALU.mult, accum_out=sums[:, u : u + 1])
+
+        def scale(u):
+            weight = pages.tile([P, PAGE], F32, name="weight", align_bytes=64)
+            nc.vector.tensor_tensor(weight[:], vs_pool[:].indirect(page_offsets(u)), squared[u][:], ALU.mult)
+            turned[u] = turn_banks.tile([P, PACK, NQ], F32, name="turned")
             for t in range(PACK):
-                nc.tensor.transpose(bank[:, t, :], weight[:, t, :], identity[:])
-            turned.append(bank)
-
-        for first in range(0, PAGES, 2):
-            for u in (first, first + 1):
-                gather_keys(u)
-            for u in (first, first + 1):
-                score_page(u)
-        for u in range(PAGES):
-            gather_vs(u)
-        v_plane = held.tile([P, PAGES * DV], U8, name="v_plane", tag="listed0", align_bytes=64)
-        nc.vector.tensor_copy(v_plane[:], vsc_pool[:].indirect(value_list[:]))
-
-        cap(0)
-        clip(0)
-        for u in range(1, PAGES):
-            cap(u)
-            square(u - 1)
-            clip(u)
-
-        def scale_on_scalar(u):
-            placed[u] = held.tile([P, PACK, NQ], BF16, name="w_places", tag="places%d" % u, align_bytes=64)
-            for t in range(PACK):
-                nc.scalar.activation(placed[u][:, t, :], turned[u][:, t, :], ACT.Copy, scale=vs_cols[u][:, t : t + 1])
+                nc.tensor.transpose(turned[u][:, t, :], weight[:, t * P : (t + 1) * P], identity[:])
 
         def weave(u):
-            woven[u] = held.tile([P, NQ, PACK], BF16, name="w_woven", tag="woven%d" % u, align_bytes=64)
-            nc.scalar.copy(woven[u][:], placed[u][:].rearrange("s t q -> s q t"))
+            woven[u] = pages.tile([P, NQ, PACK], BF16, name="woven", align_bytes=64)
+            nc.scalar.activation(woven[u][:], turned[u][:].rearrange("s t q -> s q t"), ACT.Copy, scale=CAP * CAP)
 
-        def scale_on_vector(u, slot):
-            woven[u] = held.tile([P, NQ, PACK], BF16, name="w_woven", tag=slot, align_bytes=64)
-            nc.vector.tensor_tensor(
-                woven[u][:],
-                turned[u][:].rearrange("s t q -> s q t"),
-                vs_cols[u][:].unsqueeze(1).to_broadcast([P, NQ, PACK]),
-                ALU.mult,
-            )
+        def gather_values(first, slot):
+            both = held.tile([P, 2 * DV], U32, name="v_codes", tag=slot, align_bytes=64)
+            nc.vector.tensor_copy(both[:], vw_pool[:].bitcast(U32).indirect(value_list[:, first * VLIST_COLS : (first + 2) * VLIST_COLS]))
+            for u in (first, first + 1):
+                v_codes[u] = both[:, (u - first) * DV : (u - first + 1) * DV]
 
         acc = sum_bank.tile([P, DV], F32, name="acc")
 
-        def quantise(u, slot):
-            w_codes = held.tile([P, NQ], U32, name="w_codes", tag=slot, align_bytes=64)
+        def quantise(u):
+            w_codes = pages.tile([P, NQ], U32, name="w_codes", align_bytes=64)
             w_plane = pages.tile([P, NQ], U8, name="w_plane", align_bytes=64)
             nc.vector.quantize_mx(out=w_codes[:].bitcast(FP8X4), scales=w_plane[:], in_=woven[u][:].rearrange("s q t -> s (q t)"))
             quantised[u] = (w_codes, w_plane)
@@ -193,34 +194,51 @@ def tile_attend_pkv4q_rel2_cap_kernel(tc, q_words, q_scales, k_words, k_scales, 
                 out=acc[:],
                 lhsT=w_codes[:].bitcast(FP8X4),
                 lhsT_scale=w_plane[:],
-                rhs=v_codes[:, u * DV : (u + 1) * DV].bitcast(FP8X4),
+                rhs=v_codes[u].bitcast(FP8X4),
                 rhs_scale=v_plane[:, u * DV : (u + 1) * DV],
                 start=first,
                 stop=last,
             )
 
-        total = held.tile([P, 1], F32, name="total")
-        scale_on_scalar(0)
-        square(PAGES - 1)
+        gather_keys(0)
+        for u in range(1, PAGES):
+            gather_keys(u)
+            score_page(u - 1)
+        score_page(PAGES - 1)
+
+        cap(0)
+        clip(0)
+        cap(1)
+        square(0)
+        gather_values(0, "pairs2")
+        scale(0)
+        cap(2)
+        clip(1)
+        clip_square(2)
+        scale(2)
+        cap(3)
+        square(1)
         weave(0)
-        scale_on_scalar(1)
-        summed = held.tile([P, PAGES + 1], F32, name="summed", tag="cols0", align_bytes=64)
-        nc.scalar.activation(summed[:], sums[:], ACT.Copy, accum_out=total[:])
-        weave(1)
-        v_codes = held.tile([P, PAGES * DV], U32, name="v_codes", align_bytes=64)
-        nc.vector.tensor_copy(v_codes[:], vw_pool[:].bitcast(U32).indirect(value_list[:]))
-        scale_on_vector(3, "woven3")
-        quantise(0, "codes0")
+        clip_square(3)
+        scale(1)
+        scale(3)
+        weave(2)
+        quantise(0)
         multiply(0, True, False)
-        scale_on_vector(2, "places0")
-        quantise(3, "woven0")
-        multiply(3, False, False)
-        quantise(2, "codes2")
+        gather_values(2, "squared1")
+        weave(1)
+        total = held.tile([P, 1], F32, name="total")
+        summed = held.tile([P, PAGES + 1], F32, name="summed")
+        nc.scalar.activation(summed[:], sums[:], ACT.Copy, scale=CAP * CAP, accum_out=total[:])
+        weave(3)
+        quantise(2)
+        quantise(1)
+        multiply(1, False, False)
         multiply(2, False, False)
-        quantise(1, "codes1")
-        multiply(1, False, True)
         inverse = held.tile([P, 1], F32, name="inverse")
         nc.vector.reciprocal(inverse[:], total[:])
+        quantise(3)
+        multiply(3, False, True)
         result = held.tile([P, DV], F32, name="result")
         nc.scalar.activation(result[:], acc[:], ACT.Copy, scale=inverse[:])
         nc.scalar.dma_start(out[0], result[:])

@@ -46,7 +46,7 @@ def tile_attend_pkv4q_rel2_cap_kernel(tc, q_words, q_scales, k_words, k_scales, 
         vs_runs = held.tile([P, RUN], F32, name="vs_runs", align_bytes=64)
         nc.sync.dma_start(vs_runs[:], vs[0].rearrange("(p c) -> p c", c=RUN))
         ks_pool = held.tile([P, T], U8, name="ks_pool", tag="first", align_bytes=64)
-        nc.sync.dma_start(ks_pool[KS_FIRST:P, :].bitcast(I32), k_scales.rearrange("o f t -> (o f) t").bitcast(I32))
+        nc.sync.dma_start(ks_pool[KS_FIRST:P, :].bitcast(I32), k_scales.rearrange("o f t -> f o t").bitcast(I32))
         token_list = lists.tile([P, N // 16], U16, name="token_list")
         nc.sync.dma_start(token_list[:], offs)
         value_list = lists.tile([P, PAGES * DV // 16], U16, name="value_list")
@@ -67,7 +67,7 @@ def tile_attend_pkv4q_rel2_cap_kernel(tc, q_words, q_scales, k_words, k_scales, 
         nc.gpsimd.memset(q_plane[:].bitcast(I32), 0)
         qs_rows = q_scales[0].rearrange("o (g j) q -> j g o q", j=4)
         for j in range(4):
-            nc.gpsimd.dma_start(q_plane[j:P:32, :].bitcast(I32).rearrange("g (o w) -> g o w", o=PASSES), qs_rows[j].bitcast(I32))
+            nc.sync.dma_start(q_plane[j:P:32, :].bitcast(I32).rearrange("g (o w) -> g o w", o=PASSES), qs_rows[j].bitcast(I32))
 
         nc.vector.memset(ks_pool[0:KS_FIRST, :].bitcast(I32), 0)
         nc.vector.memset(vsc_pool[0:96, :].bitcast(I32), 0)
@@ -91,10 +91,9 @@ def tile_attend_pkv4q_rel2_cap_kernel(tc, q_words, q_scales, k_words, k_scales, 
 
         ks_listed = held.tile([P, N], U8, name="ks_listed", align_bytes=64)
         nc.vector.tensor_copy(ks_listed[:], ks_pool[:].indirect(token_list[:]))
-        for o in range(PASSES):
-            for j in range(4):
-                row = KS_FIRST + BLOCKS * o
-                nc.sync.dma_start(k_planes[j:P:32, o * N : (o + 1) * N].bitcast(I32), ks_listed[row + j : row + BLOCKS : 4, :].bitcast(I32))
+        for g in range(4):
+            row = KS_FIRST + 8 * g
+            nc.sync.dma_start(k_planes[32 * g : 32 * g + 4, :].bitcast(I32), ks_listed[row : row + 8, :].bitcast(I32))
         vsc_listed = held.tile([P, PAGES * DV], U8, name="vsc_listed", align_bytes=64)
         nc.vector.tensor_copy(vsc_listed[:], vsc_pool[:].indirect(value_list[:]))
         vw_pool = held.tile([P, POOL_PAGES * DV], I32, name="vw_pool", tag="first", align_bytes=64)

@@ -27,7 +27,8 @@ KS_FIRST = P - PASSES * BLOCKS
 VS_FIRST = P - BLOCKS
 LIST_COLS = PAGE // 16
 VLIST_COLS = DV // 16
-RUN = T // P
+RUN = PACK * PACK
+HALVES = T // (P * RUN)
 SCORE_BANKS = 3
 
 FLOPS = 2 * NQ * N * D + 2 * NQ * N * DV
@@ -43,8 +44,8 @@ def tile_attend_pkv4q_rel2_cap_kernel(tc, q_words, q_scales, k_words, k_scales, 
         turn_banks = ctx.enter_context(tc.psum_pool(name="turn_banks", bufs=PAGES))
         sum_bank = ctx.enter_context(tc.psum_pool(name="sum_bank", bufs=1))
 
-        vs_runs = held.tile([P, RUN], F32, name="vs_runs", align_bytes=64)
-        nc.sync.dma_start(vs_runs[:], vs[0].rearrange("(p c) -> p c", c=RUN))
+        vs_runs = held.tile([P, HALVES, RUN], F32, name="vs_runs", align_bytes=64)
+        nc.sync.dma_start(vs_runs[:], vs[0].rearrange("(h p c) -> p h c", h=HALVES, c=RUN))
         ks_pool = held.tile([P, T], U8, name="ks_pool", tag="first", align_bytes=64)
         nc.sync.dma_start(ks_pool[KS_FIRST:P, :].bitcast(I32), k_scales.rearrange("o f t -> f o t").bitcast(I32))
         token_list = lists.tile([P, N // 16], U16, name="token_list")
@@ -80,14 +81,14 @@ def tile_attend_pkv4q_rel2_cap_kernel(tc, q_words, q_scales, k_words, k_scales, 
         nc.vector.memset(sums[:, PAGES:], 1.0 / (CAP * CAP))
 
         vs_pool = held.tile([P, T], F32, name="vs_pool", align_bytes=64)
-        vs_dealt = vs_pool[:].rearrange("m (u t a h i) -> m t h u a i", u=POOL_PAGES, t=PACK, h=2, i=PACK)
-        for t in range(PACK):
-            for h in range(2):
+        vs_dealt = vs_pool[:].rearrange("m (h a t b i) -> m h t a b i", h=HALVES, a=POOL_PAGES // HALVES, t=PACK, i=PACK)
+        for h in range(HALVES):
+            for t in range(PACK):
                 spread = turn_banks.tile([P, PACK, P], F32, name="turned")
                 for i in range(PACK):
-                    c = t + PACK * (PACK * h + i)
-                    nc.tensor.transpose(spread[:, i, :], vs_runs[:, c : c + 1].to_broadcast([P, P]), identity[:])
-                nc.scalar.activation(vs_dealt[:, t, h], spread[:].rearrange("m i (u a) -> m u a i", u=POOL_PAGES), ACT.Copy)
+                    c = PACK * i + t
+                    nc.tensor.transpose(spread[:, i, :], vs_runs[:, h, c : c + 1].to_broadcast([P, P]), identity[:])
+                nc.scalar.activation(vs_dealt[:, h, t], spread[:].rearrange("m i (a b) -> m a b i", a=POOL_PAGES // HALVES), ACT.Copy)
 
         ks_listed = held.tile([P, N], U8, name="ks_listed", align_bytes=64)
         nc.vector.tensor_copy(ks_listed[:], ks_pool[:].indirect(token_list[:]))

@@ -68,7 +68,8 @@ def tile_attend_pkv4q_rel2_cap_kernel(tc, q_words, q_scales, k_words, k_scales, 
         nc.gpsimd.memset(q_plane[:].bitcast(I32), 0)
         qs_rows = q_scales[0].rearrange("o (g j) q -> j g o q", j=4)
         for j in range(4):
-            nc.sync.dma_start(q_plane[j:P:32, :].bitcast(I32).rearrange("g (o w) -> g o w", o=PASSES), qs_rows[j].bitcast(I32))
+            queue = nc.gpsimd if j < 2 else nc.sync
+            queue.dma_start(q_plane[j:P:32, :].bitcast(I32).rearrange("g (o w) -> g o w", o=PASSES), qs_rows[j].bitcast(I32))
 
         nc.vector.memset(ks_pool[0:KS_FIRST, :].bitcast(I32), 0)
         nc.vector.memset(vsc_pool[0:96, :].bitcast(I32), 0)
@@ -119,7 +120,7 @@ def tile_attend_pkv4q_rel2_cap_kernel(tc, q_words, q_scales, k_words, k_scales, 
             return token_list[:, u * LIST_COLS : (u + 1) * LIST_COLS]
 
         def gather_keys(u):
-            k_pairs[u] = held.tile([P, PAGE], U32, name="k_pairs", tag="pairs%d" % u, align_bytes=64)
+            k_pairs[u] = held.tile([P, PAGE], U32, name="k_pairs", tag="pairs%d" % (u % 2), align_bytes=64)
             nc.vector.tensor_copy(k_pairs[u][:], kw_pool[:].bitcast(U32).indirect(page_offsets(u)))
 
         def score_page(u):
@@ -152,7 +153,7 @@ def tile_attend_pkv4q_rel2_cap_kernel(tc, q_words, q_scales, k_words, k_scales, 
             )
 
         def clip(u):
-            positive[u] = pages.tile([P, PAGE], F32, name="positive", align_bytes=64)
+            positive[u] = held.tile([P, PAGE], F32, name="positive", tag="positive%d" % u, align_bytes=64)
             nc.scalar.activation(positive[u][:], capped[u][:], ACT.Relu)
 
         def square(u):
@@ -163,16 +164,21 @@ def tile_attend_pkv4q_rel2_cap_kernel(tc, q_words, q_scales, k_words, k_scales, 
             squared[u] = held.tile([P, PAGE], F32, name="squared", tag="squared%d" % u, align_bytes=64)
             nc.vector.scalar_tensor_tensor(squared[u][:], capped[u][:], 0.0, capped[u][:], ALU.max, ALU.mult, accum_out=sums[:, u : u + 1])
 
-        def scale(u):
-            weight = pages.tile([P, PAGE], F32, name="weight", align_bytes=64)
-            nc.vector.tensor_tensor(weight[:], vs_pool[:].indirect(page_offsets(u)), squared[u][:], ALU.mult)
+        def scale(u, parts=1):
+            weight = held.tile([P, PAGE], F32, name="weight", tag="weight%d" % u, align_bytes=64)
             turned[u] = turn_banks.tile([P, PACK, NQ], F32, name="turned")
-            for t in range(PACK):
-                nc.tensor.transpose(turned[u][:, t, :], weight[:, t * P : (t + 1) * P], identity[:])
+            width = PAGE // parts
+            for part in range(parts):
+                cols = slice(part * width, (part + 1) * width)
+                offsets = page_offsets(u)[:, part * width // 16 : (part + 1) * width // 16]
+                nc.vector.tensor_tensor(weight[:, cols], vs_pool[:].indirect(offsets), squared[u][:, cols], ALU.mult)
+                for t in range(part * width // P, (part + 1) * width // P):
+                    nc.tensor.transpose(turned[u][:, t, :], weight[:, t * P : (t + 1) * P], identity[:])
 
         def weave(u):
-            woven[u] = pages.tile([P, NQ, PACK], BF16, name="woven", align_bytes=64)
-            nc.scalar.activation(woven[u][:], turned[u][:].rearrange("s t q -> s q t"), ACT.Copy, scale=CAP * CAP)
+            tile = pages.tile([P, NQ, PACK], BF16, name="woven", align_bytes=64)
+            woven[u] = tile[:]
+            nc.scalar.activation(woven[u], turned[u][:].rearrange("s t q -> s q t"), ACT.Copy, scale=CAP * CAP)
 
         def gather_values(first, slot):
             both = held.tile([P, 2 * DV], U32, name="v_codes", tag=slot, align_bytes=64)
@@ -182,17 +188,16 @@ def tile_attend_pkv4q_rel2_cap_kernel(tc, q_words, q_scales, k_words, k_scales, 
 
         acc = sum_bank.tile([P, DV], F32, name="acc")
 
-        def quantise(u):
-            w_codes = pages.tile([P, NQ], U32, name="w_codes", align_bytes=64)
+        def quantise(u, w_codes):
             w_plane = pages.tile([P, NQ], U8, name="w_plane", align_bytes=64)
-            nc.vector.quantize_mx(out=w_codes[:].bitcast(FP8X4), scales=w_plane[:], in_=woven[u][:].rearrange("s q t -> s (q t)"))
+            nc.vector.quantize_mx(out=w_codes.bitcast(FP8X4), scales=w_plane[:], in_=woven[u].rearrange("s q t -> s (q t)"))
             quantised[u] = (w_codes, w_plane)
 
         def multiply(u, first, last):
             w_codes, w_plane = quantised[u]
             nc.tensor.matmul_mx(
                 out=acc[:],
-                lhsT=w_codes[:].bitcast(FP8X4),
+                lhsT=w_codes.bitcast(FP8X4),
                 lhsT_scale=w_plane[:],
                 rhs=v_codes[u].bitcast(FP8X4),
                 rhs_scale=v_plane[:, u * DV : (u + 1) * DV],
@@ -200,44 +205,45 @@ def tile_attend_pkv4q_rel2_cap_kernel(tc, q_words, q_scales, k_words, k_scales, 
                 stop=last,
             )
 
-        gather_keys(0)
-        for u in range(1, PAGES):
-            gather_keys(u)
-            score_page(u - 1)
-        score_page(PAGES - 1)
+        for first in range(0, PAGES, 2):
+            for u in (first, first + 1):
+                gather_keys(u)
+            for u in (first, first + 1):
+                score_page(u)
 
         cap(0)
-        clip(0)
         cap(1)
-        square(0)
-        gather_values(0, "pairs2")
-        scale(0)
+        clip(0)
         cap(2)
-        clip(1)
-        clip_square(2)
-        scale(2)
+        square(0)
         cap(3)
-        square(1)
-        weave(0)
-        clip_square(3)
+        gather_values(0, "pairs1")
+        clip_square(1)
         scale(1)
-        scale(3)
-        weave(2)
-        quantise(0)
-        multiply(0, True, False)
-        gather_values(2, "squared1")
+        clip_square(2)
+        scale(0)
+        clip_square(3)
+        scale(2)
+        scale(3, parts=2)
         weave(1)
+        weave(0)
         total = held.tile([P, 1], F32, name="total")
         summed = held.tile([P, PAGES + 1], F32, name="summed")
         nc.scalar.activation(summed[:], sums[:], ACT.Copy, scale=CAP * CAP, accum_out=total[:])
+        weave(2)
         weave(3)
-        quantise(2)
-        quantise(1)
-        multiply(1, False, False)
-        multiply(2, False, False)
-        inverse = held.tile([P, 1], F32, name="inverse")
+        gather_values(2, "squared3")
+        early_codes = held.tile([P, 2, NQ], U32, name="early_codes", tag="first", align_bytes=64)
+        quantise(1, early_codes[:, 0])
+        quantise(0, early_codes[:, 1])
+        inverse = held.tile([P, 1], F32, name="inverse", tag="weight3", align_bytes=64)
         nc.vector.reciprocal(inverse[:], total[:])
-        quantise(3)
+        late_codes = held.tile([P, 2, NQ], U32, name="late_codes", align_bytes=64)
+        quantise(2, late_codes[:, 0])
+        quantise(3, late_codes[:, 1])
+        multiply(1, True, False)
+        multiply(0, False, False)
+        multiply(2, False, False)
         multiply(3, False, True)
         result = held.tile([P, DV], F32, name="result")
         nc.scalar.activation(result[:], acc[:], ACT.Copy, scale=inverse[:])

@@ -125,12 +125,13 @@ def tile_attend_pkv4q_rel2_cap_kernel(tc, q_words, q_scales, k_words, k_scales, 
 
         def score_page(u):
             k_codes = pages.tile([P, PASSES, PAGE], U16, name="k_codes", align_bytes=64)
-            parted = k_pairs[u][:].bitcast(U16).rearrange("g (i o) -> g o i", o=PASSES)
+            words = k_pairs[u][:].bitcast(U16)
             if u == 0:
+                parted = words.rearrange("g (i o) -> g o i", o=PASSES)
                 for o in range(PASSES):
                     nc.vector.tensor_copy(k_codes[:, o, :], parted[:, o, :])
             else:
-                nc.vector.tensor_copy(k_codes[:], parted)
+                nc.vector.tensor_copy(k_codes[:].rearrange("g o (h i) -> g h o i", h=2), words.rearrange("g (h i o) -> g h o i", h=2, o=PASSES))
             scores[u] = score_banks.tile([P, PAGE], F32, name="score")
             for o in range(PASSES):
                 nc.tensor.matmul_mx(
@@ -154,15 +155,11 @@ def tile_attend_pkv4q_rel2_cap_kernel(tc, q_words, q_scales, k_words, k_scales, 
 
         def clip(u):
             positive[u] = held.tile([P, PAGE], F32, name="positive", tag="positive%d" % u, align_bytes=64)
-            nc.scalar.activation(positive[u][:], capped[u][:], ACT.Relu)
+            nc.vector.tensor_scalar(positive[u][:], capped[u][:], 0.0, None, ALU.max)
 
         def square(u):
             squared[u] = held.tile([P, PAGE], F32, name="squared", tag="squared%d" % u, align_bytes=64)
             nc.scalar.activation(squared[u][:], positive[u][:], ACT.Square, accum_out=sums[:, u : u + 1])
-
-        def clip_square(u):
-            squared[u] = held.tile([P, PAGE], F32, name="squared", tag="squared%d" % u, align_bytes=64)
-            nc.vector.scalar_tensor_tensor(squared[u][:], capped[u][:], 0.0, capped[u][:], ALU.max, ALU.mult, accum_out=sums[:, u : u + 1])
 
         def scale(u, parts=1):
             weight = held.tile([P, PAGE], F32, name="weight", tag="weight%d" % u, align_bytes=64)
@@ -214,19 +211,22 @@ def tile_attend_pkv4q_rel2_cap_kernel(tc, q_words, q_scales, k_words, k_scales, 
         cap(0)
         cap(1)
         clip(0)
+        clip(1)
+        gather_values(0, "pairs0")
         cap(2)
         square(0)
+        clip(2)
         cap(3)
-        gather_values(0, "pairs1")
-        clip_square(1)
-        scale(1)
-        clip_square(2)
         scale(0)
-        clip_square(3)
+        square(1)
+        clip(3)
+        scale(1)
+        square(2)
         scale(2)
+        square(3)
         scale(3, parts=2)
-        weave(1)
         weave(0)
+        weave(1)
         total = held.tile([P, 1], F32, name="total")
         summed = held.tile([P, PAGES + 1], F32, name="summed")
         nc.scalar.activation(summed[:], sums[:], ACT.Copy, scale=CAP * CAP, accum_out=total[:])
@@ -234,17 +234,15 @@ def tile_attend_pkv4q_rel2_cap_kernel(tc, q_words, q_scales, k_words, k_scales, 
         weave(3)
         gather_values(2, "squared3")
         early_codes = held.tile([P, 2, NQ], U32, name="early_codes", tag="first", align_bytes=64)
-        quantise(1, early_codes[:, 0])
-        quantise(0, early_codes[:, 1])
+        quantise(0, early_codes[:, 0])
+        quantise(1, early_codes[:, 1])
         inverse = held.tile([P, 1], F32, name="inverse", tag="weight3", align_bytes=64)
         nc.vector.reciprocal(inverse[:], total[:])
         late_codes = held.tile([P, 2, NQ], U32, name="late_codes", align_bytes=64)
         quantise(2, late_codes[:, 0])
         quantise(3, late_codes[:, 1])
-        multiply(1, True, False)
-        multiply(0, False, False)
-        multiply(2, False, False)
-        multiply(3, False, True)
+        for u in range(PAGES):
+            multiply(u, u == 0, u == PAGES - 1)
         result = held.tile([P, DV], F32, name="result")
         nc.scalar.activation(result[:], acc[:], ACT.Copy, scale=inverse[:])
         nc.scalar.dma_start(out[0], result[:])

@@ -26,7 +26,6 @@ CAP = 2.0
 KS_FIRST = P - PASSES * BLOCKS
 VS_FIRST = P - BLOCKS
 LIST_COLS = PAGE // 16
-VLIST_COLS = DV // 16
 RUN = PACK * PACK
 HALVES = T // (P * RUN)
 SCORE_BANKS = 3
@@ -44,14 +43,14 @@ def tile_attend_pkv4q_rel2_cap_kernel(tc, q_words, q_scales, k_words, k_scales, 
         turn_banks = ctx.enter_context(tc.psum_pool(name="turn_banks", bufs=PAGES))
         sum_bank = ctx.enter_context(tc.psum_pool(name="sum_bank", bufs=1))
 
-        vs_runs = held.tile([P, HALVES, RUN], F32, name="vs_runs", align_bytes=64)
-        nc.sync.dma_start(vs_runs[:], vs[0].rearrange("(h p c) -> p h c", h=HALVES, c=RUN))
-        ks_pool = held.tile([P, T], U8, name="ks_pool", tag="first", align_bytes=64)
-        nc.sync.dma_start(ks_pool[KS_FIRST:P, :].bitcast(I32), k_scales.rearrange("o f t -> f o t").bitcast(I32))
         token_list = lists.tile([P, N // 16], U16, name="token_list")
         nc.sync.dma_start(token_list[:], offs)
+        vs_runs = held.tile([P, HALVES, RUN], F32, name="vs_runs", align_bytes=64)
+        nc.scalar.dma_start(vs_runs[:], vs[0].rearrange("(h p c) -> p h c", h=HALVES, c=RUN))
         value_list = lists.tile([P, PAGES * DV // 16], U16, name="value_list")
         nc.sync.dma_start(value_list[:], voffs)
+        ks_pool = held.tile([P, T], U8, name="ks_pool", tag="first", align_bytes=64)
+        nc.scalar.dma_start(ks_pool[KS_FIRST:P, :].bitcast(I32), k_scales.rearrange("o f t -> f o t").bitcast(I32))
         vsc_pool = held.tile([P, POOL_PAGES * DV], U8, name="vsc_pool", align_bytes=64)
         nc.scalar.dma_start(
             vsc_pool[VS_FIRST:P, :].bitcast(I32).rearrange("f (u w) -> f u w", u=POOL_PAGES),
@@ -68,8 +67,7 @@ def tile_attend_pkv4q_rel2_cap_kernel(tc, q_words, q_scales, k_words, k_scales, 
         nc.gpsimd.memset(q_plane[:].bitcast(I32), 0)
         qs_rows = q_scales[0].rearrange("o (g j) q -> j g o q", j=4)
         for j in range(4):
-            queue = nc.gpsimd if j < 2 else nc.sync
-            queue.dma_start(q_plane[j:P:32, :].bitcast(I32).rearrange("g (o w) -> g o w", o=PASSES), qs_rows[j].bitcast(I32))
+            nc.gpsimd.dma_start(q_plane[j:P:32, :].bitcast(I32).rearrange("g (o w) -> g o w", o=PASSES), qs_rows[j].bitcast(I32))
 
         nc.vector.memset(ks_pool[0:KS_FIRST, :].bitcast(I32), 0)
         nc.vector.memset(vsc_pool[0:96, :].bitcast(I32), 0)
@@ -91,11 +89,12 @@ def tile_attend_pkv4q_rel2_cap_kernel(tc, q_words, q_scales, k_words, k_scales, 
                     nc.tensor.transpose(spread[:, i, :], vs_runs[:, h, c : c + 1].to_broadcast([P, P]), identity[:])
                 nc.scalar.activation(vs_dealt[:, h, t], spread[:].rearrange("m i (a b) -> m a b i", a=POOL_PAGES // HALVES), ACT.Copy)
 
-        ks_listed = held.tile([P, N], U8, name="ks_listed", align_bytes=64)
-        nc.vector.tensor_copy(ks_listed[:], ks_pool[:].indirect(token_list[:]))
-        for g in range(4):
-            row = KS_FIRST + 8 * g
-            nc.sync.dma_start(k_planes[32 * g : 32 * g + 4, :].bitcast(I32), ks_listed[row : row + 8, :].bitcast(I32))
+        for h in range(2):
+            ks_listed = held.tile([P, N // 2], U8, name="ks_listed", tag="listed%d" % h, align_bytes=64)
+            nc.vector.tensor_copy(ks_listed[:], ks_pool[:].indirect(token_list[:, 2 * h * LIST_COLS : 2 * (h + 1) * LIST_COLS]))
+            for g in range(4):
+                row = KS_FIRST + 8 * g
+                nc.sync.dma_start(k_planes[32 * g : 32 * g + 4, h * N : (h + 1) * N].bitcast(I32), ks_listed[row : row + 8, :].bitcast(I32))
         vsc_listed = held.tile([P, PAGES * DV], U8, name="vsc_listed", align_bytes=64)
         nc.vector.tensor_copy(vsc_listed[:], vsc_pool[:].indirect(value_list[:]))
         vw_pool = held.tile([P, POOL_PAGES * DV], I32, name="vw_pool", tag="first", align_bytes=64)
@@ -134,12 +133,13 @@ def tile_attend_pkv4q_rel2_cap_kernel(tc, q_words, q_scales, k_words, k_scales, 
                 nc.vector.tensor_copy(k_codes[:].rearrange("g o (h i) -> g h o i", h=2), words.rearrange("g (h i o) -> g h o i", h=2, o=PASSES))
             scores[u] = score_banks.tile([P, PAGE], F32, name="score")
             for o in range(PASSES):
+                plane = (u // 2) * N + o * (N // 2) + (u % 2) * PAGE
                 nc.tensor.matmul_mx(
                     out=scores[u][:],
                     lhsT=q_codes[:, o, :].bitcast(FP8X4),
                     lhsT_scale=q_plane[:, o * NQ : (o + 1) * NQ],
                     rhs=k_codes[:, o, :].bitcast(FP4X4),
-                    rhs_scale=k_planes[:, o * N + u * PAGE : o * N + (u + 1) * PAGE],
+                    rhs_scale=k_planes[:, plane : plane + PAGE],
                     start=(o == 0),
                     stop=(o == PASSES - 1),
                 )
@@ -153,8 +153,8 @@ def tile_attend_pkv4q_rel2_cap_kernel(tc, q_words, q_scales, k_words, k_scales, 
                 scale=1.0 / CAP,
             )
 
-        def clip(u):
-            positive[u] = held.tile([P, PAGE], F32, name="positive", tag="positive%d" % u, align_bytes=64)
+        def clip(u, slot):
+            positive[u] = held.tile([P, PAGE], F32, name="positive", tag=slot, align_bytes=64)
             nc.vector.tensor_scalar(positive[u][:], capped[u][:], 0.0, None, ALU.max)
 
         def square(u):
@@ -173,15 +173,16 @@ def tile_attend_pkv4q_rel2_cap_kernel(tc, q_words, q_scales, k_words, k_scales, 
                     nc.tensor.transpose(turned[u][:, t, :], weight[:, t * P : (t + 1) * P], identity[:])
 
         def weave(u):
-            tile = pages.tile([P, NQ, PACK], BF16, name="woven", align_bytes=64)
-            woven[u] = tile[:]
+            woven[u] = all_woven[:, u]
             nc.scalar.activation(woven[u], turned[u][:].rearrange("s t q -> s q t"), ACT.Copy, scale=CAP * CAP)
 
-        def gather_values(first, slot):
-            both = held.tile([P, 2 * DV], U32, name="v_codes", tag=slot, align_bytes=64)
-            nc.vector.tensor_copy(both[:], vw_pool[:].bitcast(U32).indirect(value_list[:, first * VLIST_COLS : (first + 2) * VLIST_COLS]))
-            for u in (first, first + 1):
-                v_codes[u] = both[:, (u - first) * DV : (u - first + 1) * DV]
+        def gather_values(slot):
+            listed = held.tile([P, PAGES * DV], U32, name="v_codes", tag=slot, align_bytes=64)
+            for h in range(2):
+                offsets = value_list[:, h * DV // 8 : (h + 1) * DV // 8]
+                nc.vector.tensor_copy(listed[:, 2 * h * DV : 2 * (h + 1) * DV], vw_pool[:].bitcast(U32).indirect(offsets))
+            for u in range(PAGES):
+                v_codes[u] = listed[:, u * DV : (u + 1) * DV]
 
         acc = sum_bank.tile([P, DV], F32, name="acc")
 
@@ -210,21 +211,21 @@ def tile_attend_pkv4q_rel2_cap_kernel(tc, q_words, q_scales, k_words, k_scales, 
 
         cap(0)
         cap(1)
-        clip(0)
-        clip(1)
-        gather_values(0, "pairs0")
+        clip(0, "pairs1")
+        clip(1, "positive1")
         cap(2)
         square(0)
-        clip(2)
+        clip(2, "positive2")
         cap(3)
         scale(0)
         square(1)
-        clip(3)
+        clip(3, "positive3")
         scale(1)
         square(2)
         scale(2)
         square(3)
         scale(3, parts=2)
+        all_woven = held.tile([P, PAGES, NQ, PACK], BF16, name="all_woven", tag="positive3", align_bytes=64)
         weave(0)
         weave(1)
         total = held.tile([P, 1], F32, name="total")
@@ -232,17 +233,16 @@ def tile_attend_pkv4q_rel2_cap_kernel(tc, q_words, q_scales, k_words, k_scales, 
         nc.scalar.activation(summed[:], sums[:], ACT.Copy, scale=CAP * CAP, accum_out=total[:])
         weave(2)
         weave(3)
-        gather_values(2, "squared3")
-        early_codes = held.tile([P, 2, NQ], U32, name="early_codes", tag="first", align_bytes=64)
-        quantise(0, early_codes[:, 0])
-        quantise(1, early_codes[:, 1])
-        inverse = held.tile([P, 1], F32, name="inverse", tag="weight3", align_bytes=64)
-        nc.vector.reciprocal(inverse[:], total[:])
-        late_codes = held.tile([P, 2, NQ], U32, name="late_codes", align_bytes=64)
-        quantise(2, late_codes[:, 0])
-        quantise(3, late_codes[:, 1])
+        first_codes = held.tile([P, NQ], U32, name="first_codes", tag="codes", align_bytes=64)
+        quantise(0, first_codes[:])
+        gather_values("squared3")
+        w_codes = held.tile([P, PAGES - 1, NQ], U32, name="w_codes", tag="first", align_bytes=64)
+        for u in range(1, PAGES):
+            quantise(u, w_codes[:, u - 1])
         for u in range(PAGES):
             multiply(u, u == 0, u == PAGES - 1)
+        inverse = held.tile([P, 1], F32, name="inverse", tag="codes", align_bytes=64)
+        nc.vector.reciprocal(inverse[:], total[:])
         result = held.tile([P, DV], F32, name="result")
         nc.scalar.activation(result[:], acc[:], ACT.Copy, scale=inverse[:])
         nc.scalar.dma_start(out[0], result[:])

@@ -43,16 +43,25 @@ def tile_attend_pkv4q_rel2_cap_kernel(tc, q_words, q_scales, k_words, k_scales, 
         turn_banks = ctx.enter_context(tc.psum_pool(name="turn_banks", bufs=PAGES))
         sum_bank = ctx.enter_context(tc.psum_pool(name="sum_bank", bufs=1))
 
+        q_plane = held.tile([P, PASSES * NQ], U8, name="q_plane", align_bytes=64)
+        nc.gpsimd.memset(q_plane[:].bitcast(I32), 0)
+        qs_rows = q_scales[0].rearrange("o (g j) q -> j g o q", j=4)
+
+        def load_query_scales(queue, j):
+            queue.dma_start(q_plane[j:P:32, :].bitcast(I32).rearrange("g (o w) -> g o w", o=PASSES), qs_rows[j].bitcast(I32))
+
+        for j in (0, 1):
+            load_query_scales(nc.scalar, j)
+        vs_runs = held.tile([P, HALVES, RUN], F32, name="vs_runs", align_bytes=64)
+        nc.sync.dma_start(vs_runs[:], vs[0].rearrange("(h p c) -> p h c", h=HALVES, c=RUN))
+        ks_pool = held.tile([P, T], U8, name="ks_pool", tag="first", align_bytes=64)
+        nc.sync.dma_start(ks_pool[KS_FIRST:P, :].bitcast(I32), k_scales.rearrange("o f t -> f o t").bitcast(I32))
         token_list = lists.tile([P, N // 16], U16, name="token_list")
         nc.sync.dma_start(token_list[:], offs)
-        vs_runs = held.tile([P, HALVES, RUN], F32, name="vs_runs", align_bytes=64)
-        nc.scalar.dma_start(vs_runs[:], vs[0].rearrange("(h p c) -> p h c", h=HALVES, c=RUN))
         value_list = lists.tile([P, PAGES * DV // 16], U16, name="value_list")
         nc.sync.dma_start(value_list[:], voffs)
-        ks_pool = held.tile([P, T], U8, name="ks_pool", tag="first", align_bytes=64)
-        nc.scalar.dma_start(ks_pool[KS_FIRST:P, :].bitcast(I32), k_scales.rearrange("o f t -> f o t").bitcast(I32))
         vsc_pool = held.tile([P, POOL_PAGES * DV], U8, name="vsc_pool", align_bytes=64)
-        nc.scalar.dma_start(
+        nc.sync.dma_start(
             vsc_pool[VS_FIRST:P, :].bitcast(I32).rearrange("f (u w) -> f u w", u=POOL_PAGES),
             v_scales.rearrange("u f e -> f u e").bitcast(I32),
         )
@@ -60,14 +69,11 @@ def tile_attend_pkv4q_rel2_cap_kernel(tc, q_words, q_scales, k_words, k_scales, 
         nc.sync.dma_start(kw_pool[:], k_words[0].rearrange("g t b -> g (t b)").bitcast(I32))
         q_codes = held.tile([P, PASSES, NQ], I32, name="q_codes", align_bytes=64)
         nc.sync.dma_start(q_codes[:], q_words[0].rearrange("o g q r -> g o (q r)").bitcast(I32))
+        for j in (2, 3):
+            load_query_scales(nc.sync, j)
 
         identity = held.tile([P, P], F32, name="identity", align_bytes=64)
         make_identity(nc, identity[:])
-        q_plane = held.tile([P, PASSES * NQ], U8, name="q_plane", align_bytes=64)
-        nc.gpsimd.memset(q_plane[:].bitcast(I32), 0)
-        qs_rows = q_scales[0].rearrange("o (g j) q -> j g o q", j=4)
-        for j in range(4):
-            nc.gpsimd.dma_start(q_plane[j:P:32, :].bitcast(I32).rearrange("g (o w) -> g o w", o=PASSES), qs_rows[j].bitcast(I32))
 
         nc.vector.memset(ks_pool[0:KS_FIRST, :].bitcast(I32), 0)
         nc.vector.memset(vsc_pool[0:96, :].bitcast(I32), 0)
@@ -123,7 +129,7 @@ def tile_attend_pkv4q_rel2_cap_kernel(tc, q_words, q_scales, k_words, k_scales, 
             nc.vector.tensor_copy(k_pairs[u][:], kw_pool[:].bitcast(U32).indirect(page_offsets(u)))
 
         def score_page(u):
-            k_codes = pages.tile([P, PASSES, PAGE], U16, name="k_codes", align_bytes=64)
+            k_codes = held.tile([P, PASSES, PAGE], U16, name="k_codes", tag="parted%d" % u, align_bytes=64)
             words = k_pairs[u][:].bitcast(U16)
             if u == 0:
                 parted = words.rearrange("g (i o) -> g o i", o=PASSES)
@@ -153,13 +159,13 @@ def tile_attend_pkv4q_rel2_cap_kernel(tc, q_words, q_scales, k_words, k_scales, 
                 scale=1.0 / CAP,
             )
 
-        def clip(u, slot):
-            positive[u] = held.tile([P, PAGE], F32, name="positive", tag=slot, align_bytes=64)
-            nc.vector.tensor_scalar(positive[u][:], capped[u][:], 0.0, None, ALU.max)
+        def clip(u, into):
+            positive[u] = into
+            nc.vector.tensor_scalar(into, capped[u][:], 0.0, None, ALU.max)
 
         def square(u):
             squared[u] = held.tile([P, PAGE], F32, name="squared", tag="squared%d" % u, align_bytes=64)
-            nc.scalar.activation(squared[u][:], positive[u][:], ACT.Square, accum_out=sums[:, u : u + 1])
+            nc.scalar.activation(squared[u][:], positive[u], ACT.Square, accum_out=sums[:, u : u + 1])
 
         def scale(u, parts=1):
             weight = held.tile([P, PAGE], F32, name="weight", tag="weight%d" % u, align_bytes=64)
@@ -211,15 +217,18 @@ def tile_attend_pkv4q_rel2_cap_kernel(tc, q_words, q_scales, k_words, k_scales, 
 
         cap(0)
         cap(1)
-        clip(0, "pairs1")
-        clip(1, "positive1")
+        early = held.tile([P, 2, PAGE], F32, name="early", tag="parted2", align_bytes=64)
+        clip(0, early[:, 0])
+        clip(1, early[:, 1])
         cap(2)
         square(0)
-        clip(2, "positive2")
+        third = held.tile([P, PAGE], F32, name="third", align_bytes=64)
+        clip(2, third[:])
         cap(3)
         scale(0)
         square(1)
-        clip(3, "positive3")
+        last = held.tile([P, PAGE], F32, name="last", tag="positive3", align_bytes=64)
+        clip(3, last[:])
         scale(1)
         square(2)
         scale(2)

@@ -26,8 +26,6 @@ CAP = 2.0
 KS_FIRST = P - PASSES * BLOCKS
 VS_FIRST = P - BLOCKS
 LIST_COLS = PAGE // 16
-RUN = PACK * PACK
-HALVES = T // (P * RUN)
 SCORE_BANKS = 3
 
 FLOPS = 2 * NQ * N * D + 2 * NQ * N * DV
@@ -52,8 +50,8 @@ def tile_attend_pkv4q_rel2_cap_kernel(tc, q_words, q_scales, k_words, k_scales, 
 
         for j in (0, 1):
             load_query_scales(nc.scalar, j)
-        vs_runs = held.tile([P, HALVES, RUN], F32, name="vs_runs", align_bytes=64)
-        nc.sync.dma_start(vs_runs[:], vs[0].rearrange("(h p c) -> p h c", h=HALVES, c=RUN))
+        vs_cols = held.tile([P, POOL_PAGES, PACK], F32, name="vs_cols", align_bytes=64)
+        nc.sync.dma_start(vs_cols[:], vs[0].rearrange("(u s t) -> s u t", s=P, t=PACK))
         ks_pool = held.tile([P, T], U8, name="ks_pool", tag="first", align_bytes=64)
         nc.sync.dma_start(ks_pool[KS_FIRST:P, :].bitcast(I32), k_scales.rearrange("o f t -> f o t").bitcast(I32))
         token_list = lists.tile([P, N // 16], U16, name="token_list")
@@ -86,14 +84,16 @@ def tile_attend_pkv4q_rel2_cap_kernel(tc, q_words, q_scales, k_words, k_scales, 
         nc.vector.memset(sums[:, PAGES:], 1.0 / (CAP * CAP))
 
         vs_pool = held.tile([P, T], F32, name="vs_pool", align_bytes=64)
-        vs_dealt = vs_pool[:].rearrange("m (h a t b i) -> m h t a b i", h=HALVES, a=POOL_PAGES // HALVES, t=PACK, i=PACK)
-        for h in range(HALVES):
-            for t in range(PACK):
-                spread = turn_banks.tile([P, PACK, P], F32, name="turned")
-                for i in range(PACK):
-                    c = PACK * i + t
-                    nc.tensor.transpose(spread[:, i, :], vs_runs[:, h, c : c + 1].to_broadcast([P, P]), identity[:])
-                nc.scalar.activation(vs_dealt[:, h, t], spread[:].rearrange("m i (a b) -> m a b i", a=POOL_PAGES // HALVES), ACT.Copy)
+        vs_spread = vs_pool[:].rearrange("s (u m t) -> s u m t", u=POOL_PAGES, t=PACK)
+        for h in range(2):
+            half = slice(h * POOL_PAGES // 2, (h + 1) * POOL_PAGES // 2)
+            nc.scalar.activation(vs_spread[:, half], vs_cols[:, half].unsqueeze(2).to_broadcast([P, POOL_PAGES // 2, NQ, PACK]), ACT.Copy)
+        vs_listed = {}
+        for h in range(2):
+            pair = held.tile([P, 2 * PAGE], F32, name="vs_listed", tag="vs_listed%d" % h, align_bytes=64)
+            nc.scalar.activation(pair[:], vs_pool[:].indirect(token_list[:, 2 * h * LIST_COLS : 2 * (h + 1) * LIST_COLS]), ACT.Copy)
+            for u in range(2):
+                vs_listed[2 * h + u] = pair[:, u * PAGE : (u + 1) * PAGE]
 
         for h in range(2):
             ks_listed = held.tile([P, N // 2], U8, name="ks_listed", tag="listed%d" % h, align_bytes=64)
@@ -159,28 +159,36 @@ def tile_attend_pkv4q_rel2_cap_kernel(tc, q_words, q_scales, k_words, k_scales, 
                 scale=1.0 / CAP,
             )
 
-        def clip(u, into):
-            positive[u] = into
-            nc.vector.tensor_scalar(into, capped[u][:], 0.0, None, ALU.max)
+        def clip(u, engine):
+            positive[u] = pages.tile([P, PAGE], F32, name="positive", align_bytes=64)
+            if engine == "scalar":
+                nc.scalar.activation(positive[u][:], capped[u][:], ACT.Relu)
+            else:
+                nc.vector.tensor_scalar(positive[u][:], capped[u][:], 0.0, None, ALU.max)
 
         def square(u):
-            squared[u] = held.tile([P, PAGE], F32, name="squared", tag="squared%d" % u, align_bytes=64)
-            nc.scalar.activation(squared[u][:], positive[u], ACT.Square, accum_out=sums[:, u : u + 1])
+            squared[u] = pages.tile([P, PAGE], F32, name="squared", align_bytes=64)
+            nc.scalar.activation(squared[u][:], positive[u][:], ACT.Square, accum_out=sums[:, u : u + 1])
 
-        def scale(u, parts=1):
-            weight = held.tile([P, PAGE], F32, name="weight", tag="weight%d" % u, align_bytes=64)
+        def clip_and_square(u):
+            squared[u] = pages.tile([P, PAGE], F32, name="squared", align_bytes=64)
+            nc.vector.scalar_tensor_tensor(squared[u][:], capped[u][:], 0.0, capped[u][:], ALU.max, ALU.mult, accum_out=sums[:, u : u + 1])
+
+        def turn(u):
             turned[u] = turn_banks.tile([P, PACK, NQ], F32, name="turned")
-            width = PAGE // parts
-            for part in range(parts):
-                cols = slice(part * width, (part + 1) * width)
-                offsets = page_offsets(u)[:, part * width // 16 : (part + 1) * width // 16]
-                nc.vector.tensor_tensor(weight[:, cols], vs_pool[:].indirect(offsets), squared[u][:, cols], ALU.mult)
-                for t in range(part * width // P, (part + 1) * width // P):
-                    nc.tensor.transpose(turned[u][:, t, :], weight[:, t * P : (t + 1) * P], identity[:])
+            for t in range(PACK):
+                nc.tensor.transpose(turned[u][:, t, :], squared[u][:, t * P : (t + 1) * P], identity[:])
 
-        def weave(u):
-            woven[u] = all_woven[:, u]
-            nc.scalar.activation(woven[u], turned[u][:].rearrange("s t q -> s q t"), ACT.Copy, scale=CAP * CAP)
+        def weigh(u):
+            woven[u] = pages.tile([P, NQ, PACK], BF16, name="woven", align_bytes=64)
+            nc.vector.scalar_tensor_tensor(
+                woven[u][:],
+                turned[u][:].rearrange("s t q -> s q t"),
+                CAP * CAP,
+                vs_listed[u].rearrange("s (q t) -> s q t", t=PACK),
+                ALU.mult,
+                ALU.mult,
+            )
 
         def gather_values(slot):
             listed = held.tile([P, PAGES * DV], U32, name="v_codes", tag=slot, align_bytes=64)
@@ -192,10 +200,11 @@ def tile_attend_pkv4q_rel2_cap_kernel(tc, q_words, q_scales, k_words, k_scales, 
 
         acc = sum_bank.tile([P, DV], F32, name="acc")
 
-        def quantise(u, w_codes):
+        def quantise(u):
+            w_codes = pages.tile([P, NQ], U32, name="w_codes", align_bytes=64)
             w_plane = pages.tile([P, NQ], U8, name="w_plane", align_bytes=64)
-            nc.vector.quantize_mx(out=w_codes.bitcast(FP8X4), scales=w_plane[:], in_=woven[u].rearrange("s q t -> s (q t)"))
-            quantised[u] = (w_codes, w_plane)
+            nc.vector.quantize_mx(out=w_codes[:].bitcast(FP8X4), scales=w_plane[:], in_=woven[u][:].rearrange("s q t -> s (q t)"))
+            quantised[u] = (w_codes[:], w_plane)
 
         def multiply(u, first, last):
             w_codes, w_plane = quantised[u]
@@ -216,41 +225,35 @@ def tile_attend_pkv4q_rel2_cap_kernel(tc, q_words, q_scales, k_words, k_scales, 
                 score_page(u)
 
         cap(0)
+        clip(0, "scalar")
         cap(1)
-        early = held.tile([P, 2, PAGE], F32, name="early", tag="parted2", align_bytes=64)
-        clip(0, early[:, 0])
-        clip(1, early[:, 1])
-        cap(2)
         square(0)
-        third = held.tile([P, PAGE], F32, name="third", align_bytes=64)
-        clip(2, third[:])
+        turn(0)
+        gather_values("values")
+        cap(2)
         cap(3)
-        scale(0)
+        clip(1, "vector")
+        clip_and_square(2)
         square(1)
-        last = held.tile([P, PAGE], F32, name="last", tag="positive3", align_bytes=64)
-        clip(3, last[:])
-        scale(1)
-        square(2)
-        scale(2)
-        square(3)
-        scale(3, parts=2)
-        all_woven = held.tile([P, PAGES, NQ, PACK], BF16, name="all_woven", tag="positive3", align_bytes=64)
-        weave(0)
-        weave(1)
+        clip_and_square(3)
+        turn(2)
+        turn(1)
+        turn(3)
+        weigh(0)
+        weigh(2)
+        quantise(0)
+        weigh(1)
+        quantise(2)
+        weigh(3)
+        quantise(1)
+        quantise(3)
         total = held.tile([P, 1], F32, name="total")
         summed = held.tile([P, PAGES + 1], F32, name="summed")
         nc.scalar.activation(summed[:], sums[:], ACT.Copy, scale=CAP * CAP, accum_out=total[:])
-        weave(2)
-        weave(3)
-        first_codes = held.tile([P, NQ], U32, name="first_codes", tag="codes", align_bytes=64)
-        quantise(0, first_codes[:])
-        gather_values("squared3")
-        w_codes = held.tile([P, PAGES - 1, NQ], U32, name="w_codes", tag="first", align_bytes=64)
-        for u in range(1, PAGES):
-            quantise(u, w_codes[:, u - 1])
-        for u in range(PAGES):
-            multiply(u, u == 0, u == PAGES - 1)
-        inverse = held.tile([P, 1], F32, name="inverse", tag="codes", align_bytes=64)
+        order = (0, 2, 1, 3)
+        for u in order:
+            multiply(u, u == order[0], u == order[-1])
+        inverse = held.tile([P, 1], F32, name="inverse")
         nc.vector.reciprocal(inverse[:], total[:])
         result = held.tile([P, DV], F32, name="result")
         nc.scalar.activation(result[:], acc[:], ACT.Copy, scale=inverse[:])

@@ -25,6 +25,8 @@ BLOCKS = 16
 CAP = 2.0
 KS_FIRST = P - PASSES * BLOCKS
 VS_FIRST = P - BLOCKS
+VS_ROW = P - POOL_PAGES
+SCALAR_SPREAD = 6
 LIST_COLS = PAGE // 16
 SCORE_BANKS = 3
 
@@ -36,6 +38,7 @@ def tile_attend_pkv4q_rel2_cap_kernel(tc, q_words, q_scales, k_words, k_scales, 
     with ExitStack() as ctx:
         lists = ctx.enter_context(tc.tile_pool(name="lists", bufs=1))
         held = ctx.enter_context(tc.tile_pool(name="held", bufs=1))
+        placed = ctx.enter_context(tc.tile_pool(name="placed", bufs=1))
         pages = ctx.enter_context(tc.tile_pool(name="pages", bufs=PAGES))
         score_banks = ctx.enter_context(tc.psum_pool(name="score_banks", bufs=SCORE_BANKS))
         turn_banks = ctx.enter_context(tc.psum_pool(name="turn_banks", bufs=PAGES))
@@ -48,10 +51,8 @@ def tile_attend_pkv4q_rel2_cap_kernel(tc, q_words, q_scales, k_words, k_scales, 
         def load_query_scales(queue, j):
             queue.dma_start(q_plane[j:P:32, :].bitcast(I32).rearrange("g (o w) -> g o w", o=PASSES), qs_rows[j].bitcast(I32))
 
-        for j in (0, 1):
-            load_query_scales(nc.scalar, j)
-        vs_cols = held.tile([P, POOL_PAGES, PACK], F32, name="vs_cols", align_bytes=64)
-        nc.sync.dma_start(vs_cols[:], vs[0].rearrange("(u s t) -> s u t", s=P, t=PACK))
+        vs_pages = held.tile([P, PAGE], F32, name="vs_pages", align_bytes=64)
+        nc.scalar.dma_start(vs_pages[VS_ROW:P, :], vs[0].rearrange("(u c) -> u c", u=POOL_PAGES))
         ks_pool = held.tile([P, T], U8, name="ks_pool", tag="first", align_bytes=64)
         nc.sync.dma_start(ks_pool[KS_FIRST:P, :].bitcast(I32), k_scales.rearrange("o f t -> f o t").bitcast(I32))
         token_list = lists.tile([P, N // 16], U16, name="token_list")
@@ -67,15 +68,17 @@ def tile_attend_pkv4q_rel2_cap_kernel(tc, q_words, q_scales, k_words, k_scales, 
         nc.sync.dma_start(kw_pool[:], k_words[0].rearrange("g t b -> g (t b)").bitcast(I32))
         q_codes = held.tile([P, PASSES, NQ], I32, name="q_codes", align_bytes=64)
         nc.sync.dma_start(q_codes[:], q_words[0].rearrange("o g q r -> g o (q r)").bitcast(I32))
-        for j in (2, 3):
+        for j in (0, 1):
             load_query_scales(nc.sync, j)
 
         identity = held.tile([P, P], F32, name="identity", align_bytes=64)
         make_identity(nc, identity[:])
+        for j in (2, 3):
+            load_query_scales(nc.gpsimd, j)
 
+        nc.vector.memset(vs_pages[0:VS_ROW, :], 0.0)
         nc.vector.memset(ks_pool[0:KS_FIRST, :].bitcast(I32), 0)
-        nc.vector.memset(vsc_pool[0:96, :].bitcast(I32), 0)
-        nc.vector.memset(vsc_pool[96:VS_FIRST, :].bitcast(I32), 0)
+        nc.vector.memset(vsc_pool[0:VS_FIRST, :].bitcast(I32), 0)
         k_planes = held.tile([P, PASSES * N], U8, name="k_planes", align_bytes=64)
         nc.vector.memset(k_planes[:].bitcast(I32), 0)
         v_plane = held.tile([P, PAGES * DV], U8, name="v_plane", align_bytes=64)
@@ -83,33 +86,56 @@ def tile_attend_pkv4q_rel2_cap_kernel(tc, q_words, q_scales, k_words, k_scales, 
         sums = held.tile([P, PAGES + 1], F32, name="sums")
         nc.vector.memset(sums[:, PAGES:], 1.0 / (CAP * CAP))
 
-        vs_pool = held.tile([P, T], F32, name="vs_pool", align_bytes=64)
+        vs_turned = turn_banks.tile([P, PACK, P], F32, name="turned")
+        for t in range(PACK):
+            nc.tensor.transpose(vs_turned[:, t, :], vs_pages[:, t:PAGE:PACK], identity[:])
+        vs_pool = held.tile([P, T], F32, name="vs_pool", tag="window", align_bytes=64)
         vs_spread = vs_pool[:].rearrange("s (u m t) -> s u m t", u=POOL_PAGES, t=PACK)
-        for h in range(2):
-            half = slice(h * POOL_PAGES // 2, (h + 1) * POOL_PAGES // 2)
-            nc.scalar.activation(vs_spread[:, half], vs_cols[:, half].unsqueeze(2).to_broadcast([P, POOL_PAGES // 2, NQ, PACK]), ACT.Copy)
+        turned_cols = vs_turned[:, :, VS_ROW:P].rearrange("s t u -> s u t")
+
+        def spread_source(first, last, vs_cols):
+            nc.scalar.activation(vs_cols[:], turned_cols[:, first:last], ACT.Copy)
+            return vs_cols[:].unsqueeze(2).to_broadcast([P, last - first, NQ, PACK])
+
+        vector_cols = held.tile([P, POOL_PAGES - SCALAR_SPREAD, PACK], F32, name="vector_cols", align_bytes=64)
+        vector_source = spread_source(SCALAR_SPREAD, POOL_PAGES, vector_cols)
+        scalar_cols = placed.tile([P, SCALAR_SPREAD, PACK], F32, name="scalar_cols", offset=4 * PAGE - 64, align_bytes=64)
+        scalar_source = spread_source(0, SCALAR_SPREAD, scalar_cols)
+        nc.scalar.activation(vs_spread[:, 0:SCALAR_SPREAD], scalar_source, ACT.Copy)
+
+
+        ks_listed = {}
+
+        def gather_key_scales(h):
+            ks_listed[h] = held.tile([P, N // 2], U8, name="ks_listed", tag="listed%d" % h, align_bytes=64)
+            nc.vector.tensor_copy(ks_listed[h][:], ks_pool[:].indirect(token_list[:, 2 * h * LIST_COLS : 2 * (h + 1) * LIST_COLS]))
+
+        def move_key_scales(h):
+            for g in range(4):
+                row = KS_FIRST + 8 * g
+                nc.sync.dma_start(k_planes[32 * g : 32 * g + 4, h * N : (h + 1) * N].bitcast(I32), ks_listed[h][row : row + 8, :].bitcast(I32))
+
+        gather_key_scales(0)
+        move_key_scales(0)
+        gather_key_scales(1)
+        move_key_scales(1)
+        vw_pool = held.tile([P, POOL_PAGES * DV], I32, name="vw_pool", tag="first", align_bytes=64)
+        nc.sync.dma_start(
+            vw_pool[:].rearrange("g (u e) -> g u e", u=POOL_PAGES),
+            v_words.rearrange("u g e r -> g u (e r)").bitcast(I32),
+        )
+        vsc_listed = held.tile([P, PAGES * DV], U8, name="vsc_listed", align_bytes=64)
+        nc.vector.tensor_copy(vsc_listed[:], vsc_pool[:].indirect(value_list[:]))
+        for j in range(4):
+            nc.sync.dma_start(v_plane[j:P:32, :].bitcast(I32), vsc_listed[VS_FIRST + j : P : 4, :].bitcast(I32))
+
+        nc.vector.tensor_copy(vs_spread[:, SCALAR_SPREAD:POOL_PAGES], vector_source)
         vs_listed = {}
         for h in range(2):
             pair = held.tile([P, 2 * PAGE], F32, name="vs_listed", tag="vs_listed%d" % h, align_bytes=64)
             nc.scalar.activation(pair[:], vs_pool[:].indirect(token_list[:, 2 * h * LIST_COLS : 2 * (h + 1) * LIST_COLS]), ACT.Copy)
             for u in range(2):
                 vs_listed[2 * h + u] = pair[:, u * PAGE : (u + 1) * PAGE]
-
-        for h in range(2):
-            ks_listed = held.tile([P, N // 2], U8, name="ks_listed", tag="listed%d" % h, align_bytes=64)
-            nc.vector.tensor_copy(ks_listed[:], ks_pool[:].indirect(token_list[:, 2 * h * LIST_COLS : 2 * (h + 1) * LIST_COLS]))
-            for g in range(4):
-                row = KS_FIRST + 8 * g
-                nc.sync.dma_start(k_planes[32 * g : 32 * g + 4, h * N : (h + 1) * N].bitcast(I32), ks_listed[row : row + 8, :].bitcast(I32))
-        vsc_listed = held.tile([P, PAGES * DV], U8, name="vsc_listed", align_bytes=64)
-        nc.vector.tensor_copy(vsc_listed[:], vsc_pool[:].indirect(value_list[:]))
-        vw_pool = held.tile([P, POOL_PAGES * DV], I32, name="vw_pool", tag="first", align_bytes=64)
-        nc.sync.dma_start(
-            vw_pool[:].rearrange("g (u e) -> g u e", u=POOL_PAGES),
-            v_words.rearrange("u g e r -> g u (e r)").bitcast(I32),
-        )
-        for j in range(4):
-            nc.sync.dma_start(v_plane[j:P:32, :].bitcast(I32), vsc_listed[VS_FIRST + j : P : 4, :].bitcast(I32))
 
         k_pairs = {}
         scores = {}
@@ -125,7 +151,7 @@ def tile_attend_pkv4q_rel2_cap_kernel(tc, q_words, q_scales, k_words, k_scales, 
             return token_list[:, u * LIST_COLS : (u + 1) * LIST_COLS]
 
         def gather_keys(u):
-            k_pairs[u] = held.tile([P, PAGE], U32, name="k_pairs", tag="pairs%d" % (u % 2), align_bytes=64)
+            k_pairs[u] = placed.tile([P, PAGE], U32, name="k_pairs%d" % u, offset=(u % 2) * 4 * PAGE, align_bytes=64)
             nc.vector.tensor_copy(k_pairs[u][:], kw_pool[:].bitcast(U32).indirect(page_offsets(u)))
 
         def score_page(u):
@@ -150,39 +176,42 @@ def tile_attend_pkv4q_rel2_cap_kernel(tc, q_words, q_scales, k_words, k_scales, 
                     stop=(o == PASSES - 1),
                 )
 
-        def cap(u):
-            capped[u] = pages.tile([P, PAGE], F32, name="capped", align_bytes=64)
+        def cap(u, into):
+            capped[u] = into
             nc.scalar.activation(
-                capped[u][:].rearrange("q (t s) -> q t s", t=PACK),
+                into.rearrange("q (t s) -> q t s", t=PACK),
                 scores[u][:].rearrange("q (s t) -> q t s", t=PACK),
                 ACT.Tanh,
                 scale=1.0 / CAP,
             )
 
-        def clip(u, engine):
-            positive[u] = pages.tile([P, PAGE], F32, name="positive", align_bytes=64)
-            if engine == "scalar":
-                nc.scalar.activation(positive[u][:], capped[u][:], ACT.Relu)
-            else:
-                nc.vector.tensor_scalar(positive[u][:], capped[u][:], 0.0, None, ALU.max)
+        def clip_on_scalar(u):
+            clipped = held.tile([P, PAGE], F32, name="clipped", tag="clipped%d" % u, align_bytes=64)
+            positive[u] = clipped[:]
+            nc.scalar.activation(positive[u], capped[u], ACT.Relu)
+
+        def clip_on_vector(u, into):
+            positive[u] = into
+            nc.vector.tensor_scalar(into, capped[u], 0.0, None, ALU.max)
 
         def square(u):
-            squared[u] = pages.tile([P, PAGE], F32, name="squared", align_bytes=64)
-            nc.scalar.activation(squared[u][:], positive[u][:], ACT.Square, accum_out=sums[:, u : u + 1])
+            square_tile = held.tile([P, PAGE], F32, name="square_tile", tag="squared%d" % u, align_bytes=64)
+            squared[u] = square_tile[:]
+            nc.scalar.activation(squared[u], positive[u], ACT.Square, accum_out=sums[:, u : u + 1])
 
-        def clip_and_square(u):
-            squared[u] = pages.tile([P, PAGE], F32, name="squared", align_bytes=64)
-            nc.vector.scalar_tensor_tensor(squared[u][:], capped[u][:], 0.0, capped[u][:], ALU.max, ALU.mult, accum_out=sums[:, u : u + 1])
+        def clip_and_square(u, into):
+            squared[u] = into
+            nc.vector.scalar_tensor_tensor(into, capped[u], 0.0, capped[u], ALU.max, ALU.mult, accum_out=sums[:, u : u + 1])
 
         def turn(u):
             turned[u] = turn_banks.tile([P, PACK, NQ], F32, name="turned")
             for t in range(PACK):
                 nc.tensor.transpose(turned[u][:, t, :], squared[u][:, t * P : (t + 1) * P], identity[:])
 
-        def weigh(u):
-            woven[u] = pages.tile([P, NQ, PACK], BF16, name="woven", align_bytes=64)
+        def weigh(u, into):
+            woven[u] = into
             nc.vector.scalar_tensor_tensor(
-                woven[u][:],
+                into.rearrange("s (q t) -> s q t", t=PACK),
                 turned[u][:].rearrange("s t q -> s q t"),
                 CAP * CAP,
                 vs_listed[u].rearrange("s (q t) -> s q t", t=PACK),
@@ -203,7 +232,7 @@ def tile_attend_pkv4q_rel2_cap_kernel(tc, q_words, q_scales, k_words, k_scales, 
         def quantise(u):
             w_codes = pages.tile([P, NQ], U32, name="w_codes", align_bytes=64)
             w_plane = pages.tile([P, NQ], U8, name="w_plane", align_bytes=64)
-            nc.vector.quantize_mx(out=w_codes[:].bitcast(FP8X4), scales=w_plane[:], in_=woven[u][:].rearrange("s q t -> s (q t)"))
+            nc.vector.quantize_mx(out=w_codes[:].bitcast(FP8X4), scales=w_plane[:], in_=woven[u])
             quantised[u] = (w_codes[:], w_plane)
 
         def multiply(u, first, last):
@@ -224,27 +253,30 @@ def tile_attend_pkv4q_rel2_cap_kernel(tc, q_words, q_scales, k_words, k_scales, 
             for u in (first, first + 1):
                 score_page(u)
 
-        cap(0)
-        clip(0, "scalar")
-        cap(1)
+        capped_all = held.tile([P, PAGES * PAGE], F32, name="capped_all", tag="window", align_bytes=64)
+        cap(0, capped_all[:, 0 * PAGE : 1 * PAGE])
+        clip_on_scalar(0)
+        cap(1, capped_all[:, 1 * PAGE : 2 * PAGE])
         square(0)
         turn(0)
         gather_values("values")
-        cap(2)
-        cap(3)
-        clip(1, "vector")
-        clip_and_square(2)
+        late = held.tile([P, 3 * PAGE + PAGE // 2], F32, name="late", tag="first", align_bytes=64)
+        rest = held.tile([P, 3 * PAGE], BF16, name="rest", align_bytes=64)
+        cap(2, capped_all[:, 2 * PAGE : 3 * PAGE])
+        cap(3, capped_all[:, 3 * PAGE : 4 * PAGE])
+        clip_on_vector(1, late[:, 0:PAGE])
+        clip_and_square(2, late[:, PAGE : 2 * PAGE])
         square(1)
-        clip_and_square(3)
+        clip_and_square(3, late[:, 2 * PAGE : 3 * PAGE])
         turn(2)
         turn(1)
         turn(3)
-        weigh(0)
-        weigh(2)
+        weigh(0, late[:, 3 * PAGE :].bitcast(BF16))
+        weigh(2, rest[:, 0:PAGE])
         quantise(0)
-        weigh(1)
+        weigh(1, rest[:, PAGE : 2 * PAGE])
         quantise(2)
-        weigh(3)
+        weigh(3, rest[:, 2 * PAGE :])
         quantise(1)
         quantise(3)
         total = held.tile([P, 1], F32, name="total")

@@ -26,7 +26,10 @@ CAP = 2.0
 KS_FIRST = P - PASSES * BLOCKS
 VS_FIRST = P - BLOCKS
 VS_ROW = P - POOL_PAGES
-SCALAR_SPREAD = 6
+FIRST_SPREAD = 4
+PAGE_BYTES = 4 * PAGE
+PAIRS_AT = 5 * PAGE_BYTES
+CAPPED_AT = 7 * PAGE_BYTES
 LIST_COLS = PAGE // 16
 SCORE_BANKS = 3
 
@@ -53,7 +56,7 @@ def tile_attend_pkv4q_rel2_cap_kernel(tc, q_words, q_scales, k_words, k_scales, 
 
         vs_pages = held.tile([P, PAGE], F32, name="vs_pages", align_bytes=64)
         nc.scalar.dma_start(vs_pages[VS_ROW:P, :], vs[0].rearrange("(u c) -> u c", u=POOL_PAGES))
-        ks_pool = held.tile([P, T], U8, name="ks_pool", tag="first", align_bytes=64)
+        ks_pool = placed.tile([P, T], U8, name="ks_pool", offset=0, align_bytes=64)
         nc.sync.dma_start(ks_pool[KS_FIRST:P, :].bitcast(I32), k_scales.rearrange("o f t -> f o t").bitcast(I32))
         token_list = lists.tile([P, N // 16], U16, name="token_list")
         nc.sync.dma_start(token_list[:], offs)
@@ -89,7 +92,7 @@ def tile_attend_pkv4q_rel2_cap_kernel(tc, q_words, q_scales, k_words, k_scales, 
         vs_turned = turn_banks.tile([P, PACK, P], F32, name="turned")
         for t in range(PACK):
             nc.tensor.transpose(vs_turned[:, t, :], vs_pages[:, t:PAGE:PACK], identity[:])
-        vs_pool = held.tile([P, T], F32, name="vs_pool", tag="window", align_bytes=64)
+        vs_pool = held.tile([P, T], F32, name="vs_pool", align_bytes=64)
         vs_spread = vs_pool[:].rearrange("s (u m t) -> s u m t", u=POOL_PAGES, t=PACK)
         turned_cols = vs_turned[:, :, VS_ROW:P].rearrange("s t u -> s u t")
 
@@ -97,11 +100,20 @@ def tile_attend_pkv4q_rel2_cap_kernel(tc, q_words, q_scales, k_words, k_scales, 
             nc.scalar.activation(vs_cols[:], turned_cols[:, first:last], ACT.Copy)
             return vs_cols[:].unsqueeze(2).to_broadcast([P, last - first, NQ, PACK])
 
-        vector_cols = held.tile([P, POOL_PAGES - SCALAR_SPREAD, PACK], F32, name="vector_cols", align_bytes=64)
-        vector_source = spread_source(SCALAR_SPREAD, POOL_PAGES, vector_cols)
-        scalar_cols = placed.tile([P, SCALAR_SPREAD, PACK], F32, name="scalar_cols", offset=4 * PAGE - 64, align_bytes=64)
-        scalar_source = spread_source(0, SCALAR_SPREAD, scalar_cols)
-        nc.scalar.activation(vs_spread[:, 0:SCALAR_SPREAD], scalar_source, ACT.Copy)
+        first_cols = placed.tile([P, FIRST_SPREAD, PACK], F32, name="first_cols", offset=PAIRS_AT + PAGE_BYTES - 32, align_bytes=32)
+        first_source = spread_source(0, FIRST_SPREAD, first_cols)
+        other_cols = placed.tile([P, POOL_PAGES - FIRST_SPREAD, PACK], F32, name="other_cols", offset=CAPPED_AT, align_bytes=64)
+        other_source = spread_source(FIRST_SPREAD, POOL_PAGES, other_cols)
+        nc.scalar.activation(vs_spread[:, 0:FIRST_SPREAD], first_source, ACT.Copy)
+        nc.scalar.activation(vs_spread[:, FIRST_SPREAD:POOL_PAGES], other_source, ACT.Copy)
+        vs_listed = {}
+
+        def gather_vs(u, listed):
+            vs_listed[u] = listed[:]
+            nc.scalar.activation(listed[:], vs_pool[:].indirect(token_list[:, u * LIST_COLS : (u + 1) * LIST_COLS]), ACT.Copy)
+
+        for u in (0, 2):
+            gather_vs(u, held.tile([P, PAGE], F32, name="vs_listed%d" % u, align_bytes=64))
 
 
         ks_listed = {}
@@ -119,7 +131,7 @@ def tile_attend_pkv4q_rel2_cap_kernel(tc, q_words, q_scales, k_words, k_scales, 
         move_key_scales(0)
         gather_key_scales(1)
         move_key_scales(1)
-        vw_pool = held.tile([P, POOL_PAGES * DV], I32, name="vw_pool", tag="first", align_bytes=64)
+        vw_pool = placed.tile([P, POOL_PAGES * DV], I32, name="vw_pool", offset=0, align_bytes=64)
         nc.sync.dma_start(
             vw_pool[:].rearrange("g (u e) -> g u e", u=POOL_PAGES),
             v_words.rearrange("u g e r -> g u (e r)").bitcast(I32),
@@ -128,14 +140,6 @@ def tile_attend_pkv4q_rel2_cap_kernel(tc, q_words, q_scales, k_words, k_scales, 
         nc.vector.tensor_copy(vsc_listed[:], vsc_pool[:].indirect(value_list[:]))
         for j in range(4):
             nc.sync.dma_start(v_plane[j:P:32, :].bitcast(I32), vsc_listed[VS_FIRST + j : P : 4, :].bitcast(I32))
-
-        nc.vector.tensor_copy(vs_spread[:, SCALAR_SPREAD:POOL_PAGES], vector_source)
-        vs_listed = {}
-        for h in range(2):
-            pair = held.tile([P, 2 * PAGE], F32, name="vs_listed", tag="vs_listed%d" % h, align_bytes=64)
-            nc.scalar.activation(pair[:], vs_pool[:].indirect(token_list[:, 2 * h * LIST_COLS : 2 * (h + 1) * LIST_COLS]), ACT.Copy)
-            for u in range(2):
-                vs_listed[2 * h + u] = pair[:, u * PAGE : (u + 1) * PAGE]
 
         k_pairs = {}
         scores = {}
@@ -151,7 +155,7 @@ def tile_attend_pkv4q_rel2_cap_kernel(tc, q_words, q_scales, k_words, k_scales, 
             return token_list[:, u * LIST_COLS : (u + 1) * LIST_COLS]
 
         def gather_keys(u):
-            k_pairs[u] = placed.tile([P, PAGE], U32, name="k_pairs%d" % u, offset=(u % 2) * 4 * PAGE, align_bytes=64)
+            k_pairs[u] = placed.tile([P, PAGE], U32, name="k_pairs%d" % u, offset=PAIRS_AT + (u % 2) * PAGE_BYTES, align_bytes=64)
             nc.vector.tensor_copy(k_pairs[u][:], kw_pool[:].bitcast(U32).indirect(page_offsets(u)))
 
         def score_page(u):
@@ -253,25 +257,32 @@ def tile_attend_pkv4q_rel2_cap_kernel(tc, q_words, q_scales, k_words, k_scales, 
             for u in (first, first + 1):
                 score_page(u)
 
-        capped_all = held.tile([P, PAGES * PAGE], F32, name="capped_all", tag="window", align_bytes=64)
-        cap(0, capped_all[:, 0 * PAGE : 1 * PAGE])
+        capped_all = placed.tile([P, PAGES * PAGE], F32, name="capped_all", offset=CAPPED_AT, align_bytes=64)
+        cap(0, capped_all[:, 0:PAGE])
         clip_on_scalar(0)
-        cap(1, capped_all[:, 1 * PAGE : 2 * PAGE])
+        cap(1, capped_all[:, PAGE : 2 * PAGE])
         square(0)
         turn(0)
         gather_values("values")
-        late = held.tile([P, 3 * PAGE + PAGE // 2], F32, name="late", tag="first", align_bytes=64)
+        squared2 = placed.tile([P, PAGE], F32, name="squared2", offset=0, align_bytes=64)
+        squared3 = placed.tile([P, PAGE], F32, name="squared3", offset=PAGE_BYTES, align_bytes=64)
+        woven0 = placed.tile([P, PAGE], BF16, name="woven0", offset=2 * PAGE_BYTES, align_bytes=64)
+        positive1 = placed.tile([P, PAGE], F32, name="positive1", offset=7 * PAGE_BYTES // 2, align_bytes=64)
         rest = held.tile([P, 3 * PAGE], BF16, name="rest", align_bytes=64)
         cap(2, capped_all[:, 2 * PAGE : 3 * PAGE])
-        cap(3, capped_all[:, 3 * PAGE : 4 * PAGE])
-        clip_on_vector(1, late[:, 0:PAGE])
-        clip_and_square(2, late[:, PAGE : 2 * PAGE])
+        cap(3, capped_all[:, 3 * PAGE :])
+        clip_on_vector(1, positive1[:])
+        clip_and_square(2, squared2[:])
         square(1)
-        clip_and_square(3, late[:, 2 * PAGE : 3 * PAGE])
+        clip_and_square(3, squared3[:])
+        listed1 = placed.tile([P, PAGE], F32, name="listed1", offset=4 * PAGE_BYTES, align_bytes=64)
+        listed3 = placed.tile([P, PAGE], F32, name="listed3", offset=11 * PAGE_BYTES // 4, align_bytes=64)
+        gather_vs(1, listed1)
+        gather_vs(3, listed3)
         turn(2)
         turn(1)
         turn(3)
-        weigh(0, late[:, 3 * PAGE :].bitcast(BF16))
+        weigh(0, woven0[:])
         weigh(2, rest[:, 0:PAGE])
         quantise(0)
         weigh(1, rest[:, PAGE : 2 * PAGE])

@@ -180,19 +180,18 @@ def tile_attend_pkv4q_rel2_cap_kernel(tc, q_words, q_scales, k_words, k_scales, 
                     stop=(o == PASSES - 1),
                 )
 
-        def cap(u, into):
+        def cap(u, into, places=slice(0, PACK)):
             capped[u] = into
             nc.scalar.activation(
-                into.rearrange("q (t s) -> q t s", t=PACK),
-                scores[u][:].rearrange("q (s t) -> q t s", t=PACK),
+                into.rearrange("q (t s) -> q t s", t=PACK)[:, places],
+                scores[u][:].rearrange("q (s t) -> q t s", t=PACK)[:, places],
                 ACT.Tanh,
                 scale=1.0 / CAP,
             )
 
-        def clip_on_scalar(u):
-            clipped = held.tile([P, PAGE], F32, name="clipped", tag="clipped%d" % u, align_bytes=64)
-            positive[u] = clipped[:]
-            nc.scalar.activation(positive[u], capped[u], ACT.Relu)
+        def clip_on_scalar(u, into, cols):
+            positive[u] = into
+            nc.scalar.activation(into[:, cols], capped[u][:, cols], ACT.Relu)
 
         def clip_on_vector(u, into):
             positive[u] = into
@@ -258,8 +257,11 @@ def tile_attend_pkv4q_rel2_cap_kernel(tc, q_words, q_scales, k_words, k_scales, 
                 score_page(u)
 
         capped_all = placed.tile([P, PAGES * PAGE], F32, name="capped_all", offset=CAPPED_AT, align_bytes=64)
-        cap(0, capped_all[:, 0:PAGE])
-        clip_on_scalar(0)
+        positive0 = held.tile([P, PAGE], F32, name="positive0", align_bytes=64)
+        for h in range(2):
+            cap(0, capped_all[:, 0:PAGE], slice(2 * h, 2 * h + 2))
+        for h in range(2):
+            clip_on_scalar(0, positive0[:], slice(h * PAGE // 2, (h + 1) * PAGE // 2))
         cap(1, capped_all[:, PAGE : 2 * PAGE])
         square(0)
         turn(0)

@@ -26,6 +26,7 @@ CAP = 2.0
 KS_FIRST = P - PASSES * BLOCKS
 VS_FIRST = P - BLOCKS
 VS_ROW = P - POOL_PAGES
+SCALE_RUNS = ((0, 1), (1, PAGES))
 FIRST_SPREAD = 4
 PAGE_BYTES = 4 * PAGE
 PAIRS_AT = 5 * PAGE_BYTES
@@ -49,10 +50,10 @@ def tile_attend_pkv4q_rel2_cap_kernel(tc, q_words, q_scales, k_words, k_scales, 
 
         q_plane = held.tile([P, PASSES * NQ], U8, name="q_plane", align_bytes=64)
         nc.gpsimd.memset(q_plane[:].bitcast(I32), 0)
-        qs_rows = q_scales[0].rearrange("o (g j) q -> j g o q", j=4)
+        qs_rows = q_scales[0].rearrange("o (g j) q -> g j o q", j=4)
 
-        def load_query_scales(queue, j):
-            queue.dma_start(q_plane[j:P:32, :].bitcast(I32).rearrange("g (o w) -> g o w", o=PASSES), qs_rows[j].bitcast(I32))
+        def load_query_scales(queue, g):
+            queue.dma_start(q_plane[32 * g : 32 * g + 4, :].bitcast(I32).rearrange("j (o w) -> j o w", o=PASSES), qs_rows[g].bitcast(I32))
 
         vs_pages = held.tile([P, PAGE], F32, name="vs_pages", align_bytes=64)
         nc.scalar.dma_start(vs_pages[VS_ROW:P, :], vs[0].rearrange("(u c) -> u c", u=POOL_PAGES))
@@ -67,27 +68,27 @@ def tile_attend_pkv4q_rel2_cap_kernel(tc, q_words, q_scales, k_words, k_scales, 
             vsc_pool[VS_FIRST:P, :].bitcast(I32).rearrange("f (u w) -> f u w", u=POOL_PAGES),
             v_scales.rearrange("u f e -> f u e").bitcast(I32),
         )
-        kw_pool = held.tile([P, T], I32, name="kw_pool", align_bytes=64)
-        nc.sync.dma_start(kw_pool[:], k_words[0].rearrange("g t b -> g (t b)").bitcast(I32))
         q_codes = held.tile([P, PASSES, NQ], I32, name="q_codes", align_bytes=64)
         nc.sync.dma_start(q_codes[:], q_words[0].rearrange("o g q r -> g o (q r)").bitcast(I32))
-        for j in (0, 1):
-            load_query_scales(nc.sync, j)
+        load_query_scales(nc.sync, 0)
+        kw_pool = held.tile([P, T], I32, name="kw_pool", align_bytes=64)
+        nc.sync.dma_start(kw_pool[:], k_words[0].rearrange("g t b -> g (t b)").bitcast(I32))
+        load_query_scales(nc.sync, 2)
 
         identity = held.tile([P, P], F32, name="identity", align_bytes=64)
         make_identity(nc, identity[:])
-        for j in (2, 3):
-            load_query_scales(nc.gpsimd, j)
+        for g in (1, 3):
+            load_query_scales(nc.gpsimd, g)
 
         nc.vector.memset(vs_pages[0:VS_ROW, :], 0.0)
         nc.vector.memset(ks_pool[0:KS_FIRST, :].bitcast(I32), 0)
         nc.vector.memset(vsc_pool[0:VS_FIRST, :].bitcast(I32), 0)
         k_planes = held.tile([P, PASSES * N], U8, name="k_planes", align_bytes=64)
         nc.vector.memset(k_planes[:].bitcast(I32), 0)
-        v_plane = held.tile([P, PAGES * DV], U8, name="v_plane", align_bytes=64)
-        nc.vector.memset(v_plane[:].bitcast(I32), 0)
         sums = held.tile([P, PAGES + 1], F32, name="sums")
         nc.vector.memset(sums[:, PAGES:], 1.0 / (CAP * CAP))
+        v_plane = held.tile([P, PAGES * DV], U8, name="v_plane", align_bytes=64)
+        nc.vector.memset(v_plane[:].bitcast(I32), 0)
 
         vs_turned = turn_banks.tile([P, PACK, P], F32, name="turned")
         for t in range(PACK):
@@ -116,21 +117,18 @@ def tile_attend_pkv4q_rel2_cap_kernel(tc, q_words, q_scales, k_words, k_scales, 
             gather_vs(u, held.tile([P, PAGE], F32, name="vs_listed%d" % u, align_bytes=64))
 
 
-        ks_listed = {}
-
-        def gather_key_scales(h):
-            ks_listed[h] = held.tile([P, N // 2], U8, name="ks_listed", tag="listed%d" % h, align_bytes=64)
-            nc.vector.tensor_copy(ks_listed[h][:], ks_pool[:].indirect(token_list[:, 2 * h * LIST_COLS : 2 * (h + 1) * LIST_COLS]))
-
-        def move_key_scales(h):
-            for g in range(4):
+        plane_at = {}
+        for first, last in SCALE_RUNS:
+            width = (last - first) * PAGE
+            ks_listed = held.tile([P, width], U8, name="ks_listed%d" % first, align_bytes=64)
+            nc.vector.tensor_copy(ks_listed[:], ks_pool[:].indirect(token_list[:, first * LIST_COLS : last * LIST_COLS]))
+            start = PASSES * first * PAGE
+            for g in (0, 2, 1, 3):
                 row = KS_FIRST + 8 * g
-                nc.sync.dma_start(k_planes[32 * g : 32 * g + 4, h * N : (h + 1) * N].bitcast(I32), ks_listed[h][row : row + 8, :].bitcast(I32))
-
-        gather_key_scales(0)
-        move_key_scales(0)
-        gather_key_scales(1)
-        move_key_scales(1)
+                nc.sync.dma_start(k_planes[32 * g : 32 * g + 4, start : start + PASSES * width].bitcast(I32), ks_listed[row : row + 8, :].bitcast(I32))
+            for u in range(first, last):
+                for o in range(PASSES):
+                    plane_at[u, o] = start + o * width + (u - first) * PAGE
         vw_pool = placed.tile([P, POOL_PAGES * DV], I32, name="vw_pool", offset=0, align_bytes=64)
         nc.sync.dma_start(
             vw_pool[:].rearrange("g (u e) -> g u e", u=POOL_PAGES),
@@ -169,7 +167,7 @@ def tile_attend_pkv4q_rel2_cap_kernel(tc, q_words, q_scales, k_words, k_scales, 
                 nc.vector.tensor_copy(k_codes[:].rearrange("g o (h i) -> g h o i", h=2), words.rearrange("g (h i o) -> g h o i", h=2, o=PASSES))
             scores[u] = score_banks.tile([P, PAGE], F32, name="score")
             for o in range(PASSES):
-                plane = (u // 2) * N + o * (N // 2) + (u % 2) * PAGE
+                plane = plane_at[u, o]
                 nc.tensor.matmul_mx(
                     out=scores[u][:],
                     lhsT=q_codes[:, o, :].bitcast(FP8X4),

@@ -26,7 +26,6 @@ CAP = 2.0
 KS_FIRST = P - PASSES * BLOCKS
 VS_FIRST = P - BLOCKS
 VS_ROW = P - POOL_PAGES
-SCALE_RUNS = ((0, 1), (1, PAGES))
 FIRST_SPREAD = 4
 PAGE_BYTES = 4 * PAGE
 PAIRS_AT = 5 * PAGE_BYTES
@@ -58,7 +57,7 @@ def tile_attend_pkv4q_rel2_cap_kernel(tc, q_words, q_scales, k_words, k_scales, 
         vs_pages = held.tile([P, PAGE], F32, name="vs_pages", align_bytes=64)
         nc.scalar.dma_start(vs_pages[VS_ROW:P, :], vs[0].rearrange("(u c) -> u c", u=POOL_PAGES))
         ks_pool = placed.tile([P, T], U8, name="ks_pool", offset=0, align_bytes=64)
-        nc.sync.dma_start(ks_pool[KS_FIRST:P, :].bitcast(I32), k_scales.rearrange("o f t -> f o t").bitcast(I32))
+        nc.sync.dma_start(ks_pool[KS_FIRST:P, :].bitcast(I32), k_scales.rearrange("o f t -> (o f) t").bitcast(I32))
         token_list = lists.tile([P, N // 16], U16, name="token_list")
         nc.sync.dma_start(token_list[:], offs)
         value_list = lists.tile([P, PAGES * DV // 16], U16, name="value_list")
@@ -73,11 +72,10 @@ def tile_attend_pkv4q_rel2_cap_kernel(tc, q_words, q_scales, k_words, k_scales, 
         load_query_scales(nc.sync, 0)
         kw_pool = held.tile([P, T], I32, name="kw_pool", align_bytes=64)
         nc.sync.dma_start(kw_pool[:], k_words[0].rearrange("g t b -> g (t b)").bitcast(I32))
-        load_query_scales(nc.sync, 2)
 
         identity = held.tile([P, P], F32, name="identity", align_bytes=64)
         make_identity(nc, identity[:])
-        for g in (1, 3):
+        for g in (1, 2, 3):
             load_query_scales(nc.gpsimd, g)
 
         nc.vector.memset(vs_pages[0:VS_ROW, :], 0.0)
@@ -117,18 +115,12 @@ def tile_attend_pkv4q_rel2_cap_kernel(tc, q_words, q_scales, k_words, k_scales, 
             gather_vs(u, held.tile([P, PAGE], F32, name="vs_listed%d" % u, align_bytes=64))
 
 
-        plane_at = {}
-        for first, last in SCALE_RUNS:
-            width = (last - first) * PAGE
-            ks_listed = held.tile([P, width], U8, name="ks_listed%d" % first, align_bytes=64)
-            nc.vector.tensor_copy(ks_listed[:], ks_pool[:].indirect(token_list[:, first * LIST_COLS : last * LIST_COLS]))
-            start = PASSES * first * PAGE
-            for g in (0, 2, 1, 3):
-                row = KS_FIRST + 8 * g
-                nc.sync.dma_start(k_planes[32 * g : 32 * g + 4, start : start + PASSES * width].bitcast(I32), ks_listed[row : row + 8, :].bitcast(I32))
-            for u in range(first, last):
-                for o in range(PASSES):
-                    plane_at[u, o] = start + o * width + (u - first) * PAGE
+        ks_listed = held.tile([P, N], U8, name="ks_listed", align_bytes=64)
+        nc.vector.tensor_copy(ks_listed[:], ks_pool[:].indirect(token_list[:]))
+        for o in range(PASSES):
+            first = KS_FIRST + o * BLOCKS
+            for j in range(4):
+                nc.sync.dma_start(k_planes[j:P:32, o * N : (o + 1) * N].bitcast(I32), ks_listed[first + j : first + BLOCKS : 4, :].bitcast(I32))
         vw_pool = placed.tile([P, POOL_PAGES * DV], I32, name="vw_pool", offset=0, align_bytes=64)
         nc.sync.dma_start(
             vw_pool[:].rearrange("g (u e) -> g u e", u=POOL_PAGES),
@@ -167,7 +159,7 @@ def tile_attend_pkv4q_rel2_cap_kernel(tc, q_words, q_scales, k_words, k_scales, 
                 nc.vector.tensor_copy(k_codes[:].rearrange("g o (h i) -> g h o i", h=2), words.rearrange("g (h i o) -> g h o i", h=2, o=PASSES))
             scores[u] = score_banks.tile([P, PAGE], F32, name="score")
             for o in range(PASSES):
-                plane = plane_at[u, o]
+                plane = o * N + u * PAGE
                 nc.tensor.matmul_mx(
                     out=scores[u][:],
                     lhsT=q_codes[:, o, :].bitcast(FP8X4),

@@ -25,7 +25,8 @@ BLOCKS = 16
 CAP = 2.0
 KS_FIRST = P - PASSES * BLOCKS
 VS_FIRST = P - BLOCKS
-VS_ROW = P - POOL_PAGES
+VS_END = 64
+VS_ROW = VS_END - POOL_PAGES
 FIRST_SPREAD = 4
 PAGE_BYTES = 4 * PAGE
 PAIRS_AT = 5 * PAGE_BYTES
@@ -55,9 +56,9 @@ def tile_attend_pkv4q_rel2_cap_kernel(tc, q_words, q_scales, k_words, k_scales, 
             queue.dma_start(q_plane[32 * g : 32 * g + 4, :].bitcast(I32).rearrange("j (o w) -> j o w", o=PASSES), qs_rows[g].bitcast(I32))
 
         vs_pages = held.tile([P, PAGE], F32, name="vs_pages", align_bytes=64)
-        nc.scalar.dma_start(vs_pages[VS_ROW:P, :], vs[0].rearrange("(u c) -> u c", u=POOL_PAGES))
+        nc.scalar.dma_start(vs_pages[VS_ROW:VS_END, :], vs[0].rearrange("(u c) -> u c", u=POOL_PAGES))
         ks_pool = placed.tile([P, T], U8, name="ks_pool", offset=0, align_bytes=64)
-        nc.sync.dma_start(ks_pool[KS_FIRST:P, :].bitcast(I32), k_scales.rearrange("o f t -> (o f) t").bitcast(I32))
+        nc.sync.dma_start(ks_pool[KS_FIRST:P, :].bitcast(I32), k_scales.rearrange("o f t -> f o t").bitcast(I32))
         token_list = lists.tile([P, N // 16], U16, name="token_list")
         nc.sync.dma_start(token_list[:], offs)
         value_list = lists.tile([P, PAGES * DV // 16], U16, name="value_list")
@@ -67,11 +68,11 @@ def tile_attend_pkv4q_rel2_cap_kernel(tc, q_words, q_scales, k_words, k_scales, 
             vsc_pool[VS_FIRST:P, :].bitcast(I32).rearrange("f (u w) -> f u w", u=POOL_PAGES),
             v_scales.rearrange("u f e -> f u e").bitcast(I32),
         )
+        kw_pool = held.tile([P, T], I32, name="kw_pool", align_bytes=64)
+        nc.sync.dma_start(kw_pool[:], k_words[0].rearrange("g t b -> g (t b)").bitcast(I32))
         q_codes = held.tile([P, PASSES, NQ], I32, name="q_codes", align_bytes=64)
         nc.sync.dma_start(q_codes[:], q_words[0].rearrange("o g q r -> g o (q r)").bitcast(I32))
         load_query_scales(nc.sync, 0)
-        kw_pool = held.tile([P, T], I32, name="kw_pool", align_bytes=64)
-        nc.sync.dma_start(kw_pool[:], k_words[0].rearrange("g t b -> g (t b)").bitcast(I32))
 
         identity = held.tile([P, P], F32, name="identity", align_bytes=64)
         make_identity(nc, identity[:])
@@ -79,6 +80,7 @@ def tile_attend_pkv4q_rel2_cap_kernel(tc, q_words, q_scales, k_words, k_scales, 
             load_query_scales(nc.gpsimd, g)
 
         nc.vector.memset(vs_pages[0:VS_ROW, :], 0.0)
+        nc.vector.memset(vs_pages[VS_END:P, :], 0.0)
         nc.vector.memset(ks_pool[0:KS_FIRST, :].bitcast(I32), 0)
         nc.vector.memset(vsc_pool[0:VS_FIRST, :].bitcast(I32), 0)
         k_planes = held.tile([P, PASSES * N], U8, name="k_planes", align_bytes=64)
@@ -93,7 +95,7 @@ def tile_attend_pkv4q_rel2_cap_kernel(tc, q_words, q_scales, k_words, k_scales, 
             nc.tensor.transpose(vs_turned[:, t, :], vs_pages[:, t:PAGE:PACK], identity[:])
         vs_pool = held.tile([P, T], F32, name="vs_pool", align_bytes=64)
         vs_spread = vs_pool[:].rearrange("s (u m t) -> s u m t", u=POOL_PAGES, t=PACK)
-        turned_cols = vs_turned[:, :, VS_ROW:P].rearrange("s t u -> s u t")
+        turned_cols = vs_turned[:, :, VS_ROW:VS_END].rearrange("s t u -> s u t")
 
         def spread_source(first, last, vs_cols):
             nc.scalar.activation(vs_cols[:], turned_cols[:, first:last], ACT.Copy)
@@ -117,10 +119,9 @@ def tile_attend_pkv4q_rel2_cap_kernel(tc, q_words, q_scales, k_words, k_scales, 
 
         ks_listed = held.tile([P, N], U8, name="ks_listed", align_bytes=64)
         nc.vector.tensor_copy(ks_listed[:], ks_pool[:].indirect(token_list[:]))
-        for o in range(PASSES):
-            first = KS_FIRST + o * BLOCKS
-            for j in range(4):
-                nc.sync.dma_start(k_planes[j:P:32, o * N : (o + 1) * N].bitcast(I32), ks_listed[first + j : first + BLOCKS : 4, :].bitcast(I32))
+        for g in (0, 2, 1, 3):
+            row = KS_FIRST + 8 * g
+            nc.sync.dma_start(k_planes[32 * g : 32 * g + 4, :].bitcast(I32), ks_listed[row : row + 8, :].bitcast(I32))
         vw_pool = placed.tile([P, POOL_PAGES * DV], I32, name="vw_pool", offset=0, align_bytes=64)
         nc.sync.dma_start(
             vw_pool[:].rearrange("g (u e) -> g u e", u=POOL_PAGES),

@@ -27,10 +27,11 @@ KS_FIRST = P - PASSES * BLOCKS
 VS_FIRST = P - BLOCKS
 VS_END = 64
 VS_ROW = VS_END - POOL_PAGES
+SUMS = 3
 FIRST_SPREAD = 4
 PAGE_BYTES = 4 * PAGE
-PAIRS_AT = 5 * PAGE_BYTES
-CAPPED_AT = 7 * PAGE_BYTES
+PAIRS_AT = 6 * PAGE_BYTES
+CAPPED_AT = 8 * PAGE_BYTES
 LIST_COLS = PAGE // 16
 SCORE_BANKS = 3
 
@@ -57,10 +58,6 @@ def tile_attend_pkv4q_rel2_cap_kernel(tc, q_words, q_scales, k_words, k_scales, 
 
         vs_pages = held.tile([P, PAGE], F32, name="vs_pages", align_bytes=64)
         nc.scalar.dma_start(vs_pages[VS_ROW:VS_END, :], vs[0].rearrange("(u c) -> u c", u=POOL_PAGES))
-        ks_pool = placed.tile([P, T], U8, name="ks_pool", offset=0, align_bytes=64)
-        nc.sync.dma_start(ks_pool[KS_FIRST:P, :].bitcast(I32), k_scales.rearrange("o f t -> f o t").bitcast(I32))
-        token_list = lists.tile([P, N // 16], U16, name="token_list")
-        nc.sync.dma_start(token_list[:], offs)
         value_list = lists.tile([P, PAGES * DV // 16], U16, name="value_list")
         nc.sync.dma_start(value_list[:], voffs)
         vsc_pool = held.tile([P, POOL_PAGES * DV], U8, name="vsc_pool", align_bytes=64)
@@ -68,6 +65,10 @@ def tile_attend_pkv4q_rel2_cap_kernel(tc, q_words, q_scales, k_words, k_scales, 
             vsc_pool[VS_FIRST:P, :].bitcast(I32).rearrange("f (u w) -> f u w", u=POOL_PAGES),
             v_scales.rearrange("u f e -> f u e").bitcast(I32),
         )
+        ks_pool = placed.tile([P, T], U8, name="ks_pool", offset=0, align_bytes=64)
+        nc.sync.dma_start(ks_pool[KS_FIRST:P, :].bitcast(I32), k_scales.rearrange("o f t -> f o t").bitcast(I32))
+        token_list = lists.tile([P, N // 16], U16, name="token_list")
+        nc.sync.dma_start(token_list[:], offs)
         kw_pool = held.tile([P, T], I32, name="kw_pool", align_bytes=64)
         nc.sync.dma_start(kw_pool[:], k_words[0].rearrange("g t b -> g (t b)").bitcast(I32))
         q_codes = held.tile([P, PASSES, NQ], I32, name="q_codes", align_bytes=64)
@@ -76,19 +77,19 @@ def tile_attend_pkv4q_rel2_cap_kernel(tc, q_words, q_scales, k_words, k_scales, 
 
         identity = held.tile([P, P], F32, name="identity", align_bytes=64)
         make_identity(nc, identity[:])
-        for g in (1, 2, 3):
-            load_query_scales(nc.gpsimd, g)
 
+        nc.vector.memset(vsc_pool[0:VS_FIRST, :].bitcast(I32), 0)
+        nc.vector.memset(ks_pool[0:KS_FIRST, :].bitcast(I32), 0)
         nc.vector.memset(vs_pages[0:VS_ROW, :], 0.0)
         nc.vector.memset(vs_pages[VS_END:P, :], 0.0)
-        nc.vector.memset(ks_pool[0:KS_FIRST, :].bitcast(I32), 0)
-        nc.vector.memset(vsc_pool[0:VS_FIRST, :].bitcast(I32), 0)
+        sums = held.tile([P, SUMS + 1], F32, name="sums")
+        nc.vector.memset(sums[:, SUMS:], 1.0 / (CAP * CAP))
         k_planes = held.tile([P, PASSES * N], U8, name="k_planes", align_bytes=64)
-        nc.vector.memset(k_planes[:].bitcast(I32), 0)
-        sums = held.tile([P, PAGES + 1], F32, name="sums")
-        nc.vector.memset(sums[:, PAGES:], 1.0 / (CAP * CAP))
+        nc.gpsimd.memset(k_planes[:].bitcast(I32), 0)
+        for g in (1, 2, 3):
+            load_query_scales(nc.gpsimd, g)
         v_plane = held.tile([P, PAGES * DV], U8, name="v_plane", align_bytes=64)
-        nc.vector.memset(v_plane[:].bitcast(I32), 0)
+        nc.gpsimd.memset(v_plane[:].bitcast(I32), 0)
 
         vs_turned = turn_banks.tile([P, PACK, P], F32, name="turned")
         for t in range(PACK):
@@ -109,14 +110,17 @@ def tile_attend_pkv4q_rel2_cap_kernel(tc, q_words, q_scales, k_words, k_scales, 
         nc.scalar.activation(vs_spread[:, FIRST_SPREAD:POOL_PAGES], other_source, ACT.Copy)
         vs_listed = {}
 
-        def gather_vs(u, listed):
-            vs_listed[u] = listed[:]
-            nc.scalar.activation(listed[:], vs_pool[:].indirect(token_list[:, u * LIST_COLS : (u + 1) * LIST_COLS]), ACT.Copy)
+        def gather_vs(u, into):
+            vs_listed[u] = into
+            nc.scalar.activation(into, vs_pool[:].indirect(token_list[:, u * LIST_COLS : (u + 1) * LIST_COLS]), ACT.Copy)
 
-        for u in (0, 2):
-            gather_vs(u, held.tile([P, PAGE], F32, name="vs_listed%d" % u, align_bytes=64))
+        first_vs = held.tile([P, 2 * PAGE], F32, name="first_vs", align_bytes=64)
+        for i, u in enumerate((0, 2)):
+            gather_vs(u, first_vs[:, i * PAGE : (i + 1) * PAGE])
 
 
+        vsc_listed = held.tile([P, PAGES * DV], U8, name="vsc_listed", align_bytes=64)
+        nc.vector.tensor_copy(vsc_listed[:], vsc_pool[:].indirect(value_list[:]))
         ks_listed = held.tile([P, N], U8, name="ks_listed", align_bytes=64)
         nc.vector.tensor_copy(ks_listed[:], ks_pool[:].indirect(token_list[:]))
         for g in (0, 2, 1, 3):
@@ -127,8 +131,6 @@ def tile_attend_pkv4q_rel2_cap_kernel(tc, q_words, q_scales, k_words, k_scales, 
             vw_pool[:].rearrange("g (u e) -> g u e", u=POOL_PAGES),
             v_words.rearrange("u g e r -> g u (e r)").bitcast(I32),
         )
-        vsc_listed = held.tile([P, PAGES * DV], U8, name="vsc_listed", align_bytes=64)
-        nc.vector.tensor_copy(vsc_listed[:], vsc_pool[:].indirect(value_list[:]))
         for j in range(4):
             nc.sync.dma_start(v_plane[j:P:32, :].bitcast(I32), vsc_listed[VS_FIRST + j : P : 4, :].bitcast(I32))
 
@@ -195,7 +197,7 @@ def tile_attend_pkv4q_rel2_cap_kernel(tc, q_words, q_scales, k_words, k_scales, 
 
         def clip_and_square(u, into):
             squared[u] = into
-            nc.vector.scalar_tensor_tensor(into, capped[u], 0.0, capped[u], ALU.max, ALU.mult, accum_out=sums[:, u : u + 1])
+            nc.vector.scalar_tensor_tensor(into, capped[u], 0.0, capped[u], ALU.max, ALU.mult)
 
         def turn(u):
             turned[u] = turn_banks.tile([P, PACK, NQ], F32, name="turned")
@@ -215,9 +217,7 @@ def tile_attend_pkv4q_rel2_cap_kernel(tc, q_words, q_scales, k_words, k_scales, 
 
         def gather_values(slot):
             listed = held.tile([P, PAGES * DV], U32, name="v_codes", tag=slot, align_bytes=64)
-            for h in range(2):
-                offsets = value_list[:, h * DV // 8 : (h + 1) * DV // 8]
-                nc.vector.tensor_copy(listed[:, 2 * h * DV : 2 * (h + 1) * DV], vw_pool[:].bitcast(U32).indirect(offsets))
+            nc.vector.tensor_copy(listed[:], vw_pool[:].bitcast(U32).indirect(value_list[:]))
             for u in range(PAGES):
                 v_codes[u] = listed[:, u * DV : (u + 1) * DV]
 
@@ -257,21 +257,21 @@ def tile_attend_pkv4q_rel2_cap_kernel(tc, q_words, q_scales, k_words, k_scales, 
         square(0)
         turn(0)
         gather_values("values")
-        squared2 = placed.tile([P, PAGE], F32, name="squared2", offset=0, align_bytes=64)
-        squared3 = placed.tile([P, PAGE], F32, name="squared3", offset=PAGE_BYTES, align_bytes=64)
+        squares = placed.tile([P, 2 * PAGE], F32, name="squares", offset=0, align_bytes=64)
         woven0 = placed.tile([P, PAGE], BF16, name="woven0", offset=2 * PAGE_BYTES, align_bytes=64)
-        positive1 = placed.tile([P, PAGE], F32, name="positive1", offset=7 * PAGE_BYTES // 2, align_bytes=64)
+        positive1 = placed.tile([P, PAGE], F32, name="positive1", offset=3 * PAGE_BYTES, align_bytes=64)
         rest = held.tile([P, 3 * PAGE], BF16, name="rest", align_bytes=64)
         cap(2, capped_all[:, 2 * PAGE : 3 * PAGE])
         cap(3, capped_all[:, 3 * PAGE :])
         clip_on_vector(1, positive1[:])
-        clip_and_square(2, squared2[:])
+        clip_and_square(2, squares[:, 0:PAGE])
         square(1)
-        clip_and_square(3, squared3[:])
-        listed1 = placed.tile([P, PAGE], F32, name="listed1", offset=4 * PAGE_BYTES, align_bytes=64)
-        listed3 = placed.tile([P, PAGE], F32, name="listed3", offset=11 * PAGE_BYTES // 4, align_bytes=64)
-        gather_vs(1, listed1)
-        gather_vs(3, listed3)
+        clip_and_square(3, squares[:, PAGE:])
+        late_vs = placed.tile([P, 2 * PAGE], F32, name="late_vs", offset=4 * PAGE_BYTES - 64, align_bytes=64)
+        for i, u in enumerate((1, 3)):
+            gather_vs(u, late_vs[:, i * PAGE : (i + 1) * PAGE])
+        copied = held.tile([P, 2 * PAGE], F32, name="copied", align_bytes=64)
+        nc.scalar.activation(copied[:], squares[:], ACT.Copy, accum_out=sums[:, 2:3])
         turn(2)
         turn(1)
         turn(3)
@@ -284,7 +284,7 @@ def tile_attend_pkv4q_rel2_cap_kernel(tc, q_words, q_scales, k_words, k_scales, 
         quantise(1)
         quantise(3)
         total = held.tile([P, 1], F32, name="total")
-        summed = held.tile([P, PAGES + 1], F32, name="summed")
+        summed = held.tile([P, SUMS + 1], F32, name="summed")
         nc.scalar.activation(summed[:], sums[:], ACT.Copy, scale=CAP * CAP, accum_out=total[:])
         order = (0, 2, 1, 3)
         for u in order:

@@ -28,7 +28,7 @@ VS_FIRST = P - BLOCKS
 VS_END = 64
 VS_ROW = VS_END - POOL_PAGES
 SUMS = 3
-FIRST_SPREAD = 4
+FIRST_SPREAD = 3
 PAGE_BYTES = 4 * PAGE
 PAIRS_AT = 6 * PAGE_BYTES
 CAPPED_AT = 8 * PAGE_BYTES
@@ -58,6 +58,10 @@ def tile_attend_pkv4q_rel2_cap_kernel(tc, q_words, q_scales, k_words, k_scales, 
 
         vs_pages = held.tile([P, PAGE], F32, name="vs_pages", align_bytes=64)
         nc.scalar.dma_start(vs_pages[VS_ROW:VS_END, :], vs[0].rearrange("(u c) -> u c", u=POOL_PAGES))
+        ks_pool = placed.tile([P, T], U8, name="ks_pool", offset=0, align_bytes=64)
+        nc.sync.dma_start(ks_pool[KS_FIRST:P, :].bitcast(I32), k_scales.rearrange("o f t -> f o t").bitcast(I32))
+        token_list = lists.tile([P, N // 16], U16, name="token_list")
+        nc.sync.dma_start(token_list[:], offs)
         value_list = lists.tile([P, PAGES * DV // 16], U16, name="value_list")
         nc.sync.dma_start(value_list[:], voffs)
         vsc_pool = held.tile([P, POOL_PAGES * DV], U8, name="vsc_pool", align_bytes=64)
@@ -65,10 +69,6 @@ def tile_attend_pkv4q_rel2_cap_kernel(tc, q_words, q_scales, k_words, k_scales, 
             vsc_pool[VS_FIRST:P, :].bitcast(I32).rearrange("f (u w) -> f u w", u=POOL_PAGES),
             v_scales.rearrange("u f e -> f u e").bitcast(I32),
         )
-        ks_pool = placed.tile([P, T], U8, name="ks_pool", offset=0, align_bytes=64)
-        nc.sync.dma_start(ks_pool[KS_FIRST:P, :].bitcast(I32), k_scales.rearrange("o f t -> f o t").bitcast(I32))
-        token_list = lists.tile([P, N // 16], U16, name="token_list")
-        nc.sync.dma_start(token_list[:], offs)
         kw_pool = held.tile([P, T], I32, name="kw_pool", align_bytes=64)
         nc.sync.dma_start(kw_pool[:], k_words[0].rearrange("g t b -> g (t b)").bitcast(I32))
         q_codes = held.tile([P, PASSES, NQ], I32, name="q_codes", align_bytes=64)
@@ -78,15 +78,18 @@ def tile_attend_pkv4q_rel2_cap_kernel(tc, q_words, q_scales, k_words, k_scales, 
         identity = held.tile([P, P], F32, name="identity", align_bytes=64)
         make_identity(nc, identity[:])
 
-        nc.vector.memset(vsc_pool[0:VS_FIRST, :].bitcast(I32), 0)
         nc.vector.memset(ks_pool[0:KS_FIRST, :].bitcast(I32), 0)
         nc.vector.memset(vs_pages[0:VS_ROW, :], 0.0)
         nc.vector.memset(vs_pages[VS_END:P, :], 0.0)
         sums = held.tile([P, SUMS + 1], F32, name="sums")
         nc.vector.memset(sums[:, SUMS:], 1.0 / (CAP * CAP))
-        k_planes = held.tile([P, PASSES * N], U8, name="k_planes", align_bytes=64)
-        nc.gpsimd.memset(k_planes[:].bitcast(I32), 0)
-        for g in (1, 2, 3):
+        first_planes = held.tile([P, PASSES * PAGE], U8, name="first_planes", align_bytes=64)
+        nc.vector.memset(first_planes[:].bitcast(I32), 0)
+        nc.vector.memset(vsc_pool[0:VS_FIRST, :].bitcast(I32), 0)
+        load_query_scales(nc.gpsimd, 1)
+        other_planes = held.tile([P, PASSES * (N - PAGE)], U8, name="other_planes", align_bytes=64)
+        nc.gpsimd.memset(other_planes[:].bitcast(I32), 0)
+        for g in (2, 3):
             load_query_scales(nc.gpsimd, g)
         v_plane = held.tile([P, PAGES * DV], U8, name="v_plane", align_bytes=64)
         nc.gpsimd.memset(v_plane[:].bitcast(I32), 0)
@@ -119,18 +122,25 @@ def tile_attend_pkv4q_rel2_cap_kernel(tc, q_words, q_scales, k_words, k_scales, 
             gather_vs(u, first_vs[:, i * PAGE : (i + 1) * PAGE])
 
 
-        vsc_listed = held.tile([P, PAGES * DV], U8, name="vsc_listed", align_bytes=64)
-        nc.vector.tensor_copy(vsc_listed[:], vsc_pool[:].indirect(value_list[:]))
-        ks_listed = held.tile([P, N], U8, name="ks_listed", align_bytes=64)
-        nc.vector.tensor_copy(ks_listed[:], ks_pool[:].indirect(token_list[:]))
-        for g in (0, 2, 1, 3):
-            row = KS_FIRST + 8 * g
-            nc.sync.dma_start(k_planes[32 * g : 32 * g + 4, :].bitcast(I32), ks_listed[row : row + 8, :].bitcast(I32))
+        k_plane = {}
+        for first, last, planes in ((0, 1, first_planes), (1, PAGES, other_planes)):
+            width = (last - first) * PAGE
+            ks_listed = held.tile([P, width], U8, name="ks_listed%d" % first, align_bytes=64)
+            nc.vector.tensor_copy(ks_listed[:], ks_pool[:].indirect(token_list[:, first * LIST_COLS : last * LIST_COLS]))
+            for g in (0, 2, 1, 3):
+                row = KS_FIRST + 8 * g
+                nc.sync.dma_start(planes[32 * g : 32 * g + 4, :].bitcast(I32), ks_listed[row : row + 8, :].bitcast(I32))
+            for u in range(first, last):
+                for o in range(PASSES):
+                    start = o * width + (u - first) * PAGE
+                    k_plane[u, o] = planes[:, start : start + PAGE]
         vw_pool = placed.tile([P, POOL_PAGES * DV], I32, name="vw_pool", offset=0, align_bytes=64)
         nc.sync.dma_start(
             vw_pool[:].rearrange("g (u e) -> g u e", u=POOL_PAGES),
             v_words.rearrange("u g e r -> g u (e r)").bitcast(I32),
         )
+        vsc_listed = held.tile([P, PAGES * DV], U8, name="vsc_listed", align_bytes=64)
+        nc.vector.tensor_copy(vsc_listed[:], vsc_pool[:].indirect(value_list[:]))
         for j in range(4):
             nc.sync.dma_start(v_plane[j:P:32, :].bitcast(I32), vsc_listed[VS_FIRST + j : P : 4, :].bitcast(I32))
 
@@ -162,13 +172,12 @@ def tile_attend_pkv4q_rel2_cap_kernel(tc, q_words, q_scales, k_words, k_scales, 
                 nc.vector.tensor_copy(k_codes[:].rearrange("g o (h i) -> g h o i", h=2), words.rearrange("g (h i o) -> g h o i", h=2, o=PASSES))
             scores[u] = score_banks.tile([P, PAGE], F32, name="score")
             for o in range(PASSES):
-                plane = o * N + u * PAGE
                 nc.tensor.matmul_mx(
                     out=scores[u][:],
                     lhsT=q_codes[:, o, :].bitcast(FP8X4),
                     lhsT_scale=q_plane[:, o * NQ : (o + 1) * NQ],
                     rhs=k_codes[:, o, :].bitcast(FP4X4),
-                    rhs_scale=k_planes[:, plane : plane + PAGE],
+                    rhs_scale=k_plane[u, o],
                     start=(o == 0),
                     stop=(o == PASSES - 1),
                 )

@@ -27,8 +27,7 @@ KS_FIRST = P - PASSES * BLOCKS
 VS_FIRST = P - BLOCKS
 VS_END = 64
 VS_ROW = VS_END - POOL_PAGES
-SUMS = 3
-FIRST_SPREAD = 3
+SUMS = 4
 PAGE_BYTES = 4 * PAGE
 PAIRS_AT = 6 * PAGE_BYTES
 CAPPED_AT = 8 * PAGE_BYTES
@@ -45,9 +44,7 @@ def tile_attend_pkv4q_rel2_cap_kernel(tc, q_words, q_scales, k_words, k_scales, 
         held = ctx.enter_context(tc.tile_pool(name="held", bufs=1))
         placed = ctx.enter_context(tc.tile_pool(name="placed", bufs=1))
         pages = ctx.enter_context(tc.tile_pool(name="pages", bufs=PAGES))
-        score_banks = ctx.enter_context(tc.psum_pool(name="score_banks", bufs=SCORE_BANKS))
-        turn_banks = ctx.enter_context(tc.psum_pool(name="turn_banks", bufs=PAGES))
-        sum_bank = ctx.enter_context(tc.psum_pool(name="sum_bank", bufs=1))
+        banks = ctx.enter_context(tc.psum_pool(name="banks", bufs=1))
 
         q_plane = held.tile([P, PASSES * NQ], U8, name="q_plane", align_bytes=64)
         nc.gpsimd.memset(q_plane[:].bitcast(I32), 0)
@@ -94,23 +91,23 @@ def tile_attend_pkv4q_rel2_cap_kernel(tc, q_words, q_scales, k_words, k_scales, 
         v_plane = held.tile([P, PAGES * DV], U8, name="v_plane", align_bytes=64)
         nc.gpsimd.memset(v_plane[:].bitcast(I32), 0)
 
-        vs_turned = turn_banks.tile([P, PACK, P], F32, name="turned")
+        vs_turned = banks.tile([P, PACK, P], F32, name="vs_turned")
         for t in range(PACK):
             nc.tensor.transpose(vs_turned[:, t, :], vs_pages[:, t:PAGE:PACK], identity[:])
         vs_pool = held.tile([P, T], F32, name="vs_pool", align_bytes=64)
         vs_spread = vs_pool[:].rearrange("s (u m t) -> s u m t", u=POOL_PAGES, t=PACK)
         turned_cols = vs_turned[:, :, VS_ROW:VS_END].rearrange("s t u -> s u t")
 
-        def spread_source(first, last, vs_cols):
-            nc.scalar.activation(vs_cols[:], turned_cols[:, first:last], ACT.Copy)
-            return vs_cols[:].unsqueeze(2).to_broadcast([P, last - first, NQ, PACK])
+        def spread(first, last, cols):
+            nc.scalar.activation(vs_spread[:, first:last], cols.unsqueeze(2).to_broadcast([P, last - first, NQ, PACK]), ACT.Copy)
 
-        first_cols = placed.tile([P, FIRST_SPREAD, PACK], F32, name="first_cols", offset=PAIRS_AT + PAGE_BYTES - 32, align_bytes=32)
-        first_source = spread_source(0, FIRST_SPREAD, first_cols)
-        other_cols = placed.tile([P, POOL_PAGES - FIRST_SPREAD, PACK], F32, name="other_cols", offset=CAPPED_AT, align_bytes=64)
-        other_source = spread_source(FIRST_SPREAD, POOL_PAGES, other_cols)
-        nc.scalar.activation(vs_spread[:, 0:FIRST_SPREAD], first_source, ACT.Copy)
-        nc.scalar.activation(vs_spread[:, FIRST_SPREAD:POOL_PAGES], other_source, ACT.Copy)
+        second_cols = placed.tile([P, PACK, PACK], F32, name="second_cols", offset=PAIRS_AT + PAGE_BYTES - 32, align_bytes=32)
+        nc.scalar.activation(second_cols[:, 0:1], turned_cols[:, 1:2], ACT.Copy)
+        other_cols = placed.tile([P, POOL_PAGES - 2, PACK], F32, name="other_cols", offset=CAPPED_AT, align_bytes=64)
+        nc.scalar.activation(other_cols[:], turned_cols[:, 2:POOL_PAGES], ACT.Copy)
+        spread(0, 1, turned_cols[:, 0:1])
+        spread(1, 2, second_cols[:, 0:1])
+        spread(2, POOL_PAGES, other_cols[:])
         vs_listed = {}
 
         def gather_vs(u, into):
@@ -170,7 +167,7 @@ def tile_attend_pkv4q_rel2_cap_kernel(tc, q_words, q_scales, k_words, k_scales, 
                     nc.vector.tensor_copy(k_codes[:, o, :], parted[:, o, :])
             else:
                 nc.vector.tensor_copy(k_codes[:].rearrange("g o (h i) -> g h o i", h=2), words.rearrange("g (h i o) -> g h o i", h=2, o=PASSES))
-            scores[u] = score_banks.tile([P, PAGE], F32, name="score")
+            scores[u] = banks.tile([P, PAGE], F32, name="score", tag="score%d" % (u % SCORE_BANKS))
             for o in range(PASSES):
                 nc.tensor.matmul_mx(
                     out=scores[u][:],
@@ -199,17 +196,16 @@ def tile_attend_pkv4q_rel2_cap_kernel(tc, q_words, q_scales, k_words, k_scales, 
             positive[u] = into
             nc.vector.tensor_scalar(into, capped[u], 0.0, None, ALU.max)
 
-        def square(u):
-            square_tile = held.tile([P, PAGE], F32, name="square_tile", tag="squared%d" % u, align_bytes=64)
-            squared[u] = square_tile[:]
-            nc.scalar.activation(squared[u], positive[u], ACT.Square, accum_out=sums[:, u : u + 1])
+        def square(u, into, cols, column):
+            squared[u] = into
+            nc.scalar.activation(into[:, cols], positive[u][:, cols], ACT.Square, accum_out=sums[:, column : column + 1])
 
         def clip_and_square(u, into):
             squared[u] = into
             nc.vector.scalar_tensor_tensor(into, capped[u], 0.0, capped[u], ALU.max, ALU.mult)
 
         def turn(u):
-            turned[u] = turn_banks.tile([P, PACK, NQ], F32, name="turned")
+            turned[u] = banks.tile([P, PACK, NQ], F32, name="turned", tag="score2" if u == 0 else "turned%d" % u)
             for t in range(PACK):
                 nc.tensor.transpose(turned[u][:, t, :], squared[u][:, t * P : (t + 1) * P], identity[:])
 
@@ -230,7 +226,7 @@ def tile_attend_pkv4q_rel2_cap_kernel(tc, q_words, q_scales, k_words, k_scales, 
             for u in range(PAGES):
                 v_codes[u] = listed[:, u * DV : (u + 1) * DV]
 
-        acc = sum_bank.tile([P, DV], F32, name="acc")
+        acc = banks.tile([P, DV], F32, name="acc")
 
         def quantise(u):
             w_codes = pages.tile([P, NQ], U32, name="w_codes", align_bytes=64)
@@ -263,7 +259,9 @@ def tile_attend_pkv4q_rel2_cap_kernel(tc, q_words, q_scales, k_words, k_scales, 
         for h in range(2):
             clip_on_scalar(0, positive0[:], slice(h * PAGE // 2, (h + 1) * PAGE // 2))
         cap(1, capped_all[:, PAGE : 2 * PAGE])
-        square(0)
+        early_squares = held.tile([P, 2 * PAGE], F32, name="early_squares", align_bytes=64)
+        for h in range(2):
+            square(0, early_squares[:, 0:PAGE], slice(h * PAGE // 2, (h + 1) * PAGE // 2), h)
         turn(0)
         gather_values("values")
         squares = placed.tile([P, 2 * PAGE], F32, name="squares", offset=0, align_bytes=64)
@@ -274,13 +272,13 @@ def tile_attend_pkv4q_rel2_cap_kernel(tc, q_words, q_scales, k_words, k_scales, 
         cap(3, capped_all[:, 3 * PAGE :])
         clip_on_vector(1, positive1[:])
         clip_and_square(2, squares[:, 0:PAGE])
-        square(1)
+        square(1, early_squares[:, PAGE:], slice(0, PAGE), 2)
         clip_and_square(3, squares[:, PAGE:])
         late_vs = placed.tile([P, 2 * PAGE], F32, name="late_vs", offset=4 * PAGE_BYTES - 64, align_bytes=64)
         for i, u in enumerate((1, 3)):
             gather_vs(u, late_vs[:, i * PAGE : (i + 1) * PAGE])
         copied = held.tile([P, 2 * PAGE], F32, name="copied", align_bytes=64)
-        nc.scalar.activation(copied[:], squares[:], ACT.Copy, accum_out=sums[:, 2:3])
+        nc.scalar.activation(copied[:], squares[:], ACT.Copy, accum_out=sums[:, 3:4])
         turn(2)
         turn(1)
         turn(3)

@@ -29,6 +29,8 @@ VS_END = 64
 VS_ROW = VS_END - POOL_PAGES
 SUMS = 4
 PAGE_BYTES = 4 * PAGE
+KS_AT = 4 * PAGE_BYTES - PASSES * PAGE
+VSC_AT = 12 * PAGE_BYTES
 PAIRS_AT = 6 * PAGE_BYTES
 CAPPED_AT = 8 * PAGE_BYTES
 LIST_COLS = PAGE // 16
@@ -55,13 +57,13 @@ def tile_attend_pkv4q_rel2_cap_kernel(tc, q_words, q_scales, k_words, k_scales, 
 
         vs_pages = held.tile([P, PAGE], F32, name="vs_pages", align_bytes=64)
         nc.scalar.dma_start(vs_pages[VS_ROW:VS_END, :], vs[0].rearrange("(u c) -> u c", u=POOL_PAGES))
-        ks_pool = placed.tile([P, T], U8, name="ks_pool", offset=0, align_bytes=64)
+        ks_pool = placed.tile([P, T], U8, name="ks_pool", offset=KS_AT, align_bytes=64)
         nc.sync.dma_start(ks_pool[KS_FIRST:P, :].bitcast(I32), k_scales.rearrange("o f t -> f o t").bitcast(I32))
         token_list = lists.tile([P, N // 16], U16, name="token_list")
         nc.sync.dma_start(token_list[:], offs)
         value_list = lists.tile([P, PAGES * DV // 16], U16, name="value_list")
         nc.sync.dma_start(value_list[:], voffs)
-        vsc_pool = held.tile([P, POOL_PAGES * DV], U8, name="vsc_pool", align_bytes=64)
+        vsc_pool = placed.tile([P, POOL_PAGES * DV], U8, name="vsc_pool", offset=VSC_AT, align_bytes=64)
         nc.sync.dma_start(
             vsc_pool[VS_FIRST:P, :].bitcast(I32).rearrange("f (u w) -> f u w", u=POOL_PAGES),
             v_scales.rearrange("u f e -> f u e").bitcast(I32),
@@ -83,13 +85,10 @@ def tile_attend_pkv4q_rel2_cap_kernel(tc, q_words, q_scales, k_words, k_scales, 
         first_planes = held.tile([P, PASSES * PAGE], U8, name="first_planes", align_bytes=64)
         nc.vector.memset(first_planes[:].bitcast(I32), 0)
         nc.vector.memset(vsc_pool[0:VS_FIRST, :].bitcast(I32), 0)
-        load_query_scales(nc.gpsimd, 1)
-        other_planes = held.tile([P, PASSES * (N - PAGE)], U8, name="other_planes", align_bytes=64)
-        nc.gpsimd.memset(other_planes[:].bitcast(I32), 0)
-        for g in (2, 3):
+        for g in (1, 2, 3):
             load_query_scales(nc.gpsimd, g)
-        v_plane = held.tile([P, PAGES * DV], U8, name="v_plane", align_bytes=64)
-        nc.gpsimd.memset(v_plane[:].bitcast(I32), 0)
+        other_planes = placed.tile([P, PASSES * (N - PAGE)], U8, name="other_planes", offset=4 * PAGE_BYTES, align_bytes=64)
+        v_plane = placed.tile([P, PAGES * DV], U8, name="v_plane", offset=VSC_AT, align_bytes=64)
 
         vs_turned = banks.tile([P, PACK, P], F32, name="vs_turned")
         for t in range(PACK):

@@ -204,17 +204,17 @@ def tile_attend_pkv4q_rel2_cap_kernel(tc, q_words, q_scales, k_words, k_scales, 
             nc.vector.scalar_tensor_tensor(into, capped[u], 0.0, capped[u], ALU.max, ALU.mult)
 
         def turn(u):
-            turned[u] = banks.tile([P, PACK, NQ], F32, name="turned", tag="score2" if u == 0 else "turned%d" % u)
+            turned[u] = banks.tile([P, NQ, PACK], F32, name="turned", tag="score2" if u == 0 else "turned%d" % u)
             for t in range(PACK):
-                nc.tensor.transpose(turned[u][:, t, :], squared[u][:, t * P : (t + 1) * P], identity[:])
+                nc.tensor.transpose(turned[u][:, :, t], squared[u][:, t * P : (t + 1) * P], identity[:])
 
         def weigh(u, into):
             woven[u] = into
             nc.vector.scalar_tensor_tensor(
-                into.rearrange("s (q t) -> s q t", t=PACK),
-                turned[u][:].rearrange("s t q -> s q t"),
+                into,
+                turned[u][:].rearrange("s q t -> s (q t)"),
                 CAP * CAP,
-                vs_listed[u].rearrange("s (q t) -> s q t", t=PACK),
+                vs_listed[u],
                 ALU.mult,
                 ALU.mult,
             )

from contextlib import ExitStack

import concourse.mybir as mybir
from concourse.masks import make_identity

F32 = mybir.dt.float32
BF16 = mybir.dt.bfloat16
I32 = mybir.dt.int32
U32 = mybir.dt.uint32
U16 = mybir.dt.uint16
U8 = mybir.dt.uint8
FP8X4 = mybir.dt.float8_e4m3fn_x4
FP4X4 = mybir.dt.float4_e2m1fn_x4
ACT = mybir.ActivationFunctionType
ALU = mybir.AluOpType

P = 128
N, T, D, DV, NQ = 2048, 4096, 1024, 256, 128
PAGE = 512
PAGES = N // PAGE
POOL_PAGES = T // PAGE
PASSES = D // 512
PACK = 4
BLOCKS = 16
CAP = 2.0
KS_FIRST = P - PASSES * BLOCKS
VS_FIRST = P - BLOCKS
VS_END = 64
VS_ROW = VS_END - POOL_PAGES
SUMS = 4
PAGE_BYTES = 4 * PAGE
KS_AT = 4 * PAGE_BYTES - PASSES * PAGE
VSC_AT = 12 * PAGE_BYTES
PAIRS_AT = 6 * PAGE_BYTES
CAPPED_AT = 8 * PAGE_BYTES
LIST_COLS = PAGE // 16
SCORE_BANKS = 3

FLOPS = 2 * NQ * N * D + 2 * NQ * N * DV


def tile_attend_pkv4q_rel2_cap_kernel(tc, q_words, q_scales, k_words, k_scales, v_words, v_scales, vs, offs, voffs, out):
    nc = tc.nc
    with ExitStack() as ctx:
        lists = ctx.enter_context(tc.tile_pool(name="lists", bufs=1))
        held = ctx.enter_context(tc.tile_pool(name="held", bufs=1))
        placed = ctx.enter_context(tc.tile_pool(name="placed", bufs=1))
        pages = ctx.enter_context(tc.tile_pool(name="pages", bufs=PAGES))
        banks = ctx.enter_context(tc.psum_pool(name="banks", bufs=1))

        q_plane = held.tile([P, PASSES * NQ], U8, name="q_plane", align_bytes=64)
        nc.gpsimd.memset(q_plane[:].bitcast(I32), 0)
        qs_rows = q_scales[0].rearrange("o (g j) q -> g j o q", j=4)

        def load_query_scales(queue, g):
            queue.dma_start(q_plane[32 * g : 32 * g + 4, :].bitcast(I32).rearrange("j (o w) -> j o w", o=PASSES), qs_rows[g].bitcast(I32))

        vs_pages = held.tile([P, PAGE], F32, name="vs_pages", align_bytes=64)
        nc.scalar.dma_start(vs_pages[VS_ROW:VS_END, :], vs[0].rearrange("(u c) -> u c", u=POOL_PAGES))
        ks_pool = placed.tile([P, T], U8, name="ks_pool", offset=KS_AT, align_bytes=64)
        nc.sync.dma_start(ks_pool[KS_FIRST:P, :].bitcast(I32), k_scales.rearrange("o f t -> f o t").bitcast(I32))
        token_list = lists.tile([P, N // 16], U16, name="token_list")
        nc.sync.dma_start(token_list[:], offs)
        value_list = lists.tile([P, PAGES * DV // 16], U16, name="value_list")
        nc.sync.dma_start(value_list[:], voffs)
        vsc_pool = placed.tile([P, POOL_PAGES * DV], U8, name="vsc_pool", offset=VSC_AT, align_bytes=64)
        nc.sync.dma_start(
            vsc_pool[VS_FIRST:P, :].bitcast(I32).rearrange("f (u w) -> f u w", u=POOL_PAGES),
            v_scales.rearrange("u f e -> f u e").bitcast(I32),
        )
        kw_pool = held.tile([P, T], I32, name="kw_pool", align_bytes=64)
        nc.sync.dma_start(kw_pool[:], k_words[0].rearrange("g t b -> g (t b)").bitcast(I32))
        q_codes = held.tile([P, PASSES, NQ], I32, name="q_codes", align_bytes=64)
        nc.sync.dma_start(q_codes[:], q_words[0].rearrange("o g q r -> g o (q r)").bitcast(I32))
        load_query_scales(nc.sync, 0)

        identity = held.tile([P, P], F32, name="identity", align_bytes=64)
        make_identity(nc, identity[:])

        nc.vector.memset(ks_pool[0:KS_FIRST, :].bitcast(I32), 0)
        nc.vector.memset(vs_pages[0:VS_ROW, :], 0.0)
        nc.vector.memset(vs_pages[VS_END:P, :], 0.0)
        sums = held.tile([P, SUMS + 1], F32, name="sums")
        nc.vector.memset(sums[:, SUMS:], 1.0 / (CAP * CAP))
        first_planes = held.tile([P, PASSES * PAGE], U8, name="first_planes", align_bytes=64)
        nc.vector.memset(first_planes[:].bitcast(I32), 0)
        nc.vector.memset(vsc_pool[0:VS_FIRST, :].bitcast(I32), 0)
        for g in (1, 2, 3):
            load_query_scales(nc.gpsimd, g)
        other_planes = placed.tile([P, PASSES * (N - PAGE)], U8, name="other_planes", offset=4 * PAGE_BYTES, align_bytes=64)
        v_plane = placed.tile([P, PAGES * DV], U8, name="v_plane", offset=VSC_AT, align_bytes=64)

        vs_turned = banks.tile([P, PACK, P], F32, name="vs_turned")
        for t in range(PACK):
            nc.tensor.transpose(vs_turned[:, t, :], vs_pages[:, t:PAGE:PACK], identity[:])
        vs_pool = held.tile([P, T], F32, name="vs_pool", align_bytes=64)
        vs_spread = vs_pool[:].rearrange("s (u m t) -> s u m t", u=POOL_PAGES, t=PACK)
        turned_cols = vs_turned[:, :, VS_ROW:VS_END].rearrange("s t u -> s u t")

        def spread(first, last, cols):
            nc.scalar.activation(vs_spread[:, first:last], cols.unsqueeze(2).to_broadcast([P, last - first, NQ, PACK]), ACT.Copy)

        second_cols = placed.tile([P, PACK, PACK], F32, name="second_cols", offset=PAIRS_AT + PAGE_BYTES - 32, align_bytes=32)
        nc.scalar.activation(second_cols[:, 0:1], turned_cols[:, 1:2], ACT.Copy)
        other_cols = placed.tile([P, POOL_PAGES - 2, PACK], F32, name="other_cols", offset=CAPPED_AT, align_bytes=64)
        nc.scalar.activation(other_cols[:], turned_cols[:, 2:POOL_PAGES], ACT.Copy)
        spread(0, 1, turned_cols[:, 0:1])
        spread(1, 2, second_cols[:, 0:1])
        spread(2, POOL_PAGES, other_cols[:])
        vs_listed = {}

        def gather_vs(u, into):
            vs_listed[u] = into
            nc.scalar.activation(into, vs_pool[:].indirect(token_list[:, u * LIST_COLS : (u + 1) * LIST_COLS]), ACT.Copy)

        first_vs = held.tile([P, 2 * PAGE], F32, name="first_vs", align_bytes=64)
        for i, u in enumerate((0, 2)):
            gather_vs(u, first_vs[:, i * PAGE : (i + 1) * PAGE])


        k_plane = {}
        for first, last, planes in ((0, 1, first_planes), (1, PAGES, other_planes)):
            width = (last - first) * PAGE
            ks_listed = held.tile([P, width], U8, name="ks_listed%d" % first, align_bytes=64)
            nc.vector.tensor_copy(ks_listed[:], ks_pool[:].indirect(token_list[:, first * LIST_COLS : last * LIST_COLS]))
            for g in (0, 2, 1, 3):
                row = KS_FIRST + 8 * g
                nc.sync.dma_start(planes[32 * g : 32 * g + 4, :].bitcast(I32), ks_listed[row : row + 8, :].bitcast(I32))
            for u in range(first, last):
                for o in range(PASSES):
                    start = o * width + (u - first) * PAGE
                    k_plane[u, o] = planes[:, start : start + PAGE]
        vw_pool = placed.tile([P, POOL_PAGES * DV], I32, name="vw_pool", offset=0, align_bytes=64)
        nc.sync.dma_start(
            vw_pool[:].rearrange("g (u e) -> g u e", u=POOL_PAGES),
            v_words.rearrange("u g e r -> g u (e r)").bitcast(I32),
        )
        vsc_listed = held.tile([P, PAGES * DV], U8, name="vsc_listed", align_bytes=64)
        nc.vector.tensor_copy(vsc_listed[:], vsc_pool[:].indirect(value_list[:]))
        for j in range(4):
            nc.sync.dma_start(v_plane[j:P:32, :].bitcast(I32), vsc_listed[VS_FIRST + j : P : 4, :].bitcast(I32))

        k_pairs = {}
        scores = {}
        capped = {}
        positive = {}
        squared = {}
        turned = {}
        woven = {}
        v_codes = {}
        quantised = {}

        def page_offsets(u):
            return token_list[:, u * LIST_COLS : (u + 1) * LIST_COLS]

        def gather_keys(u):
            k_pairs[u] = placed.tile([P, PAGE], U32, name="k_pairs%d" % u, offset=PAIRS_AT + (u % 2) * PAGE_BYTES, align_bytes=64)
            nc.vector.tensor_copy(k_pairs[u][:], kw_pool[:].bitcast(U32).indirect(page_offsets(u)))

        def score_page(u):
            k_codes = held.tile([P, PASSES, PAGE], U16, name="k_codes", tag="parted%d" % u, align_bytes=64)
            words = k_pairs[u][:].bitcast(U16)
            if u == 0:
                parted = words.rearrange("g (i o) -> g o i", o=PASSES)
                for o in range(PASSES):
                    nc.vector.tensor_copy(k_codes[:, o, :], parted[:, o, :])
            else:
                nc.vector.tensor_copy(k_codes[:].rearrange("g o (h i) -> g h o i", h=2), words.rearrange("g (h i o) -> g h o i", h=2, o=PASSES))
            scores[u] = banks.tile([P, PAGE], F32, name="score", tag="score%d" % (u % SCORE_BANKS))
            for o in range(PASSES):
                nc.tensor.matmul_mx(
                    out=scores[u][:],
                    lhsT=q_codes[:, o, :].bitcast(FP8X4),
                    lhsT_scale=q_plane[:, o * NQ : (o + 1) * NQ],
                    rhs=k_codes[:, o, :].bitcast(FP4X4),
                    rhs_scale=k_plane[u, o],
                    start=(o == 0),
                    stop=(o == PASSES - 1),
                )

        def cap(u, into, places=slice(0, PACK)):
            capped[u] = into
            nc.scalar.activation(
                into.rearrange("q (t s) -> q t s", t=PACK)[:, places],
                scores[u][:].rearrange("q (s t) -> q t s", t=PACK)[:, places],
                ACT.Tanh,
                scale=1.0 / CAP,
            )

        def clip_on_scalar(u, into, cols):
            positive[u] = into
            nc.scalar.activation(into[:, cols], capped[u][:, cols], ACT.Relu)

        def clip_on_vector(u, into):
            positive[u] = into
            nc.vector.tensor_scalar(into, capped[u], 0.0, None, ALU.max)

        def square(u, into, cols, column):
            squared[u] = into
            nc.scalar.activation(into[:, cols], positive[u][:, cols], ACT.Square, accum_out=sums[:, column : column + 1])

        def clip_and_square(u, into):
            squared[u] = into
            nc.vector.scalar_tensor_tensor(into, capped[u], 0.0, capped[u], ALU.max, ALU.mult)

        def turn(u):
            turned[u] = banks.tile([P, NQ, PACK], F32, name="turned", tag="score2" if u == 0 else "turned%d" % u)
            for t in range(PACK):
                nc.tensor.transpose(turned[u][:, :, t], squared[u][:, t * P : (t + 1) * P], identity[:])

        def weigh(u, into):
            woven[u] = into
            nc.vector.scalar_tensor_tensor(
                into,
                turned[u][:].rearrange("s q t -> s (q t)"),
                CAP * CAP,
                vs_listed[u],
                ALU.mult,
                ALU.mult,
            )

        def gather_values(slot):
            listed = held.tile([P, PAGES * DV], U32, name="v_codes", tag=slot, align_bytes=64)
            nc.vector.tensor_copy(listed[:], vw_pool[:].bitcast(U32).indirect(value_list[:]))
            for u in range(PAGES):
                v_codes[u] = listed[:, u * DV : (u + 1) * DV]

        acc = banks.tile([P, DV], F32, name="acc")

        def quantise(u):
            w_codes = pages.tile([P, NQ], U32, name="w_codes", align_bytes=64)
            w_plane = pages.tile([P, NQ], U8, name="w_plane", align_bytes=64)
            nc.vector.quantize_mx(out=w_codes[:].bitcast(FP8X4), scales=w_plane[:], in_=woven[u])
            quantised[u] = (w_codes[:], w_plane)

        def multiply(u, first, last):
            w_codes, w_plane = quantised[u]
            nc.tensor.matmul_mx(
                out=acc[:],
                lhsT=w_codes.bitcast(FP8X4),
                lhsT_scale=w_plane[:],
                rhs=v_codes[u].bitcast(FP8X4),
                rhs_scale=v_plane[:, u * DV : (u + 1) * DV],
                start=first,
                stop=last,
            )

        for first in range(0, PAGES, 2):
            for u in (first, first + 1):
                gather_keys(u)
            for u in (first, first + 1):
                score_page(u)

        capped_all = placed.tile([P, PAGES * PAGE], F32, name="capped_all", offset=CAPPED_AT, align_bytes=64)
        positive0 = held.tile([P, PAGE], F32, name="positive0", align_bytes=64)
        for h in range(2):
            cap(0, capped_all[:, 0:PAGE], slice(2 * h, 2 * h + 2))
        for h in range(2):
            clip_on_scalar(0, positive0[:], slice(h * PAGE // 2, (h + 1) * PAGE // 2))
        cap(1, capped_all[:, PAGE : 2 * PAGE])
        early_squares = held.tile([P, 2 * PAGE], F32, name="early_squares", align_bytes=64)
        for h in range(2):
            square(0, early_squares[:, 0:PAGE], slice(h * PAGE // 2, (h + 1) * PAGE // 2), h)
        turn(0)
        gather_values("values")
        squares = placed.tile([P, 2 * PAGE], F32, name="squares", offset=0, align_bytes=64)
        woven0 = placed.tile([P, PAGE], BF16, name="woven0", offset=2 * PAGE_BYTES, align_bytes=64)
        positive1 = placed.tile([P, PAGE], F32, name="positive1", offset=3 * PAGE_BYTES, align_bytes=64)
        rest = held.tile([P, 3 * PAGE], BF16, name="rest", align_bytes=64)
        cap(2, capped_all[:, 2 * PAGE : 3 * PAGE])
        cap(3, capped_all[:, 3 * PAGE :])
        clip_on_vector(1, positive1[:])
        clip_and_square(2, squares[:, 0:PAGE])
        square(1, early_squares[:, PAGE:], slice(0, PAGE), 2)
        clip_and_square(3, squares[:, PAGE:])
        late_vs = placed.tile([P, 2 * PAGE], F32, name="late_vs", offset=4 * PAGE_BYTES - 64, align_bytes=64)
        for i, u in enumerate((1, 3)):
            gather_vs(u, late_vs[:, i * PAGE : (i + 1) * PAGE])
        copied = held.tile([P, 2 * PAGE], F32, name="copied", align_bytes=64)
        nc.scalar.activation(copied[:], squares[:], ACT.Copy, accum_out=sums[:, 3:4])
        turn(2)
        turn(1)
        turn(3)
        weigh(0, woven0[:])
        weigh(2, rest[:, 0:PAGE])
        quantise(0)
        weigh(1, rest[:, PAGE : 2 * PAGE])
        quantise(2)
        weigh(3, rest[:, 2 * PAGE :])
        quantise(1)
        quantise(3)
        total = held.tile([P, 1], F32, name="total")
        summed = held.tile([P, SUMS + 1], F32, name="summed")
        nc.scalar.activation(summed[:], sums[:], ACT.Copy, scale=CAP * CAP, accum_out=total[:])
        order = (0, 2, 1, 3)
        for u in order:
            multiply(u, u == order[0], u == order[-1])
        inverse = held.tile([P, 1], F32, name="inverse")
        nc.vector.reciprocal(inverse[:], total[:])
        result = held.tile([P, DV], F32, name="result")
        nc.scalar.activation(result[:], acc[:], ACT.Copy, scale=inverse[:])
        nc.scalar.dma_start(out[0], result[:])
